import numpy as np, ml_dtypes
CORES = [16,18,20,22]
N = 4
BF = ml_dtypes.bfloat16
def gentries(a):
    return np.ascontiguousarray(a.reshape(8, 16, -1).transpose(0, 2, 1)).reshape(8, -1)
def gtable(e):
    e = np.asarray(e); return np.ascontiguousarray(e.reshape(8, -1, 16).transpose(0, 2, 1)).reshape(128, -1).astype(np.int32)
def f(rng, *shape):
    return (rng.standard_normal(shape, dtype=np.float32) * np.exp2(rng.integers(-2, 3, shape[:-1] + (1,)))).astype(BF)
def wide(rng, *shape):
    v = f(rng, *shape).astype(np.float32); k = shape[:-2] + (1, shape[-1])
    return (v * np.exp2(rng.integers(-6, 7, k)) * (rng.random(k) > 0.0625)).astype(BF)
W, R, TK, A = 2560, 1024, 6, 160
X = np.arange(16)[:, None]
def cols(rng, lo, hi, lead, m=16):
    sh = rng.integers(lo, hi, lead + (1, W)); z = np.zeros(lead + (1, W), np.int64)
    c = np.sort((rng.integers(0, 257, lead + (m - 1, W)) >> sh) << sh, axis=-2)
    v = np.diff(np.concatenate([z, c, z + 256], axis=-2), axis=-2)
    return np.take_along_axis(v, np.argsort(rng.random(v.shape), axis=-2), -2)
def parts(rng, lo=0, hi=8):
    P = cols(rng, lo, hi, (8,)); a = cols(rng, lo, hi, (N, 8)); m = (P + a) >> 1
    m = m + (256 - np.add.reduce(m, axis=-2, keepdims=True)) * (X == rng.integers(0, 16, (N, 8, 1, W)))
    return {"P": P, "Q": np.where(rng.random((N, 8, 1, W)) < 0.5, m, a), "E": rng.integers(0, A, (8, 16, W)), "V": np.clip(f(rng, 128, W).astype(np.float32), -2, 2),
            "n": rng.integers(0, W, (N, 8, R)), "s": np.argsort(rng.random((N, 8, TK, W)), axis=-1)[..., :R], "d": rng.integers(0, 256, (N, 8, TK, 2, R)), "a": rng.integers(0, 128, (N, 8, TK, 3, R))}
def pack(v):
    def small(a): return np.ascontiguousarray(a).astype(np.float32).astype(BF)
    def alike(a): return small(np.stack([np.reshape(a, (128, W))] * N))
    return {"pt": alike(v["P"]), "qd": small(v["Q"].reshape(N, 128, W)), "nx": alike(v["E"]), "vf": alike(v["V"]), "n0": np.stack([gtable(a) for a in v["n"]]),
            "spot": np.stack([gtable(a.reshape(8, -1)) for a in v["s"]]), "ud": small(v["d"].reshape(N, 8, 2 * TK * R)), "ua": small(v["a"].reshape(N, 8, 3 * TK * R))}
def setup_inputs(rng):
    return pack(parts(rng))
def setup_inputs_spread(rng):
    v = parts(rng, 0, 9); v["V"] = np.clip(wide(rng, 128, W).astype(np.float32) * 0.5, -2, 2)
    r = rng.random((N, 8, R)); v["n"] = (W * r * r * r).astype(np.int64); r = rng.random((8, 16, W)); v["E"] = (A * r * r).astype(np.int64)
    r = rng.random(v["d"].shape); v["d"] = (256 * np.where(rng.random((N, 8, TK, 2, 1)) < 0.5, r * r, 1 - r * r * r)).astype(np.int64) & 255
    r = rng.random(v["a"].shape); v["a"] = (128 * np.where(rng.random((N, 8, TK, 3, 1)) < 0.5, r * r, 1 - r * r * r)).astype(np.int64) & 127
    return pack(v)
def two(rng, lead):
    a = rng.integers(0, 16, lead + (1, W)); b = (a + rng.integers(1, 16, lead + (1, W))) & 15; k = rng.choice(np.array([256, 256, 256, 255, 128, 1]), lead + (1, W))
    return k * (X == a) + (256 - k) * (X == b)
def setup_inputs_ends(rng):
    v = parts(rng); v["P"] = two(rng, (8,)); v["Q"] = two(rng, (N, 8)); x = np.arange(16)
    v["P"][7, :, W - 1] = 256 * (x == 15); v["Q"][:, 7, :, W - 1] = 256 * (x == 0); v["P"][2, :, 0] = 256 * (x == 14); v["Q"][:, 2, :, 0] = 256 * (x == 1)
    v["E"] = (A - 1) * rng.integers(0, 2, (8, 16, W)); v["V"] = 4.0 * rng.integers(0, 2, (128, W)) - 2.0
    v["n"] = (W - 1) * rng.integers(0, 2, (N, 8, R)); v["n"][:, :, R - 1] = W - 1; v["n"][:, :, 0] = 0
    ends = np.concatenate([np.arange(R // 2), np.arange(W - R // 2, W)]); v["s"] = ends[np.argsort(rng.random((N, 8, TK, R)), axis=-1)]
    v["d"] = 255 * rng.integers(0, 2, v["d"].shape); v["a"] = 127 * rng.integers(0, 2, v["a"].shape)
    return pack(v)
def odd(v, par):
    return np.where((X & 1) == par, np.repeat(v, 2, axis=-2), 0)
def setup_inputs_corners(rng):
    v = parts(rng); par = rng.integers(0, 2, (8, 1, W)); D = odd(cols(rng, 0, 8, (N, 8), 8), 1 - par)
    y = np.arange(8)[:, None]; i = rng.integers(0, 8, (8, 1, W)); j = (i + rng.integers(1, 8, (8, 1, W))) & 7; b = rng.integers(1, 65, (8, 1, W))
    P = odd(np.where(rng.random((8, 1, W)) < 0.4, (256 - b) * (y == i) + b * (y == j), cols(rng, 0, 8, (8,), 8)), par)
    top = (X == np.argmax(P, axis=-2)[..., None, :]) * 1; big = (X == np.argmax(D, axis=-2)[..., None, :]) * 1
    rest = P * (1 - top); nxt = (X == np.argmax(rest, axis=-2)[..., None, :]) * 1
    D = D + rng.integers(0, 2, (N, 8, 1, W)) * (top - big); edge = (X == np.where(par == 1, 0, 15)) * 1
    k = rng.integers(1, 4, (N, 8, 1, W)); both = ((k >= 2) & (np.max(rest, axis=-2, keepdims=True) >= 1)) * 1
    near = P + k * (edge - top) + both * (top - nxt)
    kind = np.array([0, 1, 1, 2, 3, 2, 0, 3])[(np.arange(N)[:, None] + np.arange(8)) & 7][:, :, None, None]
    v["P"] = P; v["Q"] = np.where(kind == 0, P, np.where(kind == 1, D, np.where(kind == 2, near, v["Q"])))
    v["d"] = np.where(rng.random(v["d"].shape) < 0.7, rng.choice(np.array([0, 1, 2, 3, 252, 253, 254, 255]), v["d"].shape), v["d"])
    v["a"] = np.where(rng.random(v["a"].shape) < 0.7, rng.choice(np.array([0, 1, 126, 127]), v["a"].shape), v["a"])
    v["n"] = np.where(rng.random(v["n"].shape) < 0.2, rng.choice(np.array([0, W - 1]), v["n"].shape), v["n"])
    v["E"] = np.where(rng.random(v["E"].shape) < 0.2, rng.choice(np.array([0, A - 1]), v["E"].shape), v["E"])
    return pack(v)
def setup_inputs_ties(rng):
    v = parts(rng); P = cols(rng, 4, 8, (8,)); Q = np.where(rng.random((N, 8, 1, W)) < 0.33, P, cols(rng, 4, 8, (N, 8)))
    o = np.argsort(rng.random((8, 16, W)), axis=-2); k = rng.choice(np.array([41, 47, 55, 61]), (8, 1, W)); i = rng.integers(0, 4, (N, 8, 1, W)); own = rng.random((8, 1, W)) < 0.4
    one = 256 * (o == 4); half = 128 * ((o == i) | (o == ((i + 1) & 3)))
    v["P"] = np.where(own, np.where(o < 4, k, (256 - 4 * k) * (o == 4)), P)
    v["Q"] = np.where(own, np.where(rng.random((N, 8, 1, W)) < 0.5, one, half), Q)
    v["d"] = np.clip(16 * rng.integers(0, 17, v["d"].shape) - rng.integers(0, 2, v["d"].shape), 0, 255)
    v["a"] = rng.choice(np.array([0, 16, 31, 32, 33, 48, 63, 64, 65, 80, 96, 112, 127]), v["a"].shape)
    v["a"][:, :, :, 1] = np.where(rng.random((N, 8, TK, R)) < 0.3, 64, v["a"][:, :, :, 1])
    return pack(v)
def setup_inputs_alike(rng):
    v = parts(rng); c = rng.integers(0, W - 1, (N, 8, 1)); v["n"] = c + np.zeros((N, 8, R), np.int64); v["n"][:, 1::2, R - 1] += 1
    b = rng.integers(0, A - 3, (8, 1, 1)); v["E"] = b + 3 * rng.integers(0, 2, (8, 16, W))
    k = rng.integers(0, W, 64)[rng.integers(0, 64, W)]; v["P"] = v["P"][:, :, k]
    return pack(v)
def check_ranges(d):
    bad = []
    for k, lo, hi in (("pt", 0, 256), ("qd", 0, 256), ("nx", 0, A - 1), ("vf", -2, 2), ("n0", 0, W - 1), ("spot", 0, W - 1), ("ud", 0, 255), ("ua", 0, 127)):
        a = np.asarray(d[k]).astype(np.float64)
        if not (np.min(a) >= lo and np.max(a) <= hi): bad.append("range of " + k)
        if k != "vf" and not np.all(a == np.floor(a)): bad.append("whole numbers of " + k)
        if k in ("pt", "nx", "vf") and not np.all(a == a[:1]): bad.append(k + " alike on all ranks")
        if k in ("pt", "qd") and not np.all(np.add.reduce(a.reshape(N, 8, 16, W), axis=2) == 256): bad.append("sums of " + k)
    s = np.sort(np.stack([gentries(np.asarray(a)) for a in d["spot"]]).reshape(N, 8, TK, R), axis=-1)
    if np.any(s[..., 1:] == s[..., :-1]): bad.append("repeated places in spot")
    return bad
def pick(tab, n):
    return np.take_along_axis(tab, n[:, :, None, :], 3)
def at(v, x):
    return np.take_along_axis(v, x[:, :, None, :], 2)[:, :, 0]
def first(m):
    return np.argmax(m, axis=2)
def teach(Q, rej, pl, p):
    for r in range(N):
        for g in range(8):
            k = rej[r, g]; Q[r, g][:, pl[r, g, k]] = p[r, g][:, k]
def reference(pt, qd, nx, vf, n0, spot, ud, ua):
    def ints(a): return a.astype(np.float32).astype(np.int64)
    P = ints(pt).reshape(N, 8, 16, W); Q = ints(qd).reshape(N, 8, 16, W); E = ints(nx).reshape(N, 8, 16, W); v = vf.astype(np.float64).reshape(N, 8, 16, W)
    n = np.stack([gentries(a) for a in n0]).astype(np.int64); pl = np.stack([gentries(a) for a in spot]).astype(np.int64).reshape(N, 8, TK, R)
    u = ints(ud).reshape(N, 8, TK, 2, R); w = ints(ua).reshape(N, 8, TK, 3, R); h = np.zeros((N, 8, 16, R)); seen = []
    for t in range(TK):
        p = pick(P, n); q = pick(Q, n)
        x = first(np.add.accumulate(q, axis=2) > u[:, :, t, 0][:, :, None])
        rej = w[:, :, t, 0] * at(q, x) >= 128 * at(p, x)
        p1 = np.maximum(p - q, 0)
        teach(Q, rej, pl[:, :, t], p)
        n, x, rej, p1, h = [np.roll(a, 1, axis=0) for a in (n, x, rej, p1, h)]
        s = np.add.reduce(p1, axis=2); p = pick(P, n); q = pick(Q, n)
        y = first(np.add.accumulate(q, axis=2) > u[:, :, t, 1][:, :, None])
        again = rej & (w[:, :, t, 1] * at(q, y) * s >= 32768 * at(p1, y))
        c = np.add.accumulate(np.maximum(256 * p1 - s[:, :, None] * q, 0), axis=2)
        z = first(128 * c > w[:, :, t, 2][:, :, None] * c[:, :, 15:])
        x = np.where(again, z, np.where(rej, y, x))
        if t < TK - 1: teach(Q, again, pl[:, :, t], p)
        row = np.concatenate([x[:, :1], (x[:, 1:] + x[:, :-1]) & 15], axis=1)
        n = 16 * at(pick(E, n), row) + x
        h = np.tanh(h + pick(v, n)); seen.append(n)
    yn = np.stack(seen, axis=2).reshape(N, 8, TK * R)
    return {"yh": h.reshape(N, 128, R).astype(np.float32), "yn": np.stack([gtable(a) for a in yn]).astype(np.float32)}

def check_inputs(d):
    bad = list(check_ranges(d))
    if not bad:
        for name, y in reference(**d).items():
            for q in range(N):
                v = np.abs(np.asarray(y[q], np.float64)); s = np.sqrt(np.mean(v * v))
                if v.max() > 3 * s or s < 2.0 ** -3: bad.append('%s of rank %d is uneven or too small' % (name, q))
    return bad

@@ -1,0 +1,548 @@
+from concourse.bass import DstId, RemoteDMATransfer
+from concourse.mybir import AluOpType as OP, ActivationFunctionType as AF
+
+W, R, TK, NR = 2560, 1024, 6, 4
+H = 65536.0
+BF, F32, F16, I32, U16 = "bfloat16", "float32", "float16", "int32", "uint16"
+
+SCRATCH = {
+    "Qw": ("sbuf", [128, 17 * W], BF), "Pt": ("sbuf", [128, W], BF), "Et": ("sbuf", [128, W], BF), "Vt": ("sbuf", [128, W], BF),
+    "uu": ("sbuf", [128, 3 * TK * R], BF), "rin": ("sbuf", [128, TK * R], BF), "pin": ("sbuf", [128, TK * R], BF),
+    "qa": ("sbuf", [128, 2 * R], BF), "da": ("sbuf", [128, 2 * R], BF),
+    "zer": ("sbuf", [128, 512], BF), "one": ("sbuf", [128, 144], BF), "TH": ("sbuf", [128, R], F16),
+    "n0i": ("sbuf", [128, 64], I32), "spi": ("sbuf", [128, TK * 64], I32),
+    "sP": ("sbuf", [128, TK * 64], F16),
+    "nl": ("sbuf", [128, (TK + 1) * 64], U16), "nin": ("sbuf", [128, TK * 64], U16), "hl": ("sbuf", [128, 128], U16),
+    "of1": ("sbuf", [128, 64], U16), "of2": ("sbuf", [128, 64], U16),
+    "Z1": ("sbuf", [128, TK * 128], BF), "Zin": ("sbuf", [128, TK * 128], BF),
+    "gg": ("sbuf", [128, 128], F32), "HL": ("sbuf", [128, 128], F16), "I16": ("sbuf", [128, 128], F16),
+    "nF": ("sbuf", [128, TK * 64], F32), "eB": ("sbuf", [128, TK, 2, 64], BF), "eD": ("dram", [8, TK, 3, 2, 8, 64], BF),
+    "ci": ("sbuf", [128, 8], I32), "cf": ("sbuf", [128, 32], F32),
+    "Ls32": ("sbuf", [128, 128], F32), "WB32": ("sbuf", [128, 192], F32),
+    "ps": ("psum", [128, 4096], F32),
+}
+for _n in ("q2", "m1", "m2", "cm", "cnt", "Eg", "sel", "Vg", "Sb", "KB"):
+    SCRATCH[_n] = ("sbuf", [128, R], BF)
+for _n in ("pr", "yy", "mn", "hA", "hs"):
+    SCRATCH[_n] = ("sbuf", [128, R], F32)
+for _n in ("BM", "Lc", "Dm", "t1", "t2", "t3", "t4", "I128", "I1", "MA", "MV", "In8", "Jh", "Lsn", "Dn", "E64", "bw0", "bw1",
+           "Sh", "bk0", "bk1", "SA", "SC", "SD", "iG", "iD", "u2", "ub", "tb", "kk"):
+    SCRATCH[_n] = ("sbuf", [128, 128], BF)
+for _n in ("WAz", "WAe", "WBr", "WBc", "WBz", "WBy", "iM", "iU"):
+    SCRATCH[_n] = ("sbuf", [128, 192], BF)
+
+SEMAPHORES = (["eV", "eS", "eP", "eG"] + ["d%d" % i for i in range(30)] + ["l%d" % i for i in range(40)]
+              + ["a%d" % i for i in range(58)])
+
+CY, PCY, GA, SCAT, LAT, FIX = 0.00100, 0.00050, 1.56, 3.8, 0.10, 0.06
+RLAT, GISS, LOOK = 2.2, 0.5, 0.12
+VG = (1,)
+X1 = X2 = ((0, 1), (1, 2), (2, 3), (3, 4))
+FY = False
+BUMP = {
+    'PMAZin0WBycm0b448': 5, 'PLsnr0': 0.9, 'PLs32mn1i1': -0.9, 'PShub1b192': 5, 'PDnm21': 0.6, 'Sb128ub0': 2.5,
+    'ViMc12c13WAz': 1.2, 'Vci3ci4ci5ci6cfb': -5, 'PWAesel1b320': 0.3, 'Vn0inl0nl1': -2.5, 'PLcq2q3': 1.3, 'ViUc15WBr': -5,
+    'Vb352of21': 2.5, 'Sm20': -2.5, 'PWB32mn1i4b64': 1.2,
+    'VeB0eB1eB2eB3eB4eB5eB6eB7eB8eB9eB10eB11eB12eB13eB14eB15b64gg1': 2.5, 'PLs32mn0i1': -0.3, 'SQnl1q3': 1.2,
+    'Vpq0mn0cm0': -3.1, 'PDnm20': 5.9, 'PWB32mn0i0b64': 2.4, 'VPnl1q3d3': 0.6, 'PSDuraurb': 1.2, 'Vof20p0i0Q': -5, 'Vzer': 5,
+    'PWB32mn1i0b64': 1.2, 'Vb0of10': -0.3, 'ViMc21bk0': 2.5, 'PWBzcm1b384': -2.5, 'PSDu0au0b': -2.5, 'ViMc22bk1': 5,
+    'Vpq1mn1cm1': -5.3, 'SEnin1Eg2': -5, 'ViMc15c17WBc': 2.5, 'ViUc20c19t3': 2.5}
+
+
+def build(g, core, T, topo, rank):
+    ops = []
+    lastw, readers = {}, {}
+    nsem = {"d": 0, "l": 0, "a": 0}
+
+    def newsem(k):
+        nsem[k] += 1
+        return "%s%d" % (k, nsem[k] - 1)
+
+    def add(eng, fn, rd, wr, cost, kind="c", sem=None, inc=0, done=0.0, after=(), f=1.0, hold=0, start=False):
+        i = len(ops)
+        deps = {}
+        psum = lambda k: k[0] == "b" and k != str(k)
+        for k in rd:
+            if k in lastw:
+                deps[lastw[k]] = True
+        for k in wr:
+            for j in readers.get(k, []) + ([lastw[k]] if k in lastw else []):
+                deps[j] = deps.get(j, False) or not psum(k)
+        for j in after:
+            deps.setdefault(j, False)
+        for k in rd:
+            readers.setdefault(k, []).append(i)
+        for k in wr:
+            lastw[k] = i
+            readers[k] = []
+        role = str(eng) + "".join(k if k == str(k) else k[0] + str(k[-1]) for k in list(rd) + list(wr) if not (psum(k) and len(k) == 2))
+        ops.append(dict(eng=eng, fn=fn, deps=deps, cost=cost, kind=kind, sem=sem, inc=inc, done=done, wr=wr, f=f, hold=hold,
+                        start=start, role=role, bank=[k[1] for k in wr if psum(k) and len(k) == 3]))
+        return i
+
+    def vc(n, f=1.0):
+        return FIX + max(64, n * f) * CY
+
+    V, S, P = g.vector, g.scalar, g.tensor
+
+    def ts(out, in0, s1, s2, o0, o1, rd, wr, n, f=1.0):
+        if o1 is None:
+            return add("V", lambda: V.tensor_scalar(out, in0, s1, None, o0), rd, wr, vc(n, f), f=f)
+        return add("V", lambda: V.tensor_scalar(out, in0, s1, s2, o0, o1), rd, wr, vc(n, f), f=f)
+
+    def tt(out, a, b, o, rd, wr, n, f=1.0):
+        return add("V", lambda: V.tensor_tensor(out, a, b, o), rd, wr, vc(n, f), f=f)
+
+    def cp(out, a, rd, wr, n, f=1.0):
+        return add("V", lambda: V.tensor_copy(out, a), rd, wr, vc(n, f), f=f)
+
+    def act(out, a, fn, rd, wr, n, f=1.0, bias=0.0, scale=1.0):
+        return add("S", lambda: S.activation(out, a, fn, bias=bias, scale=scale), rd, wr, vc(n, f), f=f)
+
+    def mm(items, rd, wr, hold=0):
+        def run():
+            r = None
+            for (o, l, x, st, sp, c) in items:
+                r = P.matmul(o, l, x, st, sp)
+            return r
+        return add("P", run, rd, wr, 0.02 + sum(it[5] for it in items) * PCY, hold=hold, start=items[0][3])
+
+    def dma(q, out, a, rd, wr, done, sem=None, accum=False):
+        e = {"Y": g.sync, "S": g.scalar, "G": g}[q]
+        if accum:
+            fn = lambda: e.dma_start(out, a, accum_op=OP.add)
+        else:
+            fn = lambda: e.dma_start(out, a)
+        return add(q, fn, rd, wr, 1.0 if q == "G" else 0.1, "dma", sem or newsem("d"), 16, done)
+
+    def send(items, rd, nbytes):
+        trs, arr, tot = [], [], 0
+        for k, (off, srcs, dst, alu, wr) in enumerate(items):
+            to = T.cores[(rank + off) % NR]
+            en = topo.engines(core, to)
+            m = len(en) // len(items)
+            mask = sum(1 << e for e in en[k * m:(k + 1) * m])
+            rid, pid = topo.addr(to)[:2]
+            sem = newsem("a")
+            trs.append(RemoteDMATransfer(dst_ids=[DstId(rid=rid, pnc=pid)], dma_engine_mask=mask, remote_sem=T.sem[sem],
+                                         srcs=srcs, dsts=[dst], alu_op=alu))
+            frm = T.cores[(rank - off) % NR]
+            arr.append((sem, len(topo.engines(frm, core)) // len(items), wr))
+            tot += m
+        ls = newsem("l")
+        i = add("G", lambda: g.remote_dma_fused(trs, local_sem=T.sem[ls]), rd, [], GISS, "send", ls, tot, RLAT + nbytes / 200e3)
+        for (sem, m, wr) in arr:
+            add(None, None, [], wr, 0.0, "arr", sem, m, 0.0, after=[i])
+
+    def gp(fn, rd, wr, n):
+        return add("G", fn, rd + ["pool"], wr + ["pool"], 0.15 + 2 * n * CY)
+
+    dma("Y", T.n0i[:], T.n0[:], [], ["n0i"], 2.0)
+    dma("Y", T.Qw[:, 0:W], T.qd[:], [], ["Q", "k1"], 5.0)
+    dma("S", T.Pt[:], T.pt[:], [], ["P", "k2"], 5.0)
+    su = newsem("d")
+    dma("S", T.uu[0:8, 0:2 * R], T.ud[:, 0:2 * R], [], ["u0a"], 3.0, su)
+    dma("S", T.uu[32:40, 0:3 * R], T.ua[:, 0:3 * R], [], ["u0b"], 3.0, su)
+    dma("Y", T.spi[:], T.spot[:], [], ["spi"], 3.0)
+    add("V", lambda: V.memset(T.one[:], 1.0), [], ["one"], vc(144))
+    dma("Y", T.uu[40:41, :], T.one[:], ["one"], ["u1"], 3.0)
+    dma("Y", T.eD[:], T.ua[:], ["k1", "k2"], ["eD"], 3.0)
+    dma("Y", T.Et[:], T.nx[:], ["k1", "k2"], ["E"], 4.0)
+    su = newsem("d")
+    for i in range(16):
+        dma("Y", T.eB[8 * i:8 * i + 8, :, :, :], T.eD[:, :, 2, :, i % 8, :], ["eD"], [("eB", i)], 3.0, su)
+    EB = [("eB", i) for i in range(16)]
+
+    gp(lambda: g.iota(T.ci[:, 0:1], [[0, 1]], 0, 1), [], ["ci0"], 1)
+    io = lambda out, pat, base, cm: (lambda: g.iota(out, pat, base, cm, allow_small_or_imprecise_dtypes=True))
+    gp(io(T.iG[:], [[1, 8], [0, 16]], 0, 0), [], ["iG"], 128)
+    gp(io(T.iD[:], [[1, 128]], 0, -1), [], ["iD"], 128)
+    gp(io(T.iM[:], [[1, 192]], 0, 0), [], ["iM"], 192)
+    gp(io(T.iU[:], [[0, 3], [1, 64]], 0, 0), [], ["iU"], 192)
+    p0 = T.ci[:, 0:1]
+    AND, SHR = OP.bitwise_and, OP.logical_shift_right
+    ts(T.ci[:, 1:2], p0, 15, None, AND, None, ["ci0"], ["ci1"], 1)
+    ts(T.ci[:, 2:3], p0, 4, None, SHR, None, ["ci0"], ["ci2"], 1)
+    cp(T.cf[:, 0:3], T.ci[:, 0:3], ["ci0", "ci1", "ci2"], ["cfa"], 3)
+    ts(T.ci[:, 3:4], p0, 7, None, AND, None, ["ci0"], ["ci3"], 1)
+    ts(T.ci[:, 4:5], p0, 3, 7, SHR, AND, ["ci0"], ["ci4"], 1)
+    ts(T.ci[:, 5:6], p0, 6, None, SHR, None, ["ci0"], ["ci5"], 1)
+    ts(T.ci[:, 6:7], p0, 63, None, AND, None, ["ci0"], ["ci6"], 1)
+    cp(T.cf[:, 3:7], T.ci[:, 3:7], ["ci3", "ci4", "ci5", "ci6"], ["cfb"], 4)
+    C = lambda k: T.cf[:, k:k + 1]
+    cP, cX, cG, cG8, cJ, cU, c63 = [C(k) for k in range(7)]
+    ncol = [7]
+
+    def col(a, scale, bias, rd):
+        k = ncol[0]
+        ncol[0] += 1
+        act(C(k), a, AF.Identity, rd, [("c", k)], 1, bias=bias, scale=scale)
+        return C(k), ("c", k)
+
+    def vcol(a, s1, s2, o0, o1, rd):
+        k = ncol[0]
+        ncol[0] += 1
+        ts(C(k), a, s1, s2, o0, o1, rd, [("c", k)], 1)
+        return C(k), ("c", k)
+
+    EQ, MUL, ADD, SUB = OP.is_equal, OP.mult, OP.add, OP.subtract
+
+    def mat(name, idx, c, w, rd, o1=MUL, n=128):
+        ts(T[name][:, 0:n], T[idx][:, 0:n], c, w, EQ, o1, [idx] + rd, [name], n, 0.5)
+
+    def scaled(name, src, w, rd=(), n=128):
+        act(T[name][:], T[src][:], AF.Identity, [src] + list(rd), [name], n, scale=w)
+
+    mat("BM", "iG", cG, 1.0, ["cfa"])
+    mat("SA", "iG", cP, -1.0, ["cfa"])
+    c32, k32 = col(cP, 1.0, -32.0, ["cfa"])
+    c40, k40 = vcol(cP, 40.0, -128.0, EQ, MUL, ["cfa"])
+    mat("SC", "iG", c32, c40, [k32, k40], ADD)
+    gp(lambda: g.affine_select(T.Lc[:], T.BM[:], [[1, 128]], OP.is_ge, 0.0, 0, -1), ["BM"], ["Lc"], 128)
+    mat("I128", "iD", 0.0, 128.0, [])
+    mat("I16", "iD", 0.0, 1.0, [])
+    cA, kA = vcol(cX, 15.0, -H, OP.not_equal, MUL, ["cfa"])
+    cB, kB = vcol(cX, 15.0, -2 * H, EQ, MUL, ["cfa"])
+    cC, kC = col(cB, -0.5, 0.0, [kB])
+    mat("t1", "iD", 0.0, H, [])
+    mat("t2", "iD", 1.0, cA, [kA])
+    scaled("t3", "BM", cB, [kB])
+    mat("t4", "iD", -15.0, cC, [kC])
+    tt(T.t1[:], T.t1[:], T.t2[:], ADD, ["t1", "t2"], ["t1"], 128)
+    tt(T.t3[:], T.t3[:], T.t4[:], ADD, ["t3", "t4"], ["t3"], 128)
+    tt(T.Dm[:], T.t1[:], T.t3[:], ADD, ["t1", "t3"], ["Dm"], 128)
+    cWa, kWa = col(cG, 16.0, 15.0, ["cfa"])
+    cWz, kWz = col(cX, float(W), float(W), ["cfa"])
+    mat("WAz", "iM", cWa, cWz, [kWa, kWz], n=144)
+    cp(T.nl[:, 0:64], T.n0i[:], ["n0i"], [("nl", 0, 0), ("nl", 0, 1)], 64)
+    ts(T.sP[:], T.spi[:], -1024.0, None, ADD, None, ["spi"], ["sP"], TK * 64)
+    add("V", lambda: V.memset(T.zer[:], 0.0), [], ["zer"], vc(256))
+    mat("WAe", "iM", cWa, 16.0, [kWa], n=144)
+    mat("SD", "iG", c32, 1.0 / 128, [k32])
+    scaled("Jh", "BM", 0.5)
+    scaled("I1", "I128", 1.0 / 128)
+    scaled("In8", "I128", -8.0 / 128)
+    scaled("Dn", "Dm", -1.0 / H)
+    ca, ka = col(cU, 34.0 / 128, -33.0 / 128, ["cfb"])
+    scaled("MA", "I128", ca, [ka])
+    gp(lambda: g.affine_select(T.t2[:], T.BM[:], [[1, 128]], OP.is_gt, 0.0, 0, -1), ["BM"], ["t2"], 128)
+    scaled("Ls32", "t2", 1.0)
+    scaled("Lsn", "t2", -128.0)
+    cWb, kWb = col(cG, 1.0, 56.0, ["cfa"])
+    mat("WBr", "iU", cWb, 1.0, [kWb], n=192)
+    scaled("WB32", "WBr", -1.0 / 128, n=192)
+    c0, k0 = vcol(cX, 0.0, 8.0, EQ, MUL, ["cfa"])
+    cWc, kWc = col(c0, 1.0, 0.5, [k0])
+    mat("WBc", "iM", cWb, cWc, [kWb, kWc], n=192)
+    cWy, kWy = col(cX, 1.0, 1.0, ["cfa"])
+    scaled("WBz", "WBr", cWy, [kWy], n=192)
+    mat("WBy", "iM", cWb, cWy, [kWb, kWy], n=192)
+    gp(io(T.cnt[:], [[1, 64], [0, 16]], 0, 0), [], [("cnt", 0), ("cnt", 1)], R)
+    ts(T.TH[:], T.cnt[:], c63, None, EQ, None, [("cnt", 0), ("cnt", 1), "cfb"], ["TH"], R, 0.5)
+    gp(io(T.KB[0:64, :], [[0, 64], [-256, 16]], -256, 0), [], ["KB0"], R)
+    gp(io(T.KB[64:128, :], [[0, 64], [256, 16]], 0, 0), [], ["KB1"], R)
+    for u in range(2):
+        a = T.KB[64 * u:64 * u + 64, :]
+        gp((lambda a: (lambda: g.affine_select(a, a, [[-1, 64], [0, 16]], EQ, 0.0, 0, 1)))(a), ["KB%d" % u], ["KB%d" % u], R)
+    c78, k78 = vcol(cG8, 7.0, None, OP.not_equal, None, ["cfb"])
+    ca, ka = col(c63, 1.0, 1.0, ["cfb"])
+    mat("E64", "iU", c63, 1.0, ["cfb"])
+    mat("t3", "iU", ca, c78, [ka, k78])
+    tt(T.Sh[:], T.t3[:], T.E64[:], ADD, ["t3", "E64"], ["Sh"], 128)
+    act(T.MV[:, 0:64], T.E64[:, 0:64], AF.Identity, ["E64"], ["MV0"], 64, scale=-33.0)
+    act(T.MV[:, 64:128], T.E64[:, 64:128], AF.Identity, ["E64"], ["MV1"], 64)
+    cb, kb = col(cG8, 16.0, cJ, ["cfb"])
+    mat("bk0", "iM", cb, 1.0, [kb])
+    cc, kc = col(cb, 1.0, 8.0, [kb])
+    mat("bk1", "iM", cc, 1.0, [kc])
+    scaled("bw0", "bk0", float(W))
+    scaled("bw1", "bk1", float(W))
+    ca, ka = vcol(cG8, 0.0, cU, EQ, ADD, ["cfb"])
+    cSq, kSq = col(ca, 1.0, -10.0, [ka])
+    ca, ka = vcol(cX, 1.0, cX, ADD, MUL, ["cfa"])
+    cSe, kSe = col(ca, -256.0, 0.0, [ka])
+
+    send([(1, [T.nl[:, 0:64]], T.nin[:, 0:64], 0, [("nin", 0, 0), ("nin", 0, 1)])], [("nl", 0, 0), ("nl", 0, 1)], 16e3)
+
+    Qr, Qx = T.Qw[:, 0:W], T.Qw[:, :]
+    hs_ = lambda b, h, o=0: b[:, o + 512 * h:o + 512 * h + 512]
+    qs_ = lambda b, u, o=0: b[:, o + 256 * u:o + 256 * u + 256]
+    rot = [0, 1, 2]
+
+    def h_step(t):
+        off = (TK - 1 - t) % NR
+        if off == 0:
+            lst, o, key = T.nl, (t + 1) * 64, lambda h: ("nl", t + 1, h)
+        elif off == 1:
+            lst, o, key = T.nin, (t + 1) * 64, lambda h: ("nin", t + 1, h)
+        else:
+            lst, o, key = T.hl, (off - 2) * 64, lambda h: ("hl", off, h)
+        for u in range(4):
+            vi, h = T.Vt[:, :].indirect(lst[:, o + 16 * u:o + 16 * u + 16]), u // 2
+            if t == 0:
+                act(qs_(T.hA, u), vi, AF.Tanh, ["Vt", key(h)], [("hA", u)], 256, GA)
+            elif t < TK - 1:
+                act(qs_(T.Vg, u), vi, AF.Copy, ["Vt", key(h)], [("Vg", u)], 256, GA)
+            else:
+                tt(qs_(T.hs, u), vi, qs_(T.hA, u), ADD, ["Vt", key(h), ("hA", u)], [("hs", u)], 256, GA)
+                act(qs_(T.hs, u), qs_(T.hs, u), AF.Tanh, [("hs", u)], [("hs", u)], 256)
+                if u % 2:
+                    dma("Y", hs_(T.yh, h), hs_(T.hs, h), [("hs", u - 1), ("hs", u)], [("yh", h)], 3.0)
+        if 0 < t < TK - 1:
+            hk = [("hA", u) for u in range(4)]
+            dma("G", T.hA[:], T.Vg[:], hk + [("Vg", u) for u in range(4)], hk, 4.0, accum=True)
+            for h in range(2):
+                act(hs_(T.hA, h), hs_(T.hA, h), AF.Tanh, hk[2 * h:2 * h + 2], hk[2 * h:2 * h + 2], 512)
+
+    for t in range(TK):
+        par, o2, oc = t % 2, (t % 2) * R, t * 64
+        UK = ["u0a", "u0b"] if t == 0 else ["ura", "urb"]
+        bank = lambda k, h: T.ps[:, 512 * (3 * h + rot[k]):512 * (3 * h + rot[k]) + 512]
+        bk = lambda k, h: ("b", 3 * h + rot[k])
+        sm = lambda h, a, n, st=1: T.ps[:, 512 * (6 + h) + a:512 * (6 + h) + a + n:st]
+        sk = lambda h, a: ("b", 6 + h, a)
+        ud = lambda k, h: T.uu[0:8, (2 * t + k) * R + 512 * h:(2 * t + k) * R + 512 * h + 512]
+        ua = lambda k, h, n: T.uu[32:32 + n, (3 * t + k) * R + 512 * h:(3 * t + k) * R + 512 * h + 512]
+        QK = lambda h: [("q", par, 2 * h), ("q", par, 2 * h + 1)]
+        DK = lambda h: [("d", par, 2 * h), ("d", par, 2 * h + 1)]
+        lh = lambda b, h: b[:, oc + 32 * h:oc + 32 * h + 32]
+
+        def reduce_list(wide, src, h, out, last=True):
+            return [(out, wide[:, 15 - j:143 - j], src[:, 512 * h + j:512 * h + 512:16], False, last and j == 15, 64) for j in range(16)]
+
+        fh = lambda b, h: b[:, 2 * oc + 64 * h:2 * oc + 64 * h + 64]
+
+        def reduce_fold(wide, src, h, out, first=False):
+            return [(out, wide[:, 56 - 8 * i:184 - 8 * i], src[:, 512 * h + i:512 * h + 512:8], first and i == 0, i == 7, 64) for i in range(8)]
+
+        def unfold(w, src, h, out, last):
+            return [(out, T[w + str(b)][:], src[:, 64 * h + b:64 * h + 64:2], False, last and b == 1, 64) for b in range(2)]
+
+        for h in range(2):
+            mm([(bank(0, h), T.SA[0:8, :], ud(0, h), True, False, 512)], ["SA"] + UK, [bk(0, h)])
+            mm([(bank(1, h), T.SC[32:41, :], ua(0, h, 9), True, True, 512)], ["SC", "u1"] + UK, [bk(1, h)])
+        for u in range(4):
+            lst = T.nl[:, oc + 16 * u:oc + 16 * u + 16]
+            act(qs_(T.qa, u, o2), Qr.indirect(lst), AF.Copy, ["Q", ("nl", t, u // 2)], [("q", par, u)], 256, GA)
+            tt(qs_(T.da, u, o2), T.Pt[:, :].indirect(lst), qs_(T.qa, u, o2), SUB, ["P", ("nl", t, u // 2), ("q", par, u)], [("d", par, u)], 256, GA)
+        for h in range(2):
+            q, d = hs_(T.qa, h, o2), hs_(T.da, h, o2)
+            send([(1, [d, T.zer[:]], hs_(T.rin, h, t * R), 2, [("r", t, h)]), (1, [d, q], hs_(T.pin, h, t * R), 1, [("p", t, h)])],
+                 QK(h) + DK(h) + ["zer"], 400e3)
+            mm([(bank(0, h), T.Lc[:], q, False, True, 512)], ["Lc"] + QK(h), [bk(0, h)])
+            act(hs_(T.m1, h), bank(0, h), AF.Sign, [], [bk(0, h), ("m1", h)], 512, bias=-0.5)
+            tt(hs_(T.pr, h), bank(1, h), q, MUL, QK(h), [bk(1, h), ("pr", h)], 512)
+            mm([(bank(2, h), T.I128[:], d, True, False, 512)], ["I128"] + DK(h), [bk(2, h)])
+            mm([(bank(2, h), T.Dm[:], hs_(T.m1, h), False, True, 512)], ["Dm", ("m1", h)], [bk(2, h)])
+            tt(hs_(T.cm, h), bank(2, h), hs_(T.pr, h), OP.is_gt, [("pr", h)], [bk(2, h), ("cm", h)], 512)
+            mm([(sm(h, 0, 32), T.I16[:], lh(T.sP, h), True, False, 64)] + reduce_list(T.WAz, T.cm, h, sm(h, 0, 32)),
+               ["I16", "sP", "WAz", ("cm", h)], [sk(h, 0)])
+            ts(T.of1[:, 32 * h:32 * h + 32], sm(h, 0, 32), 1024.0, None, ADD, None, [], [sk(h, 0), ("of1", h)], 32)
+            mm(reduce_fold(T.WBz, T.cm, h, sm(h, 384, 64), True), ["WBz", ("cm", h)], [sk(h, 384)])
+            act(fh(T.Z1, h), sm(h, 384, 64), AF.Copy, [], [sk(h, 384), ("Z1", t, h)], 64)
+            send([(1, [fh(T.Z1, h)], fh(T.Zin, h), 0, [("Zin", t, h)])], [("Z1", t, h)], 16e3)
+        if t == 0:
+            su = newsem("d")
+            dma("Y", T.uu[0:8, 2 * R:2 * TK * R], T.ud[:, 2 * R:], [("r", 0, 1)], ["ura"], 4.0, su)
+            dma("Y", T.uu[32:40, 3 * R:], T.ua[:, 3 * R:], [("r", 0, 1)], ["urb"], 4.0, su)
+            dma("Y", T.Vt[:], T.vf[:], [("p", 0, 1)], ["Vt"], 6.0)
+        for (a, b) in X1:
+            tt(Qx.indirect(T.of1[:, 16 * a:16 * b]), T.da[:, o2 + 256 * a:o2 + 256 * b], T.qa[:, o2 + 256 * a:o2 + 256 * b], ADD,
+               [k for u in range(a, b) for k in (("of1", u // 2), ("q", par, u), ("d", par, u))], ["Q"], 256 * (b - a), SCAT)
+        for u in range(4):
+            act(qs_(T.Eg, u), T.Et[:, :].indirect(T.nin[:, oc + 16 * u:oc + 16 * u + 16]), AF.Copy, ["E", ("nin", t, u // 2)], [("Eg", u)], 256, GA)
+        if t > 0:
+            h_step(t - 1)
+        for h in range(2):
+            r = hs_(T.rin, h, t * R)
+            mm([(bank(0, h), T.SA[0:8, :], ud(1, h), True, False, 512)], ["SA"] + UK, [bk(0, h)])
+            mm([(bank(1, h), T.Jh[:], r, True, True, 512)], ["Jh", ("r", t, h)], [bk(1, h)])
+            if FY:
+                act(hs_(T.Sb, h), bank(1, h), AF.Copy, [], [bk(1, h), ("Sb", h)], 512)
+                mm([(bank(1, h), T.SD[32:40, :], ua(1, h, 8), True, False, 512)], ["SD"] + UK, [bk(1, h)])
+            mm([(bank(2, h), T.I128[:], r, True, True, 512)], ["I128", ("r", t, h)], [bk(2, h)])
+        for h in range(2):
+            mm([(sm(h, 64, 64), T.WBr[:, 56 - 8 * i:184 - 8 * i], T.rin[:, t * R + 512 * h + 64 * i:t * R + 512 * h + 64 * i + 64], i == 0, False, 64)
+                for i in range(8)], ["WBr", ("r", t, h), ("of1", h)], [sk(h, 64)], 1)
+        for u in range(4):
+            qi = Qr.indirect(T.nin[:, oc + 16 * u:oc + 16 * u + 16])
+            if u in VG:
+                cp(qs_(T.q2, u), qi, ["Q", ("nin", t, u // 2)], [("q2", u)], 256, GA)
+            else:
+                act(qs_(T.q2, u), qi, AF.Copy, ["Q", ("nin", t, u // 2)], [("q2", u)], 256, GA)
+        for h in range(2):
+            r, q2, K2 = hs_(T.rin, h, t * R), hs_(T.q2, h), [("q2", 2 * h), ("q2", 2 * h + 1)]
+            c64 = slice(64 * h, 64 * h + 64)
+            mm([(bank(0, h), T.Lc[:], q2, False, True, 512)], ["Lc"] + K2, [bk(0, h)])
+            act(hs_(T.m2, h), bank(0, h), AF.Sign, [], [bk(0, h), ("m2", h)], 512, bias=-0.5)
+            if FY:
+                tt(hs_(T.yy, h), Qr.indirect(lh(T.nin, h)), hs_(T.Sb, h), MUL, ["Q", ("nin", t, h), ("Sb", h)], [("yy", h)], 512, GA)
+            else:
+                tt(hs_(T.yy, h), bank(1, h), q2, MUL, K2, [bk(1, h), ("yy", h)], 512)
+            tt(hs_(T.mn, h), bank(2, h), hs_(T.yy, h), OP.min, [("yy", h)], [bk(2, h), ("mn", h)], 512)
+            if not FY:
+                mm([(bank(1, h), T.SD[32:40, :], ua(1, h, 8), True, False, 512)], ["SD"] + UK, [bk(1, h)])
+            for i0 in (0, 4):
+                mm([(sm(h, 64, 64), T.WB32[:, 56 - 8 * i:184 - 8 * i], T.mn[:, 512 * h + 64 * i:512 * h + 64 * i + 64], False, i == 7, 256)
+                    for i in range(i0, i0 + 4)], ["WB32", ("mn", h), ("i", i0)], [sk(h, 64)], -1 if i0 else 0)
+            mm([(bank(1, h), T.Dn[:], hs_(T.m2, h), False, True, 512)], ["Dn", ("m2", h)], [bk(1, h)])
+            mm([(bank(2, h), T.Lsn[:], r, True, False, 512)], ["Lsn", ("r", t, h)], [bk(2, h)])
+            for u in range(2):
+                mm([(bank(2, h)[:, 256 * u:256 * u + 256], T.Ls32[:], qs_(T.mn, 2 * h + u), False, False, 1024)], ["Ls32", ("mn", h), ("i", u)], [bk(2, h)])
+            tt(bank(1, h), bank(1, h), hs_(T.yy, h), MUL, [("yy", h)], [bk(1, h), ("pq", h)], 512)
+            tt(hs_(T.cm, h), bank(1, h), hs_(T.mn, h), OP.is_lt, [("pq", h), ("mn", h)], [bk(1, h), ("cm", h)], 512)
+            tt(T.gg[:, c64], sm(h, 64, 64), T.eB[:, t, h, :], MUL, EB, [sk(h, 64), ("gg", h)], 64)
+            cp(T.HL[:, c64], T.gg[:, c64], [("gg", h)], [("HL", h)], 64)
+            tt(T.HL[64:128, c64], T.gg[64:128, c64], T.HL[64:128, c64], SUB, [("gg", h), ("HL", h)], [("HL", h)], 64, 2)
+            mm([(bank(2, h)[:, 64 * i:64 * i + 64], T.TH[:, 128 * i:128 * i + 128], T.HL[:, c64], False, i == 7, 64) for i in range(8)],
+               ["TH", ("HL", h)], [bk(2, h)])
+            act(hs_(T.cnt, h), bank(2, h), AF.Sign, [], [bk(2, h), ("cnt", h)], 512, bias=1.0 / 512)
+            mm([(sm(h, 448, 64), T.MA[:], fh(T.Zin, h), True, False, 64)] + reduce_fold(T.WBy, T.cm, h, sm(h, 448, 64)),
+               ["MA", ("Zin", t, h), "WBy", ("cm", h)], [sk(h, 448)])
+            act(T.u2[:, c64], sm(h, 448, 64), AF.Relu, [], [sk(h, 448), ("u2", h)], 64)
+            if t < TK - 1:
+                mm([(sm(h, 352, 32), T.I16[:], lh(T.sP, h), True, False, 64)] + unfold("bw", T.u2, h, sm(h, 352, 32), True),
+                   ["I16", "sP", "bw0", "bw1", ("u2", h)], [sk(h, 352)])
+                ts(T.of2[:, 32 * h:32 * h + 32], sm(h, 352, 32), 1024.0, None, ADD, None, [], [sk(h, 352), ("of2", h)], 32)
+        if t < TK - 1:
+            for (a, b) in X2:
+                cp(Qx.indirect(T.of2[:, 16 * a:16 * b]), T.pin[:, t * R + 256 * a:t * R + 256 * b],
+                   [k for u in range(a, b) for k in (("of2", u // 2), ("p", t, u // 2), ("i", u))], ["Q"], 256 * (b - a), SCAT)
+        for h in range(2):
+            c64 = slice(64 * h, 64 * h + 64)
+            ub = T.ub[:, c64]
+            mm([(bank(0, h), T.I1[:], hs_(T.Eg, h), True, False, 512)], ["I1", ("Eg", 2 * h), ("Eg", 2 * h + 1)], [bk(0, h)])
+            mm([(sm(h, 128, 64), T.MV[:], T.u2[:, c64], True, False, 64)] + reduce_fold(T.WBc, T.cnt, h, sm(h, 128, 64)),
+               ["WBc", "MV0", "MV1", ("cnt", h), ("u2", h)], [sk(h, 128)])
+            act(ub, sm(h, 128, 64), AF.Relu, [], [sk(h, 128), ("ub", h)], 64)
+            mm([(sm(h, 192, 64), T.Sh[:], ub, True, True, 64)], ["Sh", ("ub", h)], [sk(h, 192)])
+            act(T.tb[:, c64], sm(h, 192, 64), AF.Sign, [], [sk(h, 192), ("tb", h)], 64, bias=-17.5)
+            mm([(sm(h, 256, 64), T.Sh[:], ub, True, False, 64), (sm(h, 256, 64), T.In8[:], T.tb[:, c64], False, True, 64)],
+               ["Sh", "In8", ("ub", h), ("tb", h)], [sk(h, 256)])
+            act(T.kk[:, c64], sm(h, 256, 64), AF.Square, [kSq], [sk(h, 256), ("kk", h)], 64, bias=cSq)
+            mm([(bank(0, h)[:, i:512:8], T.KB[:, 128 * i:128 * i + 128], T.kk[:, c64], False, i == 7, 64) for i in range(8)],
+               ["KB0", "KB1", ("kk", h)], [bk(0, h)])
+            act(hs_(T.sel, h), bank(0, h), AF.Relu, [kSe], [bk(0, h), ("sel", h)], 512, bias=cSe)
+            un = unfold("bk", T.ub, h, sm(h, 320, 32), False)
+            mm([un[0][:3] + (True, False, 64), un[1]], ["bk0", "bk1", ("ub", h), ("kk", h)], [sk(h, 320)], 1)
+            mm(reduce_list(T.WAe, T.sel, h, sm(h, 320, 32)), ["WAe", ("sel", h)], [sk(h, 320)], -1)
+            nn = T.nl[:, oc + 64 + 32 * h:oc + 96 + 32 * h]
+            ts(nn, sm(h, 320, 32), -1.0, None, ADD, None, [], [sk(h, 320), ("nl", t + 1, h)], 32)
+            if t < TK - 1:
+                it = [(1, [nn], T.nin[:, oc + 64 + 32 * h:oc + 96 + 32 * h], 0, [("nin", t + 1, h)])]
+                off = (TK - 1 - t) % NR
+                if off > 1:
+                    it.append((off, [nn], T.hl[:, (off - 2) * 64 + 32 * h:(off - 2) * 64 + 32 * h + 32], 0, [("hl", off, h)]))
+                send(it, [("nl", t + 1, h)], 8e3)
+        if t >= TK - 2:
+            a = 0 if t == TK - 2 else t
+            cp(T.nF[:, 64 * a:oc + 64], T.nl[:, 64 * a + 64:oc + 128], [("nl", k + 1, h) for k in range(a, t + 1) for h in range(2)],
+               [("nF", t)], oc + 64 - 64 * a)
+        rot = [rot[1], rot[2], rot[0]]
+    dma("S", T.yn[:], T.nF[:], [("nF", TK - 2), ("nF", TK - 1)], ["yn"], 2.5)
+    h_step(TK - 1)
+    return ops
+
+
+def order(ops, bump=None):
+    n = len(ops)
+    deps = [dict(o["deps"]) for o in ops]
+    succ = [[] for _ in ops]
+    for i in range(n):
+        for j in deps[i]:
+            succ[j].append(i)
+    pri = [0.0] * n
+    for i in range(n - 1, -1, -1):
+        pri[i] = ops[i]["cost"] + ops[i]["done"] + LAT + max([pri[j] for j in succ[i]] + [0.0])
+    bump = BUMP if bump is None else bump
+    pri = [p + bump.get(o["role"], 0.0) for p, o in zip(pri, ops)]
+    left = [len(d) for d in deps]
+    ready = {i: 0.0 for i in range(n) if left[i] == 0}
+    free, end, seq, user, held = {}, [0.0] * n, [], {}, {}
+    while ready:
+        st = {}
+        for i, r in ready.items():
+            o = ops[i]
+            if o["bank"]:
+                b = o["bank"][0]
+                if o["start"] and held.get(b):
+                    continue
+                if b in user and ops[user[b]]["eng"] != o["eng"]:
+                    r = max(r, end[user[b]] + LAT)
+            st[i] = max(r, free.get(o["eng"], 0.0))
+        i0 = min(st, key=lambda i: (st[i], -pri[i], i))
+        e = ops[i0]["eng"]
+        i = i0 if e is None else max((k for k in st if ops[k]["eng"] == e and st[k] <= st[i0] + LOOK), key=lambda k: (pri[k], -k))
+        del ready[i]
+        o = ops[i]
+        if o["bank"]:
+            b = o["bank"][0]
+            if b in user:
+                deps[i].setdefault(user[b], False)
+            user[b] = i
+            if o["hold"]:
+                held[b] = o["hold"] > 0
+        if e is not None:
+            free[e] = st[i] + o["cost"]
+        end[i] = st[i] + o["cost"] + o["done"]
+        seq.append(i)
+        for j in succ[i]:
+            left[j] -= 1
+            if left[j] == 0:
+                ready[j] = max(end[k] + (0.0 if ops[k]["eng"] == ops[j]["eng"] and ops[k]["kind"] == "c" and not raw else LAT)
+                               for k, raw in deps[j].items())
+    return seq, max(end), [dict(o, deps=d) for o, d in zip(ops, deps)]
+
+
+def emit(g, T, ops, seq):
+    queue = {"V": g.vector, "S": g.scalar, "P": g.tensor, "G": g, "Y": g.sync}
+
+    def must(j, o, raw):
+        if o["kind"] == "arr":
+            return False
+        return ops[j]["kind"] != "c" or o["kind"] != "c" or ops[j]["eng"] != o["eng"] or raw
+
+    need = set(j for o in ops for j, raw in o["deps"].items() if must(j, o, raw))
+    total, event = {}, {}
+    for i in seq:
+        o = ops[i]
+        if o["kind"] == "c":
+            if i in need:
+                s = "e" + o["eng"]
+                total[s] = total.get(s, 0) + 1
+                event[i] = (s, total[s])
+        else:
+            total[o["sem"]] = total.get(o["sem"], 0) + o["inc"]
+    for i in seq:
+        if ops[i]["kind"] != "c":
+            event[i] = (ops[i]["sem"], total[ops[i]["sem"]])
+    seen = {e: {} for e in queue}
+    for i in seq:
+        o = ops[i]
+        if o["kind"] == "arr":
+            continue
+        want = {}
+        for j, raw in o["deps"].items():
+            if must(j, o, raw):
+                s, v = event[j]
+                want[s] = max(want.get(s, 0), v)
+        for s, v in want.items():
+            if seen[o["eng"]].get(s, 0) < v:
+                queue[o["eng"]].wait_ge(T.sem[s], v)
+                seen[o["eng"]][s] = v
+        r = o["fn"]()
+        if o["kind"] == "dma":
+            r.then_inc(T.sem[o["sem"]], 16)
+        elif o["kind"] == "c" and i in event:
+            r.then_inc(T.sem[event[i][0]], 1)
+    for s, v in total.items():
+        if max(seen[e].get(s, 0) for e in seen) < v:
+            g.wait_ge(T.sem[s], v)
+
+
+def rank_program(g, core, T, topo):
+    rank = T.rank_of(core)
+    if rank is None:
+        return
+    seq, _t, ops = order(build(g, core, T, topo, rank))
+    emit(g, T, ops, seq)

@@ -7,58 +7,58 @@ BF, F32, F16, I32, U16 = "bfloat16", "float32", "float16", "int32", "uint16"
 
 SCRATCH = {
     "Qw": ("sbuf", [128, 17 * W], BF), "Pt": ("sbuf", [128, W], BF), "Et": ("sbuf", [128, W], BF), "Vt": ("sbuf", [128, W], BF),
-    "uu": ("sbuf", [128, 3 * TK * R], BF), "rin": ("sbuf", [128, TK * R], BF), "pin": ("sbuf", [128, TK * R], BF),
-    "qa": ("sbuf", [128, 2 * R], BF), "da": ("sbuf", [128, 2 * R], BF),
-    "zer": ("sbuf", [128, 512], BF), "one": ("sbuf", [128, 144], BF), "TH": ("sbuf", [128, R], F16),
+    "uu": ("sbuf", [128, 3 * TK * R], BF), "pin": ("sbuf", [128, 2 * TK * R], BF),
+    "pq": ("sbuf", [128, 4 * R], BF), "dW": ("sbuf", [128, 2 * R], BF), "rr": ("sbuf", [128, R], BF), "In1": ("sbuf", [128, 128], BF),
+    "TH": ("sbuf", [128, 512], F16),
     "n0i": ("sbuf", [128, 64], I32), "spi": ("sbuf", [128, TK * 64], I32),
     "sP": ("sbuf", [128, TK * 64], F16),
     "nl": ("sbuf", [128, (TK + 1) * 64], U16), "nin": ("sbuf", [128, TK * 64], U16), "hl": ("sbuf", [128, 128], U16),
     "of1": ("sbuf", [128, 64], U16), "of2": ("sbuf", [128, 64], U16),
     "Z1": ("sbuf", [128, TK * 128], BF), "Zin": ("sbuf", [128, TK * 128], BF),
-    "gg": ("sbuf", [128, 128], F32), "HL": ("sbuf", [128, 128], F16), "I16": ("sbuf", [128, 128], F16),
-    "nF": ("sbuf", [128, TK * 64], F32), "eB": ("sbuf", [128, TK, 2, 64], BF), "eD": ("dram", [8, TK, 3, 2, 8, 64], BF),
-    "ci": ("sbuf", [128, 8], I32), "cf": ("sbuf", [128, 32], F32),
-    "Ls32": ("sbuf", [128, 128], F32), "WB32": ("sbuf", [128, 192], F32),
+    "HL": ("sbuf", [128, 320], F16), "HF": ("sbuf", [128, 256], F16), "I16": ("sbuf", [128, 128], F16),
+    "In16": ("sbuf", [128, 128], F16), "I32": ("sbuf", [128, 128], F32), "gg": ("sbuf", [128, 192], F32),
+    "nF": ("sbuf", [128, TK * 64], F32), "eT": ("sbuf", [128, 64], BF),
+    "ci": ("sbuf", [128, 8], I32), "cf": ("sbuf", [128, 32], F32), "cj": ("sbuf", [128, 8], F32),
+    "Ls32": ("sbuf", [128, 128], F32), "B32": ("sbuf", [128, 8], F32), "B8": ("sbuf", [128, 8], BF),
     "ps": ("psum", [128, 4096], F32),
 }
-for _n in ("q2", "m1", "m2", "cm", "cnt", "Eg", "sel", "Vg", "Sb", "KB"):
+for _n in ("q2", "m1", "m2", "cm", "cn", "cnt", "Eg", "sel", "Vg", "KB"):
     SCRATCH[_n] = ("sbuf", [128, R], BF)
-for _n in ("pr", "yy", "mn", "hA", "hs"):
+for _n in ("pr", "mn", "hA", "hs"):
     SCRATCH[_n] = ("sbuf", [128, R], F32)
-for _n in ("BM", "Lc", "Dm", "t1", "t2", "t3", "t4", "I128", "I1", "MA", "MV", "In8", "Jh", "Lsn", "Dn", "E64", "bw0", "bw1",
-           "Sh", "bk0", "bk1", "SA", "SC", "SD", "iG", "iD", "u2", "ub", "tb", "kk"):
+for _n in ("BM", "Lc", "Dm", "t1", "t2", "t3", "t4", "t5", "I128", "Lsn", "I1", "MV", "In8", "Jh", "E64", "bw0", "bw1",
+           "Sh", "bk0", "bk1", "SA", "SC", "iG", "iD", "iX", "G8", "KA", "u2", "ub", "tb", "kk"):
     SCRATCH[_n] = ("sbuf", [128, 128], BF)
-for _n in ("WAz", "WAe", "WBr", "WBc", "WBz", "WBy", "iM", "iU"):
+for _n in ("WAz", "WAe", "WBc", "WBy", "iM", "iU"):
     SCRATCH[_n] = ("sbuf", [128, 192], BF)
 
 SEMAPHORES = (["eV", "eS", "eP", "eG"] + ["d%d" % i for i in range(30)] + ["l%d" % i for i in range(40)]
               + ["a%d" % i for i in range(58)])
 
-CY, PCY, GA, SCAT, LAT, FIX = 0.00100, 0.00050, 1.56, 3.8, 0.10, 0.06
-RLAT, GISS, LOOK = 2.2, 0.5, 0.12
-VG = (1,)
-X1 = X2 = ((0, 1), (1, 2), (2, 3), (3, 4))
-FY = False
-BUMP = {
-    'PMAZin0WBycm0b448': 5, 'PLsnr0': 0.9, 'PLs32mn1i1': -0.9, 'PShub1b192': 5, 'PDnm21': 0.6, 'Sb128ub0': 2.5,
-    'ViMc12c13WAz': 1.2, 'Vci3ci4ci5ci6cfb': -5, 'PWAesel1b320': 0.3, 'Vn0inl0nl1': -2.5, 'PLcq2q3': 1.3, 'ViUc15WBr': -5,
-    'Vb352of21': 2.5, 'Sm20': -2.5, 'PWB32mn1i4b64': 1.2,
-    'VeB0eB1eB2eB3eB4eB5eB6eB7eB8eB9eB10eB11eB12eB13eB14eB15b64gg1': 2.5, 'PLs32mn0i1': -0.3, 'SQnl1q3': 1.2,
-    'Vpq0mn0cm0': -3.1, 'PDnm20': 5.9, 'PWB32mn0i0b64': 2.4, 'VPnl1q3d3': 0.6, 'PSDuraurb': 1.2, 'Vof20p0i0Q': -5, 'Vzer': 5,
-    'PWB32mn1i0b64': 1.2, 'Vb0of10': -0.3, 'ViMc21bk0': 2.5, 'PWBzcm1b384': -2.5, 'PSDu0au0b': -2.5, 'ViMc22bk1': 5,
-    'Vpq1mn1cm1': -5.3, 'SEnin1Eg2': -5, 'ViMc15c17WBc': 2.5, 'ViUc20c19t3': 2.5}
+ORDER = {
+    "V": "hv0- hv1- hv2- hv3- d0 d1 pr0 d2 cm0 d3 pr1 o10 cm1 x10 x11 o11 x12 x13 g1 g3 y0 mn0 y1 mn1 gA0 gB0 gC0 pq0 cn0 gA1 gB1 gC1 pq1 o20 cn1 x20 x21 o21 x22 x23 nn0 nn1 nf",
+    "S": "ht0- ht1- ht2- ht3- q0 q1 q2 q3 m0 m1 Vg0- Vg1- Z0 Vg2- Vg3- Z1 eC Eg0 Eg1 Eg2 Eg3 g0 g1 g2 g3 n0 n1 hF0 th0- u0 ct0 hF1 ub0 u1 tb0 ct1 kk0 ub1 se0 tb1 kk1 se1 th1-",
+    "P": "a0 c0 a1 c1 L0 e0 D0 L1 uo0 e1 D1 fz0 b0 uo1 fz1 eT b1 J0 R0 J1 R1 M0 M1 T0 E0 fw0 N0 C0 T1 E1 fw1 tr0 C1 fy0 Th0 up0 N1 C2 tr1 C3 fc0 fy1 Th1 s0 up1 I0 k0 I1 fc1 K0 s1 v0 k1 W0 K1 v1 W1",
+    "G": "sr0 sr1 sz ha- sn",
+}
+ORDER = {'V': 'hv0- hv1- hv2- hv3- d1 pr0 d2 cm0 d3 pr1 o10 cm1 x10 o11 x12 g1 g3 y0 mn0 y1 mn1 gA0 gB0 pq0 gC0 cn0 gA1 gB1 pq1 gC1 cn1 o20 x20 o21 x22 nn0 nn1 d0+ nf', 'S': 'ht0- ht1- ht2- ht3- q0 q1 q2 m0 q3 m1 Vg3- Vg1- Z0 Vg0- Eg2 Z1 Eg0 Vg2- Eg3 Eg1 eC g0 g2 n0 n1 hF0 u0 th0- hF1 ct0 ct1 ub0 u1 tb0 ub1 kk0 tb1 kk1 se0 se1 th1-', 'P': 'L0 eT e0 D0 c1 L1 uo0 e1 D1 fz0 b1 fz1 uo1 J0 R1 b0 J1 M0 M1 R0 N0 E0 fw0 N1 C0 fw1 E1 tr0 C1 fy0 C2 up0 tr1 Th0 C3 Th1 fy1 fc0 s0 fc1 I1 up1 k0 s1 I0 K0 k1 v0 a1+ K1 a0+ v1 W0 W1 c0+', 'G': 'sn- sr0 sr1 ha- sz'}
+ORDER = {'V': 'hv0- hv1- hv2- hv3- q1 q3 pr0 p3 pr1 cm0 cm1 o10 x10 o11 x12 g1 g3 y0 mn0 y1 mn1 gA0 gB0 pq0 gC0 gA1 gB1 cn0 gC1 pq1 cn1 o20 x20 o21 x22 nn0 x23 nn1 nf', 'S': 'ht0- ht1- ht2- ht3- m0 p2 m1 Vg3- Vg2- Vg1- Z1 Vg0- r0 Eg2 Eg0 r1 eC Z0 g0 g2 n0 Eg1 n1 Eg3 hF0 th0- u0 hF1 ct0 ct1 ub0 u1 tb0 ub1 kk0 tb1 kk1 se0 se1 th1- p0+ p1+ q0+ q2+', 'P': 'W1- a0 c0 L0 e0 a1 L1 D0 e1 b0 D1 uo0 uo1 fz1 U0 eT fz0 U1 J0 b1 R0 R1 M0 M1 J1 N0 E0 fw0 C0 N1 fw1 C2 tr0 C1 E1 fy0 tr1 Th0 up0 C3 Th1 fy1 fc0 I0 s0 fc1 k0 s1 k1 up1 K0 I1 K1 v0 v1 W0 c1+', 'G': 'sn- sr0 sr1 ha- sz lv'}
+OPT = dict(on_v=("g1", "g3", "q1", "q3", "p3"), direct=(0, 1), full=False, lo="V", x1=((0, 2), (2, 4)), x2=((0, 2), (2, 3), (3, 4)))
+COST = dict(cy=0.0009, pcy=0.00045, ga=1.56, sc=3.8, fix=0.06, lat=0.10, same=0.06, rlat=2.0, riss=0.5, giss=1.0, dlat=1.6, bw=400e3)
 
 
-def build(g, core, T, topo, rank):
+def build(g, core, T, topo, rank, opt=OPT):
     ops = []
     lastw, readers = {}, {}
     nsem = {"d": 0, "l": 0, "a": 0}
+    tok = [0]
+    on_v = opt["on_v"]
 
     def newsem(k):
         nsem[k] += 1
         return "%s%d" % (k, nsem[k] - 1)
 
-    def add(eng, fn, rd, wr, cost, kind="c", sem=None, inc=0, done=0.0, after=(), f=1.0, hold=0, start=False):
+    def add(name, eng, fn, rd, wr, cost, kind="c", sem=None, inc=0, after=(), hold=0, start=False):
         i = len(ops)
         deps = {}
         psum = lambda k: k[0] == "b" and k != str(k)
@@ -75,47 +75,47 @@ def build(g, core, T, topo, rank):
         for k in wr:
             lastw[k] = i
             readers[k] = []
-        role = str(eng) + "".join(k if k == str(k) else k[0] + str(k[-1]) for k in list(rd) + list(wr) if not (psum(k) and len(k) == 2))
-        ops.append(dict(eng=eng, fn=fn, deps=deps, cost=cost, kind=kind, sem=sem, inc=inc, done=done, wr=wr, f=f, hold=hold,
-                        start=start, role=role, bank=[k[1] for k in wr if psum(k) and len(k) == 3]))
+        ops.append(dict(name=name, tok=tok[0], eng=eng, fn=fn, deps=deps, cost=cost, kind=kind, sem=sem, inc=inc, hold=hold,
+                        start=start, bank=[k[1] for k in wr if psum(k) and len(k) == 3]))
         return i
 
-    def vc(n, f=1.0):
-        return FIX + max(64, n * f) * CY
-
     V, S, P = g.vector, g.scalar, g.tensor
+    vc = lambda n, f: (f, n) if f == str(f) else ("cy", max(64, n * f))
 
-    def ts(out, in0, s1, s2, o0, o1, rd, wr, n, f=1.0):
+    def ts(name, out, in0, s1, s2, o0, o1, rd, wr, n, f=1.0):
         if o1 is None:
-            return add("V", lambda: V.tensor_scalar(out, in0, s1, None, o0), rd, wr, vc(n, f), f=f)
-        return add("V", lambda: V.tensor_scalar(out, in0, s1, s2, o0, o1), rd, wr, vc(n, f), f=f)
+            return add(name, "V", lambda: V.tensor_scalar(out, in0, s1, None, o0), rd, wr, vc(n, f))
+        return add(name, "V", lambda: V.tensor_scalar(out, in0, s1, s2, o0, o1), rd, wr, vc(n, f))
 
-    def tt(out, a, b, o, rd, wr, n, f=1.0):
-        return add("V", lambda: V.tensor_tensor(out, a, b, o), rd, wr, vc(n, f), f=f)
+    def tt(name, out, a, b, o, rd, wr, n, f=1.0):
+        return add(name, "V", lambda: V.tensor_tensor(out, a, b, o), rd, wr, vc(n, f))
 
-    def cp(out, a, rd, wr, n, f=1.0):
-        return add("V", lambda: V.tensor_copy(out, a), rd, wr, vc(n, f), f=f)
+    def cp(name, out, a, rd, wr, n, f=1.0):
+        return add(name, "V", lambda: V.tensor_copy(out, a), rd, wr, vc(n, f))
 
-    def act(out, a, fn, rd, wr, n, f=1.0, bias=0.0, scale=1.0):
-        return add("S", lambda: S.activation(out, a, fn, bias=bias, scale=scale), rd, wr, vc(n, f), f=f)
+    def act(name, out, a, fn, rd, wr, n, f=1.0, bias=0.0, scale=1.0):
+        return add(name, "S", lambda: S.activation(out, a, fn, bias=bias, scale=scale), rd, wr, vc(n, f))
 
-    def mm(items, rd, wr, hold=0):
+    def copy(name, out, a, rd, wr, n, f=1.0):
+        return cp(name, out, a, rd, wr, n, f) if name in on_v else act(name, out, a, AF.Copy, rd, wr, n, f)
+
+    def mm(name, items, rd, wr, hold=0):
         def run():
             r = None
             for (o, l, x, st, sp, c) in items:
                 r = P.matmul(o, l, x, st, sp)
             return r
-        return add("P", run, rd, wr, 0.02 + sum(it[5] for it in items) * PCY, hold=hold, start=items[0][3])
+        return add(name, "P", run, rd, wr, ("pcy", sum(it[5] for it in items)), hold=hold, start=items[0][3])
 
-    def dma(q, out, a, rd, wr, done, sem=None, accum=False):
+    def dma(q, out, a, rd, wr, nbytes, sem=None, accum=False, name=None):
         e = {"Y": g.sync, "S": g.scalar, "G": g}[q]
         if accum:
             fn = lambda: e.dma_start(out, a, accum_op=OP.add)
         else:
             fn = lambda: e.dma_start(out, a)
-        return add(q, fn, rd, wr, 1.0 if q == "G" else 0.1, "dma", sem or newsem("d"), 16, done)
+        return add(name, q, fn, rd, wr, ("dma", nbytes), "dma", sem or newsem("d"), 16)
 
-    def send(items, rd, nbytes):
+    def send(name, items, rd, nbytes):
         trs, arr, tot = [], [], 0
         for k, (off, srcs, dst, alu, wr) in enumerate(items):
             to = T.cores[(rank + off) % NR]
@@ -130,45 +130,33 @@ def build(g, core, T, topo, rank):
             arr.append((sem, len(topo.engines(frm, core)) // len(items), wr))
             tot += m
         ls = newsem("l")
-        i = add("G", lambda: g.remote_dma_fused(trs, local_sem=T.sem[ls]), rd, [], GISS, "send", ls, tot, RLAT + nbytes / 200e3)
+        i = add(name, "G", lambda: g.remote_dma_fused(trs, local_sem=T.sem[ls]), rd, [], ("send", nbytes), "send", ls, tot)
         for (sem, m, wr) in arr:
-            add(None, None, [], wr, 0.0, "arr", sem, m, 0.0, after=[i])
+            add(None, None, None, [], wr, ("arr", 0), "arr", sem, m, after=[i])
 
     def gp(fn, rd, wr, n):
-        return add("G", fn, rd + ["pool"], wr + ["pool"], 0.15 + 2 * n * CY)
+        return add(None, "G", fn, rd + ["pool"], wr + ["pool"], ("gp", n))
 
-    dma("Y", T.n0i[:], T.n0[:], [], ["n0i"], 2.0)
-    dma("Y", T.Qw[:, 0:W], T.qd[:], [], ["Q", "k1"], 5.0)
-    dma("S", T.Pt[:], T.pt[:], [], ["P", "k2"], 5.0)
+    tok[0] = -1
+    dma("Y", T.n0i[:], T.n0[:], [], ["n0i"], 32e3)
+    dma("Y", T.Qw[:, 0:W], T.qd[:], [], ["Q", "k1"], 1300e3)
+    dma("S", T.Pt[:], T.pt[:], [], ["P", "k2"], 1300e3, name="ld")
     su = newsem("d")
-    dma("S", T.uu[0:8, 0:2 * R], T.ud[:, 0:2 * R], [], ["u0a"], 3.0, su)
-    dma("S", T.uu[32:40, 0:3 * R], T.ua[:, 0:3 * R], [], ["u0b"], 3.0, su)
-    dma("Y", T.spi[:], T.spot[:], [], ["spi"], 3.0)
-    add("V", lambda: V.memset(T.one[:], 1.0), [], ["one"], vc(144))
-    dma("Y", T.uu[40:41, :], T.one[:], ["one"], ["u1"], 3.0)
-    dma("Y", T.eD[:], T.ua[:], ["k1", "k2"], ["eD"], 3.0)
-    dma("Y", T.Et[:], T.nx[:], ["k1", "k2"], ["E"], 4.0)
-    su = newsem("d")
-    for i in range(16):
-        dma("Y", T.eB[8 * i:8 * i + 8, :, :, :], T.eD[:, :, 2, :, i % 8, :], ["eD"], [("eB", i)], 3.0, su)
-    EB = [("eB", i) for i in range(16)]
+    dma("S", T.uu[0:8, 0:2 * R], T.ud[:, 0:2 * R], [], ["u0a"], 1300e3, su, name="ld")
+    dma("S", T.uu[32:40, 0:3 * R], T.ua[:, 0:3 * R], [], ["u0b"], 1300e3, su, name="ld")
+    dma("Y", T.spi[:], T.spot[:], [], ["spi"], 1300e3)
+    dma("Y", T.Et[:], T.nx[:], ["k1", "k2"], ["E"], 700e3)
 
     gp(lambda: g.iota(T.ci[:, 0:1], [[0, 1]], 0, 1), [], ["ci0"], 1)
     io = lambda out, pat, base, cm: (lambda: g.iota(out, pat, base, cm, allow_small_or_imprecise_dtypes=True))
     gp(io(T.iG[:], [[1, 8], [0, 16]], 0, 0), [], ["iG"], 128)
     gp(io(T.iD[:], [[1, 128]], 0, -1), [], ["iD"], 128)
     gp(io(T.iM[:], [[1, 192]], 0, 0), [], ["iM"], 192)
-    gp(io(T.iU[:], [[0, 3], [1, 64]], 0, 0), [], ["iU"], 192)
     p0 = T.ci[:, 0:1]
     AND, SHR = OP.bitwise_and, OP.logical_shift_right
-    ts(T.ci[:, 1:2], p0, 15, None, AND, None, ["ci0"], ["ci1"], 1)
-    ts(T.ci[:, 2:3], p0, 4, None, SHR, None, ["ci0"], ["ci2"], 1)
-    cp(T.cf[:, 0:3], T.ci[:, 0:3], ["ci0", "ci1", "ci2"], ["cfa"], 3)
-    ts(T.ci[:, 3:4], p0, 7, None, AND, None, ["ci0"], ["ci3"], 1)
-    ts(T.ci[:, 4:5], p0, 3, 7, SHR, AND, ["ci0"], ["ci4"], 1)
-    ts(T.ci[:, 5:6], p0, 6, None, SHR, None, ["ci0"], ["ci5"], 1)
-    ts(T.ci[:, 6:7], p0, 63, None, AND, None, ["ci0"], ["ci6"], 1)
-    cp(T.cf[:, 3:7], T.ci[:, 3:7], ["ci3", "ci4", "ci5", "ci6"], ["cfb"], 4)
+    ts(None, T.ci[:, 1:2], p0, 15, None, AND, None, ["ci0"], ["ci1"], 1)
+    ts(None, T.ci[:, 2:3], p0, 4, None, SHR, None, ["ci0"], ["ci2"], 1)
+    cp(None, T.cf[:, 0:3], T.ci[:, 0:3], ["ci0", "ci1", "ci2"], ["cfa"], 3)
     C = lambda k: T.cf[:, k:k + 1]
     cP, cX, cG, cG8, cJ, cU, c63 = [C(k) for k in range(7)]
     ncol = [7]
@@ -176,31 +164,31 @@ def build(g, core, T, topo, rank):
     def col(a, scale, bias, rd):
         k = ncol[0]
         ncol[0] += 1
-        act(C(k), a, AF.Identity, rd, [("c", k)], 1, bias=bias, scale=scale)
+        act(None, C(k), a, AF.Identity, rd, [("c", k)], 1, bias=bias, scale=scale)
         return C(k), ("c", k)
 
     def vcol(a, s1, s2, o0, o1, rd):
         k = ncol[0]
         ncol[0] += 1
-        ts(C(k), a, s1, s2, o0, o1, rd, [("c", k)], 1)
+        ts(None, C(k), a, s1, s2, o0, o1, rd, [("c", k)], 1)
         return C(k), ("c", k)
 
-    EQ, MUL, ADD, SUB = OP.is_equal, OP.mult, OP.add, OP.subtract
+    EQ, MUL, ADD, SUB, MAX = OP.is_equal, OP.mult, OP.add, OP.subtract, OP.max
 
     def mat(name, idx, c, w, rd, o1=MUL, n=128):
-        ts(T[name][:, 0:n], T[idx][:, 0:n], c, w, EQ, o1, [idx] + rd, [name], n, 0.5)
+        ts(None, T[name][:, 0:n], T[idx][:, 0:n], c, w, EQ, o1, [idx] + rd, [name], n, 0.5)
 
     def scaled(name, src, w, rd=(), n=128):
-        act(T[name][:], T[src][:], AF.Identity, [src] + list(rd), [name], n, scale=w)
+        act(None, T[name][:], T[src][:], AF.Identity, [src] + list(rd), [name], n, scale=w)
 
     mat("BM", "iG", cG, 1.0, ["cfa"])
     mat("SA", "iG", cP, -1.0, ["cfa"])
     c32, k32 = col(cP, 1.0, -32.0, ["cfa"])
-    c40, k40 = vcol(cP, 40.0, -128.0, EQ, MUL, ["cfa"])
-    mat("SC", "iG", c32, c40, [k32, k40], ADD)
+    mat("SC", "iG", c32, 1.0, [k32])
     gp(lambda: g.affine_select(T.Lc[:], T.BM[:], [[1, 128]], OP.is_ge, 0.0, 0, -1), ["BM"], ["Lc"], 128)
+    gp(io(T.iU[:], [[0, 3], [1, 64]], 0, 0), [], ["iU"], 192)
+    cp(None, T.nl[:, 0:64], T.n0i[:], ["n0i"], [("nl", 0, 0), ("nl", 0, 1)], 64)
     mat("I128", "iD", 0.0, 128.0, [])
-    mat("I16", "iD", 0.0, 1.0, [])
     cA, kA = vcol(cX, 15.0, -H, OP.not_equal, MUL, ["cfa"])
     cB, kB = vcol(cX, 15.0, -2 * H, EQ, MUL, ["cfa"])
     cC, kC = col(cB, -0.5, 0.0, [kB])
@@ -208,273 +196,366 @@ def build(g, core, T, topo, rank):
     mat("t2", "iD", 1.0, cA, [kA])
     scaled("t3", "BM", cB, [kB])
     mat("t4", "iD", -15.0, cC, [kC])
-    tt(T.t1[:], T.t1[:], T.t2[:], ADD, ["t1", "t2"], ["t1"], 128)
-    tt(T.t3[:], T.t3[:], T.t4[:], ADD, ["t3", "t4"], ["t3"], 128)
-    tt(T.Dm[:], T.t1[:], T.t3[:], ADD, ["t1", "t3"], ["Dm"], 128)
+    tt(None, T.t1[:], T.t1[:], T.t2[:], ADD, ["t1", "t2"], ["t1"], 128, 2)
+    tt(None, T.t3[:], T.t3[:], T.t4[:], ADD, ["t3", "t4"], ["t3"], 128, 2)
+    tt(None, T.Dm[:], T.t1[:], T.t3[:], ADD, ["t1", "t3"], ["Dm"], 128, 2)
     cWa, kWa = col(cG, 16.0, 15.0, ["cfa"])
-    cWz, kWz = col(cX, float(W), float(W), ["cfa"])
-    mat("WAz", "iM", cWa, cWz, [kWa, kWz], n=144)
-    cp(T.nl[:, 0:64], T.n0i[:], ["n0i"], [("nl", 0, 0), ("nl", 0, 1)], 64)
-    ts(T.sP[:], T.spi[:], -1024.0, None, ADD, None, ["spi"], ["sP"], TK * 64)
-    add("V", lambda: V.memset(T.zer[:], 0.0), [], ["zer"], vc(256))
-    mat("WAe", "iM", cWa, 16.0, [kWa], n=144)
-    mat("SD", "iG", c32, 1.0 / 128, [k32])
-    scaled("Jh", "BM", 0.5)
-    scaled("I1", "I128", 1.0 / 128)
-    scaled("In8", "I128", -8.0 / 128)
-    scaled("Dn", "Dm", -1.0 / H)
-    ca, ka = col(cU, 34.0 / 128, -33.0 / 128, ["cfb"])
-    scaled("MA", "I128", ca, [ka])
-    gp(lambda: g.affine_select(T.t2[:], T.BM[:], [[1, 128]], OP.is_gt, 0.0, 0, -1), ["BM"], ["t2"], 128)
-    scaled("Ls32", "t2", 1.0)
-    scaled("Lsn", "t2", -128.0)
+    if opt["direct"]:
+        cWz, kWz = col(cX, float(W), float(W), ["cfa"])
+        mat("WAz", "iM", cWa, cWz, [kWa, kWz], n=144)
+    mat("I16", "iD", 0.0, 1.0, [])
+    ts(None, T.sP[:], T.spi[:], -1024.0, None, ADD, None, ["spi"], ["sP"], TK * 64)
+    ts(None, T.ci[:, 3:4], p0, 7, None, AND, None, ["ci0"], ["ci3"], 1)
+    ts(None, T.ci[:, 4:5], p0, 3, 7, SHR, AND, ["ci0"], ["ci4"], 1)
+    ts(None, T.ci[:, 5:6], p0, 6, None, SHR, None, ["ci0"], ["ci5"], 1)
+    ts(None, T.ci[:, 6:7], p0, 63, None, AND, None, ["ci0"], ["ci6"], 1)
+    cp(None, T.cf[:, 3:7], T.ci[:, 3:7], ["ci3", "ci4", "ci5", "ci6"], ["cfb"], 4)
     cWb, kWb = col(cG, 1.0, 56.0, ["cfa"])
-    mat("WBr", "iU", cWb, 1.0, [kWb], n=192)
-    scaled("WB32", "WBr", -1.0 / 128, n=192)
+    cWy, kWy = col(cX, 1.0, 1.0, ["cfa"])
+    mat("WBy", "iM", cWb, cWy, [kWb, kWy], n=192)
+    cb, kb = col(cG8, 16.0, cJ, ["cfb"])
+    cc, kc = col(cb, 1.0, 8.0, [kb])
+    mat("bw0", "iM", cb, float(W), [kb])
+    mat("bw1", "iM", cc, float(W), [kc])
+    scaled("Jh", "BM", 1.0 / 256)
+    scaled("I1", "I128", 1.0 / 128)
+    scaled("In1", "I128", -1.0 / 128)
+    mat("B8", "iM", cG, 1.0, ["cfa"], n=8)
+    scaled("B32", "B8", -1.0, n=8)
+    gp(lambda: g.affine_select(T.t5[:], T.BM[:], [[1, 128]], OP.is_gt, 0.0, 0, -1), ["BM"], ["t5"], 128)
+    gp(io(T.iX[:], [[0, 8], [256, 16]], 0, 0), [], ["iX"], 128)
+    scaled("Ls32", "t5", 128.0)
+    scaled("Lsn", "t5", -128.0)
+    mat("E64", "iU", c63, 1.0, ["cfb"])
+    act(None, T.MV[:, 0:64], T.E64[:, 0:64], AF.Identity, ["E64"], ["MV0"], 64, scale=-33.0)
+    act(None, T.MV[:, 64:128], T.E64[:, 64:128], AF.Identity, ["E64"], ["MV1"], 64)
+    add(None, "V", lambda: V.memset(T.HL[:], 0.0), [], [("HL", 0), ("HL", 1)], vc(320, 0.5))
+    if opt["lo"] != "V":
+        add(None, "V", lambda: V.memset(T.gg[:], 0.0), [], [("gg", 0), ("gg", 1)], vc(192, 1))
+        scaled("I32", "I128", 1.0 / 128)
+        scaled("In16", "I128", -1.0 / 128)
+    mat("G8", "iG", cG8, 1.0, ["cfb"])
+    ts(None, T.cj[:], T.iM[:, 0:8], cJ, None, EQ, None, ["iM", "cfb"], ["cj"], 8)
+    for i in range(4):
+        act(None, T.TH[:, 128 * i:128 * i + 128], T.G8[:], AF.Identity, ["G8", "cj"], [("TH", i)], 128, scale=T.cj[:, i:i + 1])
+    THK = [("TH", i) for i in range(4)]
+    scaled("In8", "I128", -8.0 / 128)
     c0, k0 = vcol(cX, 0.0, 8.0, EQ, MUL, ["cfa"])
     cWc, kWc = col(c0, 1.0, 0.5, [k0])
     mat("WBc", "iM", cWb, cWc, [kWb, kWc], n=192)
-    cWy, kWy = col(cX, 1.0, 1.0, ["cfa"])
-    scaled("WBz", "WBr", cWy, [kWy], n=192)
-    mat("WBy", "iM", cWb, cWy, [kWb, kWy], n=192)
-    gp(io(T.cnt[:], [[1, 64], [0, 16]], 0, 0), [], [("cnt", 0), ("cnt", 1)], R)
-    ts(T.TH[:], T.cnt[:], c63, None, EQ, None, [("cnt", 0), ("cnt", 1), "cfb"], ["TH"], R, 0.5)
-    gp(io(T.KB[0:64, :], [[0, 64], [-256, 16]], -256, 0), [], ["KB0"], R)
-    gp(io(T.KB[64:128, :], [[0, 64], [256, 16]], 0, 0), [], ["KB1"], R)
-    for u in range(2):
-        a = T.KB[64 * u:64 * u + 64, :]
-        gp((lambda a: (lambda: g.affine_select(a, a, [[-1, 64], [0, 16]], EQ, 0.0, 0, 1)))(a), ["KB%d" % u], ["KB%d" % u], R)
     c78, k78 = vcol(cG8, 7.0, None, OP.not_equal, None, ["cfb"])
     ca, ka = col(c63, 1.0, 1.0, ["cfb"])
-    mat("E64", "iU", c63, 1.0, ["cfb"])
-    mat("t3", "iU", ca, c78, [ka, k78])
-    tt(T.Sh[:], T.t3[:], T.E64[:], ADD, ["t3", "E64"], ["Sh"], 128)
-    act(T.MV[:, 0:64], T.E64[:, 0:64], AF.Identity, ["E64"], ["MV0"], 64, scale=-33.0)
-    act(T.MV[:, 64:128], T.E64[:, 64:128], AF.Identity, ["E64"], ["MV1"], 64)
-    cb, kb = col(cG8, 16.0, cJ, ["cfb"])
-    mat("bk0", "iM", cb, 1.0, [kb])
-    cc, kc = col(cb, 1.0, 8.0, [kb])
-    mat("bk1", "iM", cc, 1.0, [kc])
-    scaled("bw0", "bk0", float(W))
-    scaled("bw1", "bk1", float(W))
+    mat("t2", "iU", ca, c78, [ka, k78])
+    tt(None, T.Sh[:], T.t2[:], T.E64[:], ADD, ["t2", "E64"], ["Sh"], 128, 2)
     ca, ka = vcol(cG8, 0.0, cU, EQ, ADD, ["cfb"])
     cSq, kSq = col(ca, 1.0, -10.0, [ka])
+    ca, ka = col(cU, 2.0, -1.0, ["cfb"])
+    cb2, kb2 = col(cU, 256.0, -256.0, ["cfb"])
+    act(None, T.t4[:], T.iX[:], AF.Identity, ["iX", ka, kb2], ["t4"], 128, bias=cb2, scale=ca)
+    tt(None, T.KA[:], T.t4[:], T.G8[:], MUL, ["t4", "G8"], ["KA"], 128, 2)
+    for i in range(8):
+        ts(None, T.KB[:, 128 * i:128 * i + 128], T.KA[:], T.cj[:, i:i + 1], None, MUL, None, ["KA", "cj"], [("KB", i)], 128, 0.5)
+    KBK = [("KB", i) for i in range(8)]
     ca, ka = vcol(cX, 1.0, cX, ADD, MUL, ["cfa"])
     cSe, kSe = col(ca, -256.0, 0.0, [ka])
+    scaled("bk0", "bw0", 1.0 / W)
+    scaled("bk1", "bw1", 1.0 / W)
+    mat("WAe", "iM", cWa, 16.0, [kWa], n=144)
 
-    send([(1, [T.nl[:, 0:64]], T.nin[:, 0:64], 0, [("nin", 0, 0), ("nin", 0, 1)])], [("nl", 0, 0), ("nl", 0, 1)], 16e3)
+    send("sn", [(1, [T.nl[:, 0:64]], T.nin[:, 0:64], 0, [("nin", 0)])], [("nl", 0, 0), ("nl", 0, 1), "pool"], 16e3)
 
     Qr, Qx = T.Qw[:, 0:W], T.Qw[:, :]
     hs_ = lambda b, h, o=0: b[:, o + 512 * h:o + 512 * h + 512]
     qs_ = lambda b, u, o=0: b[:, o + 256 * u:o + 256 * u + 256]
     rot = [0, 1, 2]
 
+    def pq_(b, slot, k, a, e):
+        o = 2 * slot * R + (a // 2) * R + 512 * k + 256 * (a % 2)
+        return b[:, o:o + 256 * (e - a)]
+
     def h_step(t):
         off = (TK - 1 - t) % NR
         if off == 0:
             lst, o, key = T.nl, (t + 1) * 64, lambda h: ("nl", t + 1, h)
         elif off == 1:
-            lst, o, key = T.nin, (t + 1) * 64, lambda h: ("nin", t + 1, h)
+            lst, o, key = T.nin, (t + 1) * 64, lambda h: ("nin", t + 1)
         else:
-            lst, o, key = T.hl, (off - 2) * 64, lambda h: ("hl", off, h)
+            lst, o, key = T.hl, (off - 2) * 64, lambda h: ("hl", off)
         for u in range(4):
             vi, h = T.Vt[:, :].indirect(lst[:, o + 16 * u:o + 16 * u + 16]), u // 2
             if t == 0:
-                act(qs_(T.hA, u), vi, AF.Tanh, ["Vt", key(h)], [("hA", u)], 256, GA)
+                act("Vg%d" % u, qs_(T.hA, u), vi, AF.Tanh, ["Vt", key(h)], [("hA", u)], 256, "ga")
             elif t < TK - 1:
-                act(qs_(T.Vg, u), vi, AF.Copy, ["Vt", key(h)], [("Vg", u)], 256, GA)
+                copy("Vg%d" % u, qs_(T.Vg, u), vi, ["Vt", key(h)], [("Vg", u)], 256, "ga")
             else:
-                tt(qs_(T.hs, u), vi, qs_(T.hA, u), ADD, ["Vt", key(h), ("hA", u)], [("hs", u)], 256, GA)
-                act(qs_(T.hs, u), qs_(T.hs, u), AF.Tanh, [("hs", u)], [("hs", u)], 256)
+                tt("hv%d" % u, qs_(T.hs, u), vi, qs_(T.hA, u), ADD, ["Vt", key(h), ("hA", u)], [("hs", u)], 256, "ga")
+                act("ht%d" % u, qs_(T.hs, u), qs_(T.hs, u), AF.Tanh, [("hs", u)], [("hs", u)], 256)
                 if u % 2:
-                    dma("Y", hs_(T.yh, h), hs_(T.hs, h), [("hs", u - 1), ("hs", u)], [("yh", h)], 3.0)
+                    dma("Y", hs_(T.yh, h), hs_(T.hs, h), [("hs", u - 1), ("hs", u)], [("yh", h)], 256e3)
         if 0 < t < TK - 1:
             hk = [("hA", u) for u in range(4)]
-            dma("G", T.hA[:], T.Vg[:], hk + [("Vg", u) for u in range(4)], hk, 4.0, accum=True)
+            dma("G", T.hA[:], T.Vg[:], hk + [("Vg", u) for u in range(4)], hk, 1000e3, accum=True, name="ha")
             for h in range(2):
-                act(hs_(T.hA, h), hs_(T.hA, h), AF.Tanh, hk[2 * h:2 * h + 2], hk[2 * h:2 * h + 2], 512)
+                act("th%d" % h, hs_(T.hA, h), hs_(T.hA, h), AF.Tanh, hk[2 * h:2 * h + 2], hk[2 * h:2 * h + 2], 512)
 
     for t in range(TK):
+        tok[0] = t
         par, o2, oc = t % 2, (t % 2) * R, t * 64
         UK = ["u0a", "u0b"] if t == 0 else ["ura", "urb"]
         bank = lambda k, h: T.ps[:, 512 * (3 * h + rot[k]):512 * (3 * h + rot[k]) + 512]
         bk = lambda k, h: ("b", 3 * h + rot[k])
-        sm = lambda h, a, n, st=1: T.ps[:, 512 * (6 + h) + a:512 * (6 + h) + a + n:st]
+        sm = lambda h, a, n: T.ps[:, 512 * (6 + h) + a:512 * (6 + h) + a + n]
         sk = lambda h, a: ("b", 6 + h, a)
         ud = lambda k, h: T.uu[0:8, (2 * t + k) * R + 512 * h:(2 * t + k) * R + 512 * h + 512]
         ua = lambda k, h, n: T.uu[32:32 + n, (3 * t + k) * R + 512 * h:(3 * t + k) * R + 512 * h + 512]
         QK = lambda h: [("q", par, 2 * h), ("q", par, 2 * h + 1)]
         DK = lambda h: [("d", par, 2 * h), ("d", par, 2 * h + 1)]
         lh = lambda b, h: b[:, oc + 32 * h:oc + 32 * h + 32]
-
-        def reduce_list(wide, src, h, out, last=True):
-            return [(out, wide[:, 15 - j:143 - j], src[:, 512 * h + j:512 * h + 512:16], False, last and j == 15, 64) for j in range(16)]
-
         fh = lambda b, h: b[:, 2 * oc + 64 * h:2 * oc + 64 * h + 64]
+        c64 = lambda b, h: b[:, 64 * h:64 * h + 64]
 
-        def reduce_fold(wide, src, h, out, first=False):
-            return [(out, wide[:, 56 - 8 * i:184 - 8 * i], src[:, 512 * h + i:512 * h + 512:8], first and i == 0, i == 7, 64) for i in range(8)]
+        def fold(wide, src, out, first):
+            return [(out, wide[:, 56 - 8 * i:184 - 8 * i], src[:, i:512:8], first and i == 0, i == 7, 64) for i in range(8)]
 
-        def unfold(w, src, h, out, last):
-            return [(out, T[w + str(b)][:], src[:, 64 * h + b:64 * h + 64:2], False, last and b == 1, 64) for b in range(2)]
+        def listed(wide, src, out, n):
+            return [(out, wide[:, 15 - j:143 - j], src[:, j:n:16], False, j == 15, 64) for j in range(16)]
+
+        def unfold(w, src, out, first, last):
+            return [(out, T[w + str(b)][:], src[:, b:64:2], first and b == 0, last and b == 1, 64) for b in range(2)]
+
+        def offsets(pn, vn, items, rd, dst, h):
+            mm(pn, [(sm(h, 0, 32), T.I16[:], lh(T.sP, h), True, False, 64)] + items, ["I16", "sP"] + rd, [sk(h, 0)])
+            ts(vn, T[dst][:, 32 * h:32 * h + 32], sm(h, 0, 32), 1024.0, None, ADD, None, [], [sk(h, 0), (dst, h)], 32)
 
         for h in range(2):
-            mm([(bank(0, h), T.SA[0:8, :], ud(0, h), True, False, 512)], ["SA"] + UK, [bk(0, h)])
-            mm([(bank(1, h), T.SC[32:41, :], ua(0, h, 9), True, True, 512)], ["SC", "u1"] + UK, [bk(1, h)])
+            mm("a%d" % h, [(bank(0, h), T.SA[0:8, :], ud(0, h), True, False, 512)], ["SA"] + UK, [bk(0, h)])
+            mm("c%d" % h, [(bank(1, h), T.SC[32:40, :], ua(0, h, 8), True, True, 512)], ["SC"] + UK, [bk(1, h)])
         for u in range(4):
             lst = T.nl[:, oc + 16 * u:oc + 16 * u + 16]
-            act(qs_(T.qa, u, o2), Qr.indirect(lst), AF.Copy, ["Q", ("nl", t, u // 2)], [("q", par, u)], 256, GA)
-            tt(qs_(T.da, u, o2), T.Pt[:, :].indirect(lst), qs_(T.qa, u, o2), SUB, ["P", ("nl", t, u // 2), ("q", par, u)], [("d", par, u)], 256, GA)
+            copy("q%d" % u, pq_(T.pq, par, 1, u, u + 1), Qr.indirect(lst), ["Q", ("nl", t, u // 2)], [("q", par, u)], 256, "ga")
+            copy("p%d" % u, pq_(T.pq, par, 0, u, u + 1), T.Pt[:, :].indirect(lst), ["P", ("nl", t, u // 2)], [("d", par, u)], 256, "ga")
         for h in range(2):
-            q, d = hs_(T.qa, h, o2), hs_(T.da, h, o2)
-            send([(1, [d, T.zer[:]], hs_(T.rin, h, t * R), 2, [("r", t, h)]), (1, [d, q], hs_(T.pin, h, t * R), 1, [("p", t, h)])],
-                 QK(h) + DK(h) + ["zer"], 400e3)
-            mm([(bank(0, h), T.Lc[:], q, False, True, 512)], ["Lc"] + QK(h), [bk(0, h)])
-            act(hs_(T.m1, h), bank(0, h), AF.Sign, [], [bk(0, h), ("m1", h)], 512, bias=-0.5)
-            tt(hs_(T.pr, h), bank(1, h), q, MUL, QK(h), [bk(1, h), ("pr", h)], 512)
-            mm([(bank(2, h), T.I128[:], d, True, False, 512)], ["I128"] + DK(h), [bk(2, h)])
-            mm([(bank(2, h), T.Dm[:], hs_(T.m1, h), False, True, 512)], ["Dm", ("m1", h)], [bk(2, h)])
-            tt(hs_(T.cm, h), bank(2, h), hs_(T.pr, h), OP.is_gt, [("pr", h)], [bk(2, h), ("cm", h)], 512)
-            mm([(sm(h, 0, 32), T.I16[:], lh(T.sP, h), True, False, 64)] + reduce_list(T.WAz, T.cm, h, sm(h, 0, 32)),
-               ["I16", "sP", "WAz", ("cm", h)], [sk(h, 0)])
-            ts(T.of1[:, 32 * h:32 * h + 32], sm(h, 0, 32), 1024.0, None, ADD, None, [], [sk(h, 0), ("of1", h)], 32)
-            mm(reduce_fold(T.WBz, T.cm, h, sm(h, 384, 64), True), ["WBz", ("cm", h)], [sk(h, 384)])
-            act(fh(T.Z1, h), sm(h, 384, 64), AF.Copy, [], [sk(h, 384), ("Z1", t, h)], 64)
-            send([(1, [fh(T.Z1, h)], fh(T.Zin, h), 0, [("Zin", t, h)])], [("Z1", t, h)], 16e3)
+            q, d = pq_(T.pq, par, 1, 2 * h, 2 * h + 2), pq_(T.pq, par, 0, 2 * h, 2 * h + 2)
+            send("sr%d" % h, [(1, [T.pq[:, (2 * par + h) * R:(2 * par + h + 1) * R]], T.pin[:, (2 * t + h) * R:(2 * t + h + 1) * R], 0, [("p", t, h)])],
+                 QK(h) + DK(h), 256e3)
+            mm("L%d" % h, [(bank(0, h), T.Lc[:], q, False, True, 512)], ["Lc"] + QK(h), [bk(0, h)])
+            act("m%d" % h, hs_(T.m1, h), bank(0, h), AF.Sign, [], [bk(0, h), ("m1", h)], 512, bias=-0.5)
+            tt("pr%d" % h, hs_(T.pr, h), bank(1, h), q, MUL, QK(h), [bk(1, h), ("pr", h)], 512)
+            mm("e%d" % h, [(bank(2, h), T.I128[:], d, True, False, 512)], ["I128"] + DK(h), [bk(2, h)])
+            mm("D%d" % h, [(bank(2, h), T.Dm[:], hs_(T.m1, h), False, True, 512)], ["Dm", ("m1", h)], [bk(2, h)])
+            tt("cm%d" % h, hs_(T.cm, h), bank(2, h), hs_(T.pr, h), OP.is_gt, [("pr", h)], [bk(2, h), ("cm", h)], 512)
+            if h in opt["direct"]:
+                offsets("uo%d" % h, "o1%d" % h, listed(T.WAz, hs_(T.cm, h), sm(h, 0, 32), 512), ["WAz", ("cm", h)], "of1", h)
+            mm("fz%d" % h, fold(T.WBy, hs_(T.cm, h), sm(h, 32, 64), True), ["WBy", ("cm", h)], [sk(h, 32)])
+            copy("Z%d" % h, fh(T.Z1, h), sm(h, 32, 64), [], [sk(h, 32), ("Z1", t, h)], 64)
+            if h not in opt["direct"]:
+                offsets("uo%d" % h, "o1%d" % h, unfold("bw", fh(T.Z1, h), sm(h, 0, 32), False, True), ["bw0", "bw1", ("Z1", t, h)], "of1", h)
+        send("sz", [(1, [T.Z1[:, 2 * oc:2 * oc + 128]], T.Zin[:, 2 * oc:2 * oc + 128], 0, [("Zin", t)])], [("Z1", t, 0), ("Z1", t, 1)], 32e3)
+        su, DW = newsem("d"), [("dW", par, x) for x in range(16)]
+        for x in range(16):
+            dma("Y", T.dW[x:128:16, o2:o2 + R], T.ua[:, (3 * t + 1) * R:(3 * t + 2) * R], ["E"], [DW[x]], 100e3, su)
         if t == 0:
             su = newsem("d")
-            dma("Y", T.uu[0:8, 2 * R:2 * TK * R], T.ud[:, 2 * R:], [("r", 0, 1)], ["ura"], 4.0, su)
-            dma("Y", T.uu[32:40, 3 * R:], T.ua[:, 3 * R:], [("r", 0, 1)], ["urb"], 4.0, su)
-            dma("Y", T.Vt[:], T.vf[:], [("p", 0, 1)], ["Vt"], 6.0)
-        for (a, b) in X1:
-            tt(Qx.indirect(T.of1[:, 16 * a:16 * b]), T.da[:, o2 + 256 * a:o2 + 256 * b], T.qa[:, o2 + 256 * a:o2 + 256 * b], ADD,
-               [k for u in range(a, b) for k in (("of1", u // 2), ("q", par, u), ("d", par, u))], ["Q"], 256 * (b - a), SCAT)
+            dma("Y", T.uu[0:8, 2 * R:2 * TK * R], T.ud[:, 2 * R:], [("p", 0, 1)], ["ura"], 200e3, su)
+            dma("Y", T.uu[32:40, 3 * R:], T.ua[:, 3 * R:], [("p", 0, 1)], ["urb"], 400e3, su)
+            dma("G", T.Vt[:], T.vf[:], [("Zin", 0)], ["Vt"], 700e3, name="lv")
+        mm("eT", [(sm(0, 128 + 8 * j, 8), ua(2, j // 4, 8)[:, 128 * (j % 4):128 * (j % 4) + 128], T.I1[32:40, 32:40], j == 0, j == 7, 64)
+                  for j in range(8)], ["I1"] + UK, [sk(0, 128)])
+        copy("eC", T.eT[:], sm(0, 128, 64), [], [sk(0, 128), "eT"], 64)
+        for (a, b) in opt["x1"]:
+            cp("x1%d" % a, Qx.indirect(T.of1[:, 16 * a:16 * b]), pq_(T.pq, par, 0, a, b),
+               [k for u in range(a, b) for k in (("of1", u // 2), ("d", par, u))], ["Q"], 256 * (b - a), "sc")
         for u in range(4):
-            act(qs_(T.Eg, u), T.Et[:, :].indirect(T.nin[:, oc + 16 * u:oc + 16 * u + 16]), AF.Copy, ["E", ("nin", t, u // 2)], [("Eg", u)], 256, GA)
-        if t > 0:
-            h_step(t - 1)
+            copy("Eg%d" % u, qs_(T.Eg, u), T.Et[:, :].indirect(T.nin[:, oc + 16 * u:oc + 16 * u + 16]), ["E", ("nin", t)], [("Eg", u)], 256, "ga")
         for h in range(2):
-            r = hs_(T.rin, h, t * R)
-            mm([(bank(0, h), T.SA[0:8, :], ud(1, h), True, False, 512)], ["SA"] + UK, [bk(0, h)])
-            mm([(bank(1, h), T.Jh[:], r, True, True, 512)], ["Jh", ("r", t, h)], [bk(1, h)])
-            if FY:
-                act(hs_(T.Sb, h), bank(1, h), AF.Copy, [], [bk(1, h), ("Sb", h)], 512)
-                mm([(bank(1, h), T.SD[32:40, :], ua(1, h, 8), True, False, 512)], ["SD"] + UK, [bk(1, h)])
-            mm([(bank(2, h), T.I128[:], r, True, True, 512)], ["I128", ("r", t, h)], [bk(2, h)])
-        for h in range(2):
-            mm([(sm(h, 64, 64), T.WBr[:, 56 - 8 * i:184 - 8 * i], T.rin[:, t * R + 512 * h + 64 * i:t * R + 512 * h + 64 * i + 64], i == 0, False, 64)
-                for i in range(8)], ["WBr", ("r", t, h), ("of1", h)], [sk(h, 64)], 1)
+            r = hs_(T.rr, h)
+            mm("b%d" % h, [(bank(0, h), T.SA[0:8, :], ud(1, h), True, False, 512)], ["SA"] + UK, [bk(0, h)])
+            mm("U%d" % h, [(bank(1, h), T.I1[:], pq_(T.pin, t, 0, 2 * h, 2 * h + 2), True, False, 512),
+                           (bank(1, h), T.In1[:], pq_(T.pin, t, 1, 2 * h, 2 * h + 2), False, True, 512)], ["I1", "In1", ("p", t, h)], [bk(1, h)])
+            act("r%d" % h, r, bank(1, h), AF.Relu, [], [bk(1, h), ("r", h)], 512)
+            mm("J%d" % h, [(bank(1, h), T.Jh[:], r, True, True, 512)], ["Jh", ("r", h)], [bk(1, h)])
+            mm("R%d" % h, [(bank(2, h), T.I128[:], r, True, False, 512)], ["I128", ("r", h)], [bk(2, h)])
         for u in range(4):
-            qi = Qr.indirect(T.nin[:, oc + 16 * u:oc + 16 * u + 16])
-            if u in VG:
-                cp(qs_(T.q2, u), qi, ["Q", ("nin", t, u // 2)], [("q2", u)], 256, GA)
-            else:
-                act(qs_(T.q2, u), qi, AF.Copy, ["Q", ("nin", t, u // 2)], [("q2", u)], 256, GA)
+            copy("g%d" % u, qs_(T.q2, u), Qr.indirect(T.nin[:, oc + 16 * u:oc + 16 * u + 16]), ["Q", ("nin", t)], [("q2", u)], 256, "ga")
         for h in range(2):
-            r, q2, K2 = hs_(T.rin, h, t * R), hs_(T.q2, h), [("q2", 2 * h), ("q2", 2 * h + 1)]
-            c64 = slice(64 * h, 64 * h + 64)
-            mm([(bank(0, h), T.Lc[:], q2, False, True, 512)], ["Lc"] + K2, [bk(0, h)])
-            act(hs_(T.m2, h), bank(0, h), AF.Sign, [], [bk(0, h), ("m2", h)], 512, bias=-0.5)
-            if FY:
-                tt(hs_(T.yy, h), Qr.indirect(lh(T.nin, h)), hs_(T.Sb, h), MUL, ["Q", ("nin", t, h), ("Sb", h)], [("yy", h)], 512, GA)
-            else:
-                tt(hs_(T.yy, h), bank(1, h), q2, MUL, K2, [bk(1, h), ("yy", h)], 512)
-            tt(hs_(T.mn, h), bank(2, h), hs_(T.yy, h), OP.min, [("yy", h)], [bk(2, h), ("mn", h)], 512)
-            if not FY:
-                mm([(bank(1, h), T.SD[32:40, :], ua(1, h, 8), True, False, 512)], ["SD"] + UK, [bk(1, h)])
-            for i0 in (0, 4):
-                mm([(sm(h, 64, 64), T.WB32[:, 56 - 8 * i:184 - 8 * i], T.mn[:, 512 * h + 64 * i:512 * h + 64 * i + 64], False, i == 7, 256)
-                    for i in range(i0, i0 + 4)], ["WB32", ("mn", h), ("i", i0)], [sk(h, 64)], -1 if i0 else 0)
-            mm([(bank(1, h), T.Dn[:], hs_(T.m2, h), False, True, 512)], ["Dn", ("m2", h)], [bk(1, h)])
-            mm([(bank(2, h), T.Lsn[:], r, True, False, 512)], ["Lsn", ("r", t, h)], [bk(2, h)])
+            r, q2, K2 = hs_(T.rr, h), hs_(T.q2, h), [("q2", 2 * h), ("q2", 2 * h + 1)]
+            mn = hs_(T.mn, h)
+            mm("M%d" % h, [(bank(0, h), T.Lc[:], q2, False, True, 512)], ["Lc"] + K2, [bk(0, h)])
+            act("n%d" % h, hs_(T.m2, h), bank(0, h), AF.Sign, [], [bk(0, h), ("m2", h)], 512, bias=-0.5)
+            tt("y%d" % h, bank(1, h), bank(1, h), q2, MUL, K2, [bk(1, h)], 512)
+            tt("mn%d" % h, mn, bank(1, h), r, OP.min, [("r", h), bk(1, h)], [("mn", h)], 512)
+            tt("pq%d" % h, hs_(T.pr, h), bank(1, h), hs_(T.dW, h, o2), MUL, DW + [bk(1, h)], [("pr", h)], 512)
+            mm("E%d" % h, [(bank(2, h), T.Dm[:], hs_(T.m2, h), False, True, 512)], ["Dm", ("m2", h)], [bk(2, h)])
+            tt("cn%d" % h, hs_(T.cn, h), bank(2, h), hs_(T.pr, h), OP.is_gt, [("pr", h)], [bk(2, h), ("cn", h)], 512)
+            mm("fy%d" % h, [(sm(h, 256, 64), T.MV[:], fh(T.Zin, h), True, False, 64)] + fold(T.WBy, hs_(T.cn, h), sm(h, 256, 64), False),
+               ["MV0", "MV1", ("Zin", t), "WBy", ("cn", h)], [sk(h, 256)])
+            act("u%d" % h, c64(T.u2, h), sm(h, 256, 64), AF.Relu, [], [sk(h, 256), ("u2", h)], 64)
+            if t < TK - 1:
+                offsets("up%d" % h, "o2%d" % h, unfold("bw", c64(T.u2, h), sm(h, 0, 32), False, True), ["bw0", "bw1", ("u2", h)], "of2", h)
+            tot = sm(h, 96, 32)
+            mm("fw%d" % h, [(tot[:, 8 * j:8 * j + 8], r[:, 128 * j:128 * j + 128], T.B8[:], j == 0, False, 64) for j in range(4)]
+               + [(tot[:, 8 * j:8 * j + 8], mn[:, 128 * j:128 * j + 128], T.B32[:], False, j == 3, 256) for j in range(4)],
+               ["B8", "B32", ("r", h), ("mn", h)], [sk(h, 96)])
+            mm("N%d" % h, [(bank(0, h), T.Lsn[:], r, True, False, 512)], ["Lsn", ("r", h)], [bk(0, h)])
             for u in range(2):
-                mm([(bank(2, h)[:, 256 * u:256 * u + 256], T.Ls32[:], qs_(T.mn, 2 * h + u), False, False, 1024)], ["Ls32", ("mn", h), ("i", u)], [bk(2, h)])
-            tt(bank(1, h), bank(1, h), hs_(T.yy, h), MUL, [("yy", h)], [bk(1, h), ("pq", h)], 512)
-            tt(hs_(T.cm, h), bank(1, h), hs_(T.mn, h), OP.is_lt, [("pq", h), ("mn", h)], [bk(1, h), ("cm", h)], 512)
-            tt(T.gg[:, c64], sm(h, 64, 64), T.eB[:, t, h, :], MUL, EB, [sk(h, 64), ("gg", h)], 64)
-            cp(T.HL[:, c64], T.gg[:, c64], [("gg", h)], [("HL", h)], 64)
-            tt(T.HL[64:128, c64], T.gg[64:128, c64], T.HL[64:128, c64], SUB, [("gg", h), ("HL", h)], [("HL", h)], 64, 2)
-            mm([(bank(2, h)[:, 64 * i:64 * i + 64], T.TH[:, 128 * i:128 * i + 128], T.HL[:, c64], False, i == 7, 64) for i in range(8)],
-               ["TH", ("HL", h)], [bk(2, h)])
-            act(hs_(T.cnt, h), bank(2, h), AF.Sign, [], [bk(2, h), ("cnt", h)], 512, bias=1.0 / 512)
-            mm([(sm(h, 448, 64), T.MA[:], fh(T.Zin, h), True, False, 64)] + reduce_fold(T.WBy, T.cm, h, sm(h, 448, 64)),
-               ["MA", ("Zin", t, h), "WBy", ("cm", h)], [sk(h, 448)])
-            act(T.u2[:, c64], sm(h, 448, 64), AF.Relu, [], [sk(h, 448), ("u2", h)], 64)
-            if t < TK - 1:
-                mm([(sm(h, 352, 32), T.I16[:], lh(T.sP, h), True, False, 64)] + unfold("bw", T.u2, h, sm(h, 352, 32), True),
-                   ["I16", "sP", "bw0", "bw1", ("u2", h)], [sk(h, 352)])
-                ts(T.of2[:, 32 * h:32 * h + 32], sm(h, 352, 32), 1024.0, None, ADD, None, [], [sk(h, 352), ("of2", h)], 32)
+                mm("C%d" % (2 * h + u), [(bank(0, h)[:, 256 * u:256 * u + 256], T.Ls32[:], qs_(T.mn, 2 * h + u), False, False, 1024)],
+                   ["Ls32", ("mn", h)], [bk(0, h)])
+            e, hi, lo = T.eT[:, 32 * h:32 * h + 32], T.HL[:, 128 * h:128 * h + 32], T.HL[:, 128 * h + 64:128 * h + 96]
+            tr = sm(h, 128, 128)
+            if opt["lo"] == "V":
+                tt("gA%d" % h, hi, tot, e, MUL, ["eT"], [sk(h, 96), ("HL", h)], 32)
+                tt("gB%d" % h, tot, tot, e, MUL, ["eT"], [sk(h, 96)], 32)
+                tt("gC%d" % h, lo, tot, hi, SUB, [("HL", h), sk(h, 96)], [sk(h, 96), ("HL", h)], 32)
+                mm("tr%d" % h, [(tr, T.HL[:, 128 * h:128 * h + 128], T.I16[:], True, True, 128)], ["I16", ("HL", h)], [sk(h, 128)])
+            else:
+                gg, o = T.gg[:, 96 * h + 64:96 * h + 96], 128 * h + 64
+                tt("gB%d" % h, gg, tot, e, MUL, ["eT"], [sk(h, 96), ("gg", h)], 32)
+                if opt["lo"] == "S":
+                    copy("gA%d" % h, lo, gg, [("gg", h)], [("HL", h)], 32)
+                else:
+                    tt("gA%d" % h, lo, tot, e, MUL, ["eT"], [sk(h, 96), ("HL", h)], 32)
+                mm("tr%d" % h, [(tr[0:96, :], T.gg[:, 96 * h:96 * h + 96], T.I32[:], True, False, 512),
+                                (tr[0:96, :], T.HL[:, o:o + 96], T.I16[:], False, False, 128),
+                                (tr[0:96, :], T.HL[:, o - 64:o + 32], T.In16[:], False, True, 128)],
+                   ["I16", "In16", "I32", ("HL", h), ("gg", h)], [sk(h, 128)])
+            hf = T.HF[:, 128 * h:128 * h + 128]
+            tr, hf = (tr, hf) if opt["lo"] == "V" else (tr[0:96, :], hf[0:96, :])
+            copy("hF%d" % h, hf, tr, [], [sk(h, 128), ("HF", h)], 128)
+            mm("Th%d" % h, [(bank(0, h)[:, 128 * j:128 * j + 128], T.TH[0:hf.shape[0], 128 * j:128 * j + 128], hf, False, j == 3, 128) for j in range(4)],
+               THK + [("HF", h)], [bk(0, h)])
+            act("ct%d" % h, hs_(T.cnt, h), bank(0, h), AF.Sign, [], [bk(0, h), ("cnt", h)], 512, bias=1.0 / 512)
         if t < TK - 1:
-            for (a, b) in X2:
-                cp(Qx.indirect(T.of2[:, 16 * a:16 * b]), T.pin[:, t * R + 256 * a:t * R + 256 * b],
-                   [k for u in range(a, b) for k in (("of2", u // 2), ("p", t, u // 2), ("i", u))], ["Q"], 256 * (b - a), SCAT)
+            for (a, b) in opt["x2"]:
+                cp("x2%d" % a, Qx.indirect(T.of2[:, 16 * a:16 * b]), pq_(T.pin, t, 0, a, b),
+                   [k for u in range(a, b) for k in (("of2", u // 2), ("p", t, u // 2))], ["Q"], 256 * (b - a), "sc")
         for h in range(2):
-            c64 = slice(64 * h, 64 * h + 64)
-            ub = T.ub[:, c64]
-            mm([(bank(0, h), T.I1[:], hs_(T.Eg, h), True, False, 512)], ["I1", ("Eg", 2 * h), ("Eg", 2 * h + 1)], [bk(0, h)])
-            mm([(sm(h, 128, 64), T.MV[:], T.u2[:, c64], True, False, 64)] + reduce_fold(T.WBc, T.cnt, h, sm(h, 128, 64)),
-               ["WBc", "MV0", "MV1", ("cnt", h), ("u2", h)], [sk(h, 128)])
-            act(ub, sm(h, 128, 64), AF.Relu, [], [sk(h, 128), ("ub", h)], 64)
-            mm([(sm(h, 192, 64), T.Sh[:], ub, True, True, 64)], ["Sh", ("ub", h)], [sk(h, 192)])
-            act(T.tb[:, c64], sm(h, 192, 64), AF.Sign, [], [sk(h, 192), ("tb", h)], 64, bias=-17.5)
-            mm([(sm(h, 256, 64), T.Sh[:], ub, True, False, 64), (sm(h, 256, 64), T.In8[:], T.tb[:, c64], False, True, 64)],
-               ["Sh", "In8", ("ub", h), ("tb", h)], [sk(h, 256)])
-            act(T.kk[:, c64], sm(h, 256, 64), AF.Square, [kSq], [sk(h, 256), ("kk", h)], 64, bias=cSq)
-            mm([(bank(0, h)[:, i:512:8], T.KB[:, 128 * i:128 * i + 128], T.kk[:, c64], False, i == 7, 64) for i in range(8)],
-               ["KB0", "KB1", ("kk", h)], [bk(0, h)])
-            act(hs_(T.sel, h), bank(0, h), AF.Relu, [kSe], [bk(0, h), ("sel", h)], 512, bias=cSe)
-            un = unfold("bk", T.ub, h, sm(h, 320, 32), False)
-            mm([un[0][:3] + (True, False, 64), un[1]], ["bk0", "bk1", ("ub", h), ("kk", h)], [sk(h, 320)], 1)
-            mm(reduce_list(T.WAe, T.sel, h, sm(h, 320, 32)), ["WAe", ("sel", h)], [sk(h, 320)], -1)
-            nn = T.nl[:, oc + 64 + 32 * h:oc + 96 + 32 * h]
-            ts(nn, sm(h, 320, 32), -1.0, None, ADD, None, [], [sk(h, 320), ("nl", t + 1, h)], 32)
-            if t < TK - 1:
-                it = [(1, [nn], T.nin[:, oc + 64 + 32 * h:oc + 96 + 32 * h], 0, [("nin", t + 1, h)])]
-                off = (TK - 1 - t) % NR
-                if off > 1:
-                    it.append((off, [nn], T.hl[:, (off - 2) * 64 + 32 * h:(off - 2) * 64 + 32 * h + 32], 0, [("hl", off, h)]))
-                send(it, [("nl", t + 1, h)], 8e3)
-        if t >= TK - 2:
-            a = 0 if t == TK - 2 else t
-            cp(T.nF[:, 64 * a:oc + 64], T.nl[:, 64 * a + 64:oc + 128], [("nl", k + 1, h) for k in range(a, t + 1) for h in range(2)],
-               [("nF", t)], oc + 64 - 64 * a)
-        rot = [rot[1], rot[2], rot[0]]
-    dma("S", T.yn[:], T.nF[:], [("nF", TK - 2), ("nF", TK - 1)], ["yn"], 2.5)
-    h_step(TK - 1)
+            ub = c64(T.ub, h)
+            mm("I%d" % h, [(bank(1, h), T.I1[:], hs_(T.Eg, h), True, False, 512)], ["I1", ("Eg", 2 * h), ("Eg", 2 * h + 1)], [bk(1, h)])
+            mm("fc%d" % h, [(sm(h, 320, 64), T.MV[:], c64(T.u2, h), True, False, 64)] + fold(T.WBc, hs_(T.cnt, h), sm(h, 320, 64), False),
+               ["WBc", "MV0", "MV1", ("cnt", h), ("u2", h)], [sk(h, 320)])
+            act("ub%d" % h, ub, sm(h, 320, 64), AF.Relu, [], [sk(h, 320), ("ub", h)], 64)
+            mm("s%d" % h, [(sm(h, 384, 64), T.Sh[:], ub, True, True, 64)], ["Sh", ("ub", h)], [sk(h, 384)])
+            act("tb%d" % h, c64(T.tb, h), sm(h, 384, 64), AF.Sign, [], [sk(h, 384), ("tb", h)], 64, bias=-17.5)
+            mm("k%d" % h, [(sm(h, 448, 64), T.Sh[:], ub, True, False, 64), (sm(h, 448, 64), T.In8[:], c64(T.tb, h), False, True, 64)],
+               ["Sh", "In8", ("ub", h), ("tb", h)], [sk(h, 448)])
+            act("kk%d" % h, c64(T.kk, h), sm(h, 448, 64), AF.Square, [kSq], [sk(h, 448), ("kk", h)], 64, bias=cSq)
+            mm("K%d" % h, [(bank(1, h)[:, i:512:8], T.KB[:, 128 * i:128 * i + 128], c64(T.kk, h), False, i == 7, 64) for i in range(8)],
+               KBK + [("kk", h)], [bk(1, h)])
+            act("se%d" % h, hs_(T.sel, h), bank(1, h), AF.Relu, [kSe], [bk(1, h), ("sel", h)], 512, bias=cSe)
+            if not opt["full"]:
+                nx_ = sm(h, 0, 32)
+                mm("v%d" % h, unfold("bk", ub, nx_, True, False), ["bk0", "bk1", ("ub", h), ("kk", h)], [sk(h, 0)], 1)
+                mm("W%d" % h, listed(T.WAe, hs_(T.sel, h), nx_, 512), ["WAe", ("sel", h)], [sk(h, 0)], -1)
+                ts("nn%d" % h, T.nl[:, oc + 64 + 32 * h:oc + 96 + 32 * h], nx_, -1.0, None, ADD, None, [], [sk(h, 0), ("nl", t + 1, h)], 32)
+        if opt["full"]:
+            nx_ = sm(0, 256, 64)
+            mm("v1", [(nx_, T["bk%d" % b][:], T.ub[:, b:128:2], b == 0, False, 64) for b in range(2)],
+               ["bk0", "bk1", ("ub", 0), ("ub", 1), ("kk", 0)], [sk(0, 256)], 1)
+            mm("W1", listed(T.WAe, T.sel, nx_, R), ["WAe", ("sel", 0), ("sel", 1)], [sk(0, 256)], -1)
+            ts("nn1", T.nl[:, oc + 64:oc + 128], nx_, -1.0, None, ADD, None, [], [sk(0, 256), ("nl", t + 1, 0), ("nl", t + 1, 1)], 64)
+        if t < TK - 1:
+            nn = T.nl[:, oc + 64:oc + 128]
+            it = [(1, [nn], T.nin[:, oc + 64:oc + 128], 0, [("nin", t + 1)])]
+            off = (TK - 1 - t) % NR
+            if off > 1:
+                it.append((off, [nn], T.hl[:, (off - 2) * 64:(off - 2) * 64 + 64], 0, [("hl", off)]))
+            send("sn", it, [("nl", t + 1, 0), ("nl", t + 1, 1)], 16e3)
+        else:
+            cp("nf", T.nF[:], T.nl[:, 64:], [("nl", k + 1, h) for k in range(TK) for h in range(2)], ["nF"], TK * 64)
+            dma("Y", T.yn[:], T.nF[:], ["nF"], ["yn"], 200e3)
+        h_step(t)
+        rot = [rot[2], rot[0], rot[1]]
     return ops
 
 
-def order(ops, bump=None):
+def times(o, c):
+    k, n = o["cost"]
+    if k == "cy":
+        return c["fix"] + n * c["cy"], 0.0
+    if k in ("ga", "sc"):
+        return c["fix"] + n * c[k] * c["cy"], 0.0
+    if k == "pcy":
+        return n * c["pcy"], 0.0
+    if k == "gp":
+        return 0.15 + 2 * n * c["cy"], 0.0
+    if k == "dma":
+        return (c["giss"] if o["eng"] == "G" else 0.08), c["dlat"] + n / c["bw"]
+    if k == "send":
+        return c["riss"], c["rlat"] + n / c["bw"]
+    return 0.0, 0.0
+
+
+def order(ops, lists=ORDER, c=COST):
     n = len(ops)
+    named, queue, fill = {}, {e: [] for e in "VSPGY"}, {e: [] for e in "VSPGY"}
+    for i, o in enumerate(ops):
+        if o["name"] == "ld" or o["eng"] == "Y":
+            queue[o["eng"]].append(i)
+        elif o["name"]:
+            named[(o["name"], o["tok"])] = i
+        elif o["eng"]:
+            fill[o["eng"]].append(i)
+    for t in range(-1, TK + 1):
+        for e, names in lists.items():
+            for w in names.split():
+                k = (w.rstrip("+-"), t + (w[-1] == "+") - (w[-1] == "-"))
+                if k in named and ops[named[k]]["eng"] == e:
+                    queue[e].append(named.pop(k))
+    assert not named, named
     deps = [dict(o["deps"]) for o in ops]
     succ = [[] for _ in ops]
     for i in range(n):
         for j in deps[i]:
             succ[j].append(i)
-    pri = [0.0] * n
-    for i in range(n - 1, -1, -1):
-        pri[i] = ops[i]["cost"] + ops[i]["done"] + LAT + max([pri[j] for j in succ[i]] + [0.0])
-    bump = BUMP if bump is None else bump
-    pri = [p + bump.get(o["role"], 0.0) for p, o in zip(pri, ops)]
     left = [len(d) for d in deps]
+    tm = [times(o, c) for o in ops]
     ready = {i: 0.0 for i in range(n) if left[i] == 0}
-    free, end, seq, user, held = {}, [0.0] * n, [], {}, {}
-    while ready:
-        st = {}
-        for i, r in ready.items():
-            o = ops[i]
-            if o["bank"]:
-                b = o["bank"][0]
-                if o["start"] and held.get(b):
-                    continue
-                if b in user and ops[user[b]]["eng"] != o["eng"]:
-                    r = max(r, end[user[b]] + LAT)
-            st[i] = max(r, free.get(o["eng"], 0.0))
-        i0 = min(st, key=lambda i: (st[i], -pri[i], i))
-        e = ops[i0]["eng"]
-        i = i0 if e is None else max((k for k in st if ops[k]["eng"] == e and st[k] <= st[i0] + LOOK), key=lambda k: (pri[k], -k))
+    free, end, seq, user, held = {e: 0.0 for e in queue}, [0.0] * n, [], {}, {}
+    head = {e: 0 for e in queue}
+
+    def can(i):
+        if i not in ready:
+            return None
+        o, r = ops[i], ready[i]
+        if o["bank"]:
+            b = o["bank"][0]
+            if o["start"] and held.get(b):
+                return None
+            if b in user and ops[user[b]]["eng"] != o["eng"]:
+                r = max(r, end[user[b]] + c["lat"])
+        return max(r, free[o["eng"]])
+
+    def done(i, at):
+        end[i] = at
+        seq.append(i)
         del ready[i]
+        for j in succ[i]:
+            left[j] -= 1
+            if left[j] == 0:
+                ready[j] = max(end[k] + ((c["same"] if raw else 0.0) if ops[k]["eng"] == ops[j]["eng"] and ops[k]["kind"] == "c" else c["lat"])
+                               for k, raw in deps[j].items())
+                if ops[j]["kind"] == "arr":
+                    done(j, ready[j] - c["lat"])
+
+    while len(seq) < n:
+        best = None
+        for e in queue:
+            a = can(queue[e][head[e]]) if head[e] < len(queue[e]) else None
+            pick = (a, queue[e][head[e]]) if a is not None else None
+            for i in fill[e]:
+                b = can(i)
+                if b is not None and (a is None or b + tm[i][0] <= a + 0.05) and (pick is None or b < pick[0] - 0.05):
+                    pick = (b, i)
+            if pick and (best is None or pick < best):
+                best = pick
+        assert best, "the queues wait for one another"
+        st, i = best
         o = ops[i]
+        e = o["eng"]
+        if i in fill[e]:
+            fill[e].remove(i)
+        else:
+            head[e] += 1
         if o["bank"]:
             b = o["bank"][0]
             if b in user:
@@ -482,16 +563,9 @@ def order(ops, bump=None):
             user[b] = i
             if o["hold"]:
                 held[b] = o["hold"] > 0
-        if e is not None:
-            free[e] = st[i] + o["cost"]
-        end[i] = st[i] + o["cost"] + o["done"]
-        seq.append(i)
-        for j in succ[i]:
-            left[j] -= 1
-            if left[j] == 0:
-                ready[j] = max(end[k] + (0.0 if ops[k]["eng"] == ops[j]["eng"] and ops[k]["kind"] == "c" and not raw else LAT)
-                               for k, raw in deps[j].items())
-    return seq, max(end), [dict(o, deps=d) for o, d in zip(ops, deps)]
+        free[e] = st + tm[i][0]
+        done(i, free[e] + tm[i][1])
+    return seq, end, [dict(o, deps=d) for o, d in zip(ops, deps)]
 
 
 def emit(g, T, ops, seq):

@@ -2,48 +2,47 @@ from concourse.bass import DstId, RemoteDMATransfer
 from concourse.mybir import AluOpType as OP, ActivationFunctionType as AF
 
 W, R, TK, NR = 2560, 1024, 6, 4
+SG = 2.0 ** -12
 H = 65536.0
 BF, F32, F16, I32, U16 = "bfloat16", "float32", "float16", "int32", "uint16"
 
 SCRATCH = {
-    "Qw": ("sbuf", [128, 17 * W], BF), "Pt": ("sbuf", [128, W], BF), "Et": ("sbuf", [128, W], BF), "Vt": ("sbuf", [128, W], BF),
-    "uu": ("sbuf", [128, 3 * TK * R], BF), "pin": ("sbuf", [128, 2 * TK * R], BF),
-    "pq": ("sbuf", [128, 4 * R], BF), "dW": ("sbuf", [128, 2 * R], BF), "rr": ("sbuf", [128, R], BF), "In1": ("sbuf", [128, 128], BF),
-    "TH": ("sbuf", [128, 512], F16),
-    "n0i": ("sbuf", [128, 64], I32), "spi": ("sbuf", [128, TK * 64], I32),
-    "sP": ("sbuf", [128, TK * 64], F16),
+    "Qw": ("sbuf", [128, 3 * W], F32), "uu": ("sbuf", [128, 5 * TK * R], BF),
+    "pq": ("sbuf", [128, 4, 2, 512], BF), "pin": ("sbuf", [128, 2 * TK, 2, 512], BF), "dW": ("sbuf", [128, 2 * R], BF),
+    "n0i": ("sbuf", [128, 64], I32), "spi": ("sbuf", [128, TK * 64], I32), "sP": ("sbuf", [128, TK * 64], F16),
     "nl": ("sbuf", [128, (TK + 1) * 64], U16), "nin": ("sbuf", [128, TK * 64], U16), "hl": ("sbuf", [128, 128], U16),
-    "of1": ("sbuf", [128, 64], U16), "of2": ("sbuf", [128, 64], U16),
-    "Z1": ("sbuf", [128, TK * 128], BF), "Zin": ("sbuf", [128, TK * 128], BF),
-    "HL": ("sbuf", [128, 320], F16), "HF": ("sbuf", [128, 256], F16), "I16": ("sbuf", [128, 128], F16),
-    "In16": ("sbuf", [128, 128], F16), "I32": ("sbuf", [128, 128], F32), "gg": ("sbuf", [128, 192], F32),
-    "nF": ("sbuf", [128, TK * 64], F32), "eT": ("sbuf", [128, 64], BF),
+    "of1": ("sbuf", [128, 64], U16), "of2": ("sbuf", [128, 64], U16), "nF": ("sbuf", [128, TK * 64], F32),
+    "Z1": ("sbuf", [128, TK * 128], BF), "Zin": ("sbuf", [128, TK * 128], BF), "eT": ("sbuf", [128, 64], BF),
+    "HL": ("sbuf", [128, 256], F16), "HF": ("sbuf", [128, 256], F16), "I16": ("sbuf", [128, 128], F16),
+    "TH": ("sbuf", [128, R], F16), "sel": ("sbuf", [128, R], F16), "WAe": ("sbuf", [128, 144], F16),
     "ci": ("sbuf", [128, 8], I32), "cf": ("sbuf", [128, 32], F32), "cj": ("sbuf", [128, 8], F32),
-    "Ls32": ("sbuf", [128, 128], F32), "B32": ("sbuf", [128, 8], F32), "B8": ("sbuf", [128, 8], BF),
+    "Ls32": ("sbuf", [128, 128], F32), "B32": ("sbuf", [128, 8], F32),
+    "p32": ("sbuf", [128, R], F32),
     "ps": ("psum", [128, 4096], F32),
 }
-for _n in ("q2", "m1", "m2", "cm", "cn", "cnt", "Eg", "sel", "Vg", "KB"):
+for _n in ("Q0", "Pt", "Et", "Vt"):
+    SCRATCH[_n] = ("sbuf", [128, W], BF)
+for _n in ("q2", "rr", "m1", "m2", "cm", "cn", "cnt", "Eg", "Vg", "KB"):
     SCRATCH[_n] = ("sbuf", [128, R], BF)
 for _n in ("pr", "mn", "hA", "hs"):
     SCRATCH[_n] = ("sbuf", [128, R], F32)
-for _n in ("BM", "Lc", "Dm", "t1", "t2", "t3", "t4", "t5", "I128", "Lsn", "I1", "MV", "In8", "Jh", "E64", "bw0", "bw1",
-           "Sh", "bk0", "bk1", "SA", "SC", "iG", "iD", "iX", "G8", "KA", "u2", "ub", "tb", "kk"):
+for _n in ("BM", "Ln", "Dm", "Dm2", "t1", "t2", "t3", "t4", "t5", "t6", "t7", "I128", "Lsn", "I1", "MU", "MZ", "Jh", "E64", "bf0", "bf1",
+           "Sh", "bk0", "bk1", "SA", "iG", "iD", "iX", "G8", "KA", "u2", "ub", "ab", "kk"):
     SCRATCH[_n] = ("sbuf", [128, 128], BF)
-for _n in ("WAz", "WAe", "WBc", "WBy", "iM", "iU"):
+for _n in ("WAz", "WBc", "WBy", "iM", "iU"):
     SCRATCH[_n] = ("sbuf", [128, 192], BF)
 
-SEMAPHORES = (["eV", "eS", "eP", "eG"] + ["d%d" % i for i in range(30)] + ["l%d" % i for i in range(40)]
+SEMAPHORES = (["eV", "eS", "eP", "eG"] + ["d%d" % i for i in range(36)] + ["l%d" % i for i in range(36)]
               + ["a%d" % i for i in range(58)])
 
-ORDER = {
-    "V": "hv0- hv1- hv2- hv3- d0 d1 pr0 d2 cm0 d3 pr1 o10 cm1 x10 x11 o11 x12 x13 g1 g3 y0 mn0 y1 mn1 gA0 gB0 gC0 pq0 cn0 gA1 gB1 gC1 pq1 o20 cn1 x20 x21 o21 x22 x23 nn0 nn1 nf",
-    "S": "ht0- ht1- ht2- ht3- q0 q1 q2 q3 m0 m1 Vg0- Vg1- Z0 Vg2- Vg3- Z1 eC Eg0 Eg1 Eg2 Eg3 g0 g1 g2 g3 n0 n1 hF0 th0- u0 ct0 hF1 ub0 u1 tb0 ct1 kk0 ub1 se0 tb1 kk1 se1 th1-",
-    "P": "a0 c0 a1 c1 L0 e0 D0 L1 uo0 e1 D1 fz0 b0 uo1 fz1 eT b1 J0 R0 J1 R1 M0 M1 T0 E0 fw0 N0 C0 T1 E1 fw1 tr0 C1 fy0 Th0 up0 N1 C2 tr1 C3 fc0 fy1 Th1 s0 up1 I0 k0 I1 fc1 K0 s1 v0 k1 W0 K1 v1 W1",
-    "G": "sr0 sr1 sz ha- sn",
-}
-ORDER = {'V': 'hv0- hv1- hv2- hv3- d1 pr0 d2 cm0 d3 pr1 o10 cm1 x10 o11 x12 g1 g3 y0 mn0 y1 mn1 gA0 gB0 pq0 gC0 cn0 gA1 gB1 pq1 gC1 cn1 o20 x20 o21 x22 nn0 nn1 d0+ nf', 'S': 'ht0- ht1- ht2- ht3- q0 q1 q2 m0 q3 m1 Vg3- Vg1- Z0 Vg0- Eg2 Z1 Eg0 Vg2- Eg3 Eg1 eC g0 g2 n0 n1 hF0 u0 th0- hF1 ct0 ct1 ub0 u1 tb0 ub1 kk0 tb1 kk1 se0 se1 th1-', 'P': 'L0 eT e0 D0 c1 L1 uo0 e1 D1 fz0 b1 fz1 uo1 J0 R1 b0 J1 M0 M1 R0 N0 E0 fw0 N1 C0 fw1 E1 tr0 C1 fy0 C2 up0 tr1 Th0 C3 Th1 fy1 fc0 s0 fc1 I1 up1 k0 s1 I0 K0 k1 v0 a1+ K1 a0+ v1 W0 W1 c0+', 'G': 'sn- sr0 sr1 ha- sz'}
-ORDER = {'V': 'hv0- hv1- hv2- hv3- q1 q3 pr0 p3 pr1 cm0 cm1 o10 x10 o11 x12 g1 g3 y0 mn0 y1 mn1 gA0 gB0 pq0 gC0 gA1 gB1 cn0 gC1 pq1 cn1 o20 x20 o21 x22 nn0 x23 nn1 nf', 'S': 'ht0- ht1- ht2- ht3- m0 p2 m1 Vg3- Vg2- Vg1- Z1 Vg0- r0 Eg2 Eg0 r1 eC Z0 g0 g2 n0 Eg1 n1 Eg3 hF0 th0- u0 hF1 ct0 ct1 ub0 u1 tb0 ub1 kk0 tb1 kk1 se0 se1 th1- p0+ p1+ q0+ q2+', 'P': 'W1- a0 c0 L0 e0 a1 L1 D0 e1 b0 D1 uo0 uo1 fz1 U0 eT fz0 U1 J0 b1 R0 R1 M0 M1 J1 N0 E0 fw0 C0 N1 fw1 C2 tr0 C1 E1 fy0 tr1 Th0 up0 C3 Th1 fy1 fc0 I0 s0 fc1 k0 s1 k1 up1 K0 I1 K1 v0 v1 W0 c1+', 'G': 'sn- sr0 sr1 ha- sz lv'}
-OPT = dict(on_v=("g1", "g3", "q1", "q3", "p3"), direct=(0, 1), full=False, lo="V", x1=((0, 2), (2, 4)), x2=((0, 2), (2, 3), (3, 4)))
+ORDER = {'V': 'hv0- hv1- hv2- hv3- hvn- q2 pr0 pr1 cm0 cm1 o10 x10 o11 x12 nF- g0 g2 y0 mn0 pq0 cn0 y1 mn1 o20 gA0 gB0 pq1 gC0 gA1 gB1 gC1 cn1 ct0 u1 ct1 o21 x22 se0 se1 nn0 p1+ nn1 q1+ q3+', 'S': 'ht0- ht1- ht2- ht3- m1 Qc3 Qc2 Qc0 Vg0- Vg2- Vg3- Vg1- eC Z1 Eg2 r0 r1 Z0 Eg1 Eg0 g1 g3 n0 n1 Eg3 th1- u0 th0- x20 hF0 hF1 x21 ub0 kk0 ub1 ab0 kk1 ab1 x23 p0+ q0+ p2+ Qc1+ p3+ m0+', 'P': 'L0 c1 L1 e0 D0 e1 D1 uo0 b0 fz1 uo1 N0 fz0 J0 b1 J1 N1 M0 M1 R0 E0 fw0 R1 C0 fy0 E1 up0 C1 fw1 C2 tr0 C3 tr1 Th0 fy1 Th1 fc0 up1 I0 s0 fc1 K0 s1 I1 K1 v0 W0 v1 W1 c0+ a1+ eT+ a0+', 'G': 'lv- sn- sr0 sp sr1 ha- sz pc'}
+ORDER = {'V': 'x12 g0 hvn- g2 y0 mn0 pq0 cn0 hv2- y1 mn1 Qc0+ gA0 gB0 o20 gC0 pq1 gA1 hF0 gB1 gC1 cn1 ct0 u1 ub0 o21 x22 se0 se1 nn0 hv0 hv3- p0+ q1+ nn1 q2+ q3+ pr0+ kaV+ pr1+ cm0+ kbV+ nF cm1+ o10+ x10+ hv1 o11+', 'S': 'r0 kfS Vg3- Eg0 Qc3+ kiS r1 hty- g1 g3 kcS+ ht1- n0 ht2- Qc1+ n1 eC keS Eg3 u0 kgS khS x20 hF1 x21 ct1 kk0 ab0 ub1 kk1 ab1 x23 q0+ p1+ ht3- p2+ m0+ p3+ m1+ Qc2+ th0- th1- kdS+ Vg0 Eg1+ Z1+ Vg2 Eg2+ Z0+ ht0 Vg1', 'P': 'a1 c1 L0 e0 L1 D0 e1 D1 uo0 fz1 uo1 fz0 b1 b0 N1 J0 kgP+ J1 M0 eT N0 M1 R0 E0 C0 fw0 fy0 C1 up0 R1 E1 fw1 tr0 C2 Th0 tr1 C3 fy1 Th1 fc0 up1 c0+ I0 s0 fc1 K0 s1 v0 I1 K1 W0 v1 a0+ W1', 'G': 'sr0 sp sr1 sz pc ha- lv sn'}
+ORDER = {'V': 'g0 g2 y0 pq0 mn0 cn0 y1 mn1 gA0 gB0 o20 gC0 pq1 gA1 hF0 gB1 Qc0+ gC1 cn1 ct0 u1 ub0 kbV+ o21 x22 se0 se1 nn0 p0+ hv0 nn1 q1+ q2+ hvn hv1 pr0+ hv3- p2+ pr1+ cm0+ kaV+ nF hv2 cm1+ o10+ x10+ o11+ x12+', 'S': 'g3 n0 Qc1+ n1 kfS Qc2+ Eg0 u0 Eg2 x20 hF1 x21 ct1 kk0 ub1 ab0 kk1 ab1 x23 q0+ p1+ q3+ p3+ m0+ m1+ keS+ hty- Qc3+ ht1- th0- khS+ ht2- Vg2 Z0+ Z1+ kcS+ th1- kdS+ eC+ r0+ ht3- ht0 kiS+ kgS+ Vg0 r1+ g1+', 'P': 'uo0 fz1 fz0 uo1 eT b1 J0 b0 N1 M0 N0 M1 J1 R0 E0 R1 E1 fw0 kgP+ fy0 C0 up0 C1 fw1 tr0 C2 Th0 tr1 C3 Th1 fy1 fc0 up1 a1+ I0 s0 fc1 K0 s1 I1 K1 v0 W0 v1 W1 a0+ c0+ L0+ c1+ L1+ e0+ D0+ e1+ D1+', 'G': 'sn- sr0 sr1 sz pc0 pc1 ha- lv'}
+ORDER = {'V': 'P2 Z1 hv2- P3 nF- kbV+ o11 Qc1+ x12 x13 g1 r1 y0 mn0 y1 pq0 Qc0+ hv3- gA0 cn0 mn1 gB0 u0 gC0 pq1 o20 gA1 gB1 gC1 hF0 cn1 hF1 ct0 u1 ct1 o21 x22 se0 se1 nn0 hv0 q1+ p1+ hv1 nn1 q2+ kaV+ pr0+ hvn cm0+ p2+ o10+ pr1+ P1+ cm1+', 'S': 'n1 Eg2 Eg0 kfS x20 x21 ub0 Qc2+ ht1- kk0 ab0 ub1 kk1 ab1 x23 th0- kcS+ Qc3+ ht2- q0+ khS+ p0+ m0+ q3+ p3+ P0+ m1+ x10+ x11+ th1- Z0+ keS+ r0+ Vg2 kiS+ Vg0 kdS+ ht0 ht3- g0+ g2+ g3+ eC+ hty kgS+ n0+', 'P': 'c1 e0 D0 a1 L1 uo0 e1 fz0 D1 eT fz1 kgP+ b0 uo1 J0 b1 N1 N0 M0 J1 M1 fw0 R0 E0 C0 R1 fy0 E1 fw1 up0 C1 tr0 C2 tr1 Th0 C3 fy1 Th1 fc0 up1 I0 s0 fc1 K0 s1 v0 I1 K1 W0 v1 a0+ W1 L0+ c0+', 'G': 'sz sp lv ha- sr0+ sn sr1+'}
+ORDER = {'V': 'u0 pq1 gA1 gB1 gC1 o20 cn1 ct0 u1 ct1 kbV+ nF- o21 x22 se0 se1 nn0 hv0 q1+ nn1 Qc0+ hvn pr0+ m0+ hv1 kaV+ p2+ pr1+ cm0+ hv2 cm1+ o10+ x10+ o11+ x12+ g0+ hv3 y0+ r1+ mn0+ pq0+ y1+ cn0+ mn1+', 'S': 'kjS+ r0 g1 g2 n0 kdS+ n1 kiS kfS kgS+ Eg2 Eg0 hF1 x20 ub0 kk0 ub1 ab0 kk1 ab1 x23 hty- ht1- q0+ p0+ q2+ Qc2+ m1+ th0- Vg0 Qc1+ Qc3+ keS+ kcS+ ht2- Z1+ ht0 Vg2 Z0+ ht3- khS+ eC+', 'P': 'a1 c1 L1 D0 e1 D1 uo0 fz1 b0 fz0 uo1 eT J0 M0 N0 b1 N1 M1 J1 R0 fw0 E0 R1 C0 fy0 C1 fw1 up0 C2 E1 tr1 C3 Th0 fy1 Th1 I0 fc0 up1 I1 s0 fc1 K0 kgP+ s1 c0+ v0 K1 v1 W0 W1 a0+ L0+ e0+', 'G': 'sr1 sz pc0 pc1 lv ha- sn sr0+'}
+ORDER = {'V': 'cn0 y1 mn1 pq1 Qc0+ gA1 gB1 gC1 o20 hF1 cn1 nF- ct0 u1 ct1 o21 x22 se0 se1 nn0 hv0 q0+ kbV+ hv1 nn1 q1+ p2+ hvn pr0+ kaV+ pr1+ cm0+ cm1+ o10+ hv2 x10+ o11+ x12+ eC+ g0+ y0+ r1+ hv3 mn0+ pq0+', 'S': 'Qc3+ Qc1+ g1 g2 n0 n1 Eg2 kfS u0x u0 Eg0 hF1x kcS+ khS x20 ct0x ct1x ub0 u1x kk0 ab0 ub1 kk1 th0x- ab1 ht0 x23 p0+ q2+ ht1 m0+ kgS+ hty ht3- m1+ Qc2+ kiS+ kdS+ ht2 th0- Z0+ Z1+ kjS+ Vg2 Vg0 r0+ keS+', 'P': 'D1 uo0 b0 fz0 fz1 uo1 eT N0 J0 b1 M0 N1 M1 J1 R0 E0 C0 fw0 fy0 C1 R1 up0 fw1 E1 C2 tr1 C3 Th0 Th1 kgP+ fy1 I0 fc0 up1 s0 fc1 K0 s1 I1 v0 K1 W0 v1 W1 c0+ a0+ L0+ c1+ a1+ L1+ e0+ D0+ e1+', 'G': 'pc1 ha- lv sn sr0+ sr1+ sz+ pc0+'}
+HALVES, QUARTERS = ((0, 2), (2, 4)), ((0, 1), (1, 2), (2, 3), (3, 4))
+OPT = dict(direct=(0,), full=False, split=False, p32=(), x1=HALVES, q=((0, 1), (1, 2), (2, 4)), p=HALVES, g=((0, 1), (1, 2), (2, 4)), th=((0, 4),), gfull=True, last=("ct0", "ct1", "hF1", "u0", "u1"), x2=((0, 2), (2, 3), (3, 4)), eg=HALVES, vg=HALVES)
 COST = dict(cy=0.0009, pcy=0.00045, ga=1.56, sc=3.8, fix=0.06, lat=0.10, same=0.06, rlat=2.0, riss=0.5, giss=1.0, dlat=1.6, bw=400e3)
 
 
@@ -51,8 +50,8 @@ def build(g, core, T, topo, rank, opt=OPT):
     ops = []
     lastw, readers = {}, {}
     nsem = {"d": 0, "l": 0, "a": 0}
-    tok = [0]
-    on_v = opt["on_v"]
+    tok, grp = [0], ["ld"]
+    on_v = opt.get("on_v") or [w.rstrip("+-") for w in ORDER["V"].split()]
 
     def newsem(k):
         nsem[k] += 1
@@ -60,6 +59,8 @@ def build(g, core, T, topo, rank, opt=OPT):
 
     def add(name, eng, fn, rd, wr, cost, kind="c", sem=None, inc=0, after=(), hold=0, start=False):
         i = len(ops)
+        if name is None and eng and eng != "Y":
+            name = grp[0] + (eng if grp[0] != "ld" else "")
         deps = {}
         psum = lambda k: k[0] == "b" and k != str(k)
         for k in rd:
@@ -80,6 +81,7 @@ def build(g, core, T, topo, rank, opt=OPT):
         return i
 
     V, S, P = g.vector, g.scalar, g.tensor
+    EQ, MUL, ADD, SUB, MAX, MIN = OP.is_equal, OP.mult, OP.add, OP.subtract, OP.max, OP.min
     vc = lambda n, f: (f, n) if f == str(f) else ("cy", max(64, n * f))
 
     def ts(name, out, in0, s1, s2, o0, o1, rd, wr, n, f=1.0):
@@ -96,8 +98,26 @@ def build(g, core, T, topo, rank, opt=OPT):
     def act(name, out, a, fn, rd, wr, n, f=1.0, bias=0.0, scale=1.0):
         return add(name, "S", lambda: S.activation(out, a, fn, bias=bias, scale=scale), rd, wr, vc(n, f))
 
-    def copy(name, out, a, rd, wr, n, f=1.0):
-        return cp(name, out, a, rd, wr, n, f) if name in on_v else act(name, out, a, AF.Copy, rd, wr, n, f)
+    def copy(name, out, a, rd, wr, n, f=1.0, scale=1.0):
+        name = last(name)
+        if name not in on_v:
+            return act(name, out, a, AF.Copy, rd, wr, n, f, scale=scale)
+        return cp(name, out, a, rd, wr, n, f) if scale == 1.0 else ts(name, out, a, scale, None, MUL, None, rd, wr, n, f)
+
+    def last(name):
+        return name + "x" if tok[0] == TK - 1 and name in opt["last"] else name
+
+    def relu(name, out, a, rd, wr, n, bias=0.0, f=1.0):
+        name = last(name)
+        if name in on_v:
+            return ts(name, out, a, bias, 0.0, ADD, MAX, rd, wr, n, f)
+        return act(name, out, a, AF.Relu, rd, wr, n, bias=bias)
+
+    def sign(name, out, a, over, rd, wr, n, half=False):
+        name = last(name)
+        if name in on_v:
+            return ts(name, out, a, over, 0.5 if half else 2.0, OP.is_gt, SUB if half else MUL, rd, wr, n)
+        return act(name, out, a, AF.Sign, rd, wr, n, bias=-over)
 
     def mm(name, items, rd, wr, hold=0):
         def run():
@@ -105,7 +125,8 @@ def build(g, core, T, topo, rank, opt=OPT):
             for (o, l, x, st, sp, c) in items:
                 r = P.matmul(o, l, x, st, sp)
             return r
-        return add(name, "P", run, rd, wr, ("pcy", sum(it[5] for it in items)), hold=hold, start=items[0][3])
+        i = add(name, "P", run, rd, wr, ("pcy", sum(it[5] for it in items)), hold=hold, start=items[0][3])
+        ops[i]["nmm"] = len(items)
 
     def dma(q, out, a, rd, wr, nbytes, sem=None, accum=False, name=None):
         e = {"Y": g.sync, "S": g.scalar, "G": g}[q]
@@ -138,14 +159,14 @@ def build(g, core, T, topo, rank, opt=OPT):
         return add(None, "G", fn, rd + ["pool"], wr + ["pool"], ("gp", n))
 
     tok[0] = -1
+    UA = 2 * TK * R
     dma("Y", T.n0i[:], T.n0[:], [], ["n0i"], 32e3)
-    dma("Y", T.Qw[:, 0:W], T.qd[:], [], ["Q", "k1"], 1300e3)
-    dma("S", T.Pt[:], T.pt[:], [], ["P", "k2"], 1300e3, name="ld")
+    dma("S", T.Q0[:], T.qd[:], [], ["Q0"], 660e3, name="ld")
+    dma("Y", T.Pt[:], T.pt[:], [], ["P"], 660e3)
     su = newsem("d")
-    dma("S", T.uu[0:8, 0:2 * R], T.ud[:, 0:2 * R], [], ["u0a"], 1300e3, su, name="ld")
-    dma("S", T.uu[32:40, 0:3 * R], T.ua[:, 0:3 * R], [], ["u0b"], 1300e3, su, name="ld")
-    dma("Y", T.spi[:], T.spot[:], [], ["spi"], 1300e3)
-    dma("Y", T.Et[:], T.nx[:], ["k1", "k2"], ["E"], 700e3)
+    dma("S", T.uu[0:8, 0:2 * R], T.ud[:, 0:2 * R], [], ["u0a"], 40e3, su, name="ld")
+    dma("S", T.uu[0:8, UA:UA + 3 * R], T.ua[:, 0:3 * R], [], ["u0b"], 60e3, su, name="ld")
+    dma("Y", T.spi[:], T.spot[:], [], ["spi"], 200e3)
 
     gp(lambda: g.iota(T.ci[:, 0:1], [[0, 1]], 0, 1), [], ["ci0"], 1)
     io = lambda out, pat, base, cm: (lambda: g.iota(out, pat, base, cm, allow_small_or_imprecise_dtypes=True))
@@ -173,94 +194,105 @@ def build(g, core, T, topo, rank, opt=OPT):
         ts(None, C(k), a, s1, s2, o0, o1, rd, [("c", k)], 1)
         return C(k), ("c", k)
 
-    EQ, MUL, ADD, SUB, MAX = OP.is_equal, OP.mult, OP.add, OP.subtract, OP.max
+    def mat(name, idx, c, w, rd, a=0, b=128):
+        ts(None, T[name][:, a:b], T[idx][:, a:b], c, w, EQ, MUL, [idx] + rd, [name if a == 0 else name + "b"], b - a, 0.5)
 
-    def mat(name, idx, c, w, rd, o1=MUL, n=128):
-        ts(None, T[name][:, 0:n], T[idx][:, 0:n], c, w, EQ, o1, [idx] + rd, [name], n, 0.5)
+    def scaled(name, src, w, rd=(), a=0, b=128):
+        act(None, T[name][:, a:b], T[src][:, a:b], AF.Identity, [src] + list(rd), [name if a == 0 else name + "b"], b - a, scale=w)
 
-    def scaled(name, src, w, rd=(), n=128):
-        act(None, T[name][:], T[src][:], AF.Identity, [src] + list(rd), [name], n, scale=w)
+    def summed(name, parts, also=()):
+        out, key = T.ps[:, 3712:3840], ("b", 7, 128)
+        mm(None, [(out, T.I1[:], T[a][:], a == parts[0], a == parts[-1], 128) for a in parts], ["I1"] + parts, [key])
+        for nm, w in ((name, 1.0),) + also:
+            act(None, T[nm][:], out, AF.Copy, [], [key, nm], 128, scale=w)
 
-    mat("BM", "iG", cG, 1.0, ["cfa"])
-    mat("SA", "iG", cP, -1.0, ["cfa"])
-    c32, k32 = col(cP, 1.0, -32.0, ["cfa"])
-    mat("SC", "iG", c32, 1.0, [k32])
-    gp(lambda: g.affine_select(T.Lc[:], T.BM[:], [[1, 128]], OP.is_ge, 0.0, 0, -1), ["BM"], ["Lc"], 128)
-    gp(io(T.iU[:], [[0, 3], [1, 64]], 0, 0), [], ["iU"], 192)
-    cp(None, T.nl[:, 0:64], T.n0i[:], ["n0i"], [("nl", 0, 0), ("nl", 0, 1)], 64)
-    mat("I128", "iD", 0.0, 128.0, [])
-    cA, kA = vcol(cX, 15.0, -H, OP.not_equal, MUL, ["cfa"])
-    cB, kB = vcol(cX, 15.0, -2 * H, EQ, MUL, ["cfa"])
-    cC, kC = col(cB, -0.5, 0.0, [kB])
-    mat("t1", "iD", 0.0, H, [])
-    mat("t2", "iD", 1.0, cA, [kA])
-    scaled("t3", "BM", cB, [kB])
-    mat("t4", "iD", -15.0, cC, [kC])
-    tt(None, T.t1[:], T.t1[:], T.t2[:], ADD, ["t1", "t2"], ["t1"], 128, 2)
-    tt(None, T.t3[:], T.t3[:], T.t4[:], ADD, ["t3", "t4"], ["t3"], 128, 2)
-    tt(None, T.Dm[:], T.t1[:], T.t3[:], ADD, ["t1", "t3"], ["Dm"], 128, 2)
-    cWa, kWa = col(cG, 16.0, 15.0, ["cfa"])
-    if opt["direct"]:
-        cWz, kWz = col(cX, float(W), float(W), ["cfa"])
-        mat("WAz", "iM", cWa, cWz, [kWa, kWz], n=144)
-    mat("I16", "iD", 0.0, 1.0, [])
-    ts(None, T.sP[:], T.spi[:], -1024.0, None, ADD, None, ["spi"], ["sP"], TK * 64)
+    if not opt["gfull"]:
+        add(None, "V", lambda: V.memset(T.HL[:], 0.0), [], [("HL", 0), ("HL", 1)], vc(256, 0.5))
     ts(None, T.ci[:, 3:4], p0, 7, None, AND, None, ["ci0"], ["ci3"], 1)
     ts(None, T.ci[:, 4:5], p0, 3, 7, SHR, AND, ["ci0"], ["ci4"], 1)
     ts(None, T.ci[:, 5:6], p0, 6, None, SHR, None, ["ci0"], ["ci5"], 1)
     ts(None, T.ci[:, 6:7], p0, 63, None, AND, None, ["ci0"], ["ci6"], 1)
+    mat("BM", "iG", cG, -1.0 / SG, ["cfa"])
     cp(None, T.cf[:, 3:7], T.ci[:, 3:7], ["ci3", "ci4", "ci5", "ci6"], ["cfb"], 4)
+    gp(lambda: g.affine_select(T.Ln[:], T.BM[:], [[1, 128]], OP.is_ge, 0.0, 0, -1), ["BM"], ["Ln"], 128)
+    gp(io(T.iU[:], [[0, 3], [1, 64]], 0, 0), [], ["iU"], 192)
+    gp(io(T.iX[:], [[0, 8], [256, 16]], 0, 0), [], ["iX"], 128)
+    gp(lambda: g.affine_select(T.t5[:], T.BM[:], [[1, 128]], OP.is_gt, 0.0, 0, -1), ["BM"], ["t5"], 128)
+    cWa, kWa = col(cG, 16.0, 15.0, ["cfa"])
     cWb, kWb = col(cG, 1.0, 56.0, ["cfa"])
     cWy, kWy = col(cX, 1.0, 1.0, ["cfa"])
-    mat("WBy", "iM", cWb, cWy, [kWb, kWy], n=192)
+    cA, kA = vcol(cX, 15.0, -H, OP.not_equal, MUL, ["cfa"])
+    cB, kB = vcol(cX, 15.0, 2 * H * SG, EQ, MUL, ["cfa"])
+    cC, kC = vcol(cX, 15.0, H, EQ, MUL, ["cfa"])
+    cWc, kWc = vcol(cX, 0.0, 0.0625, EQ, ADD, ["cfa"])
+    mat("I128", "iD", 0.0, 128.0, [])
+    mat("SA", "iG", cP, -1.0, ["cfa"])
     cb, kb = col(cG8, 16.0, cJ, ["cfb"])
+    c64, k64 = col(c63, 1.0, 1.0, ["cfb"])
     cc, kc = col(cb, 1.0, 8.0, [kb])
-    mat("bw0", "iM", cb, float(W), [kb])
-    mat("bw1", "iM", cc, float(W), [kc])
-    scaled("Jh", "BM", 1.0 / 256)
+    scaled("t3", "BM", cB, [kB])
     scaled("I1", "I128", 1.0 / 128)
-    scaled("In1", "I128", -1.0 / 128)
-    mat("B8", "iM", cG, 1.0, ["cfa"], n=8)
-    scaled("B32", "B8", -1.0, n=8)
-    gp(lambda: g.affine_select(T.t5[:], T.BM[:], [[1, 128]], OP.is_gt, 0.0, 0, -1), ["BM"], ["t5"], 128)
-    gp(io(T.iX[:], [[0, 8], [256, 16]], 0, 0), [], ["iX"], 128)
-    scaled("Ls32", "t5", 128.0)
-    scaled("Lsn", "t5", -128.0)
-    mat("E64", "iU", c63, 1.0, ["cfb"])
-    act(None, T.MV[:, 0:64], T.E64[:, 0:64], AF.Identity, ["E64"], ["MV0"], 64, scale=-33.0)
-    act(None, T.MV[:, 64:128], T.E64[:, 64:128], AF.Identity, ["E64"], ["MV1"], 64)
-    add(None, "V", lambda: V.memset(T.HL[:], 0.0), [], [("HL", 0), ("HL", 1)], vc(320, 0.5))
-    if opt["lo"] != "V":
-        add(None, "V", lambda: V.memset(T.gg[:], 0.0), [], [("gg", 0), ("gg", 1)], vc(192, 1))
-        scaled("I32", "I128", 1.0 / 128)
-        scaled("In16", "I128", -1.0 / 128)
+    scaled("t1", "I128", H / 128)
+    mat("t2", "iD", 1.0, cA, [kA])
+    mat("t4", "iD", -15.0, cC, [kC])
+    mat("I16", "iD", 0.0, 1.0, [])
     mat("G8", "iG", cG8, 1.0, ["cfb"])
-    ts(None, T.cj[:], T.iM[:, 0:8], cJ, None, EQ, None, ["iM", "cfb"], ["cj"], 8)
-    for i in range(4):
-        act(None, T.TH[:, 128 * i:128 * i + 128], T.G8[:], AF.Identity, ["G8", "cj"], [("TH", i)], 128, scale=T.cj[:, i:i + 1])
-    THK = [("TH", i) for i in range(4)]
-    scaled("In8", "I128", -8.0 / 128)
-    c0, k0 = vcol(cX, 0.0, 8.0, EQ, MUL, ["cfa"])
-    cWc, kWc = col(c0, 1.0, 0.5, [k0])
-    mat("WBc", "iM", cWb, cWc, [kWb, kWc], n=192)
     c78, k78 = vcol(cG8, 7.0, None, OP.not_equal, None, ["cfb"])
-    ca, ka = col(c63, 1.0, 1.0, ["cfb"])
-    mat("t2", "iU", ca, c78, [ka, k78])
-    tt(None, T.Sh[:], T.t2[:], T.E64[:], ADD, ["t2", "E64"], ["Sh"], 128, 2)
-    ca, ka = vcol(cG8, 0.0, cU, EQ, ADD, ["cfb"])
-    cSq, kSq = col(ca, 1.0, -10.0, [ka])
-    ca, ka = col(cU, 2.0, -1.0, ["cfb"])
-    cb2, kb2 = col(cU, 256.0, -256.0, ["cfb"])
-    act(None, T.t4[:], T.iX[:], AF.Identity, ["iX", ka, kb2], ["t4"], 128, bias=cb2, scale=ca)
-    tt(None, T.KA[:], T.t4[:], T.G8[:], MUL, ["t4", "G8"], ["KA"], 128, 2)
+    cAb, kAb = vcol(cG8, 0.0, -17.5, EQ, ADD, ["cfb"])
+    cxx, kxx = vcol(cX, -13.0, cX, ADD, MUL, ["cfa"])
+    cp(None, T.nl[:, 0:64], T.n0i[:], ["n0i"], [("nl", 0, 0), ("nl", 0, 1)], 64)
+    cs, ks = col(cU, -0.125, 0.0625, ["cfb"])
+    ct, kt = col(cU, 208.0, -96.0, ["cfb"])
+    cw, kw = col(cU, -float(W), 0.0, ["cfb"])
+    cWc, kWc = col(cWc, 8.0, 0.0, [kWc])
+    halves = any(w in on_v for w in ("m0", "m1", "n0", "n1"))
+    summed("Dm", ["t1", "t2", "t3", "t4"], (("Dm2", 2.0),) * halves)
+    mat("WAz", "iM", cWa, float(W), [kWa], 0, 144)
+    mat("WBy", "iM", cWb, cWy, [kWb, kWy], 0, 96)
+    mat("bk0", "iM", cb, -1.0, [kb])
+    mat("bk1", "iM", cc, -1.0, [kc])
+    ts(None, T.cj[:], T.iM[:, 0:8], cJ, None, EQ, None, ["iM", "cfb"], ["cj"], 8)
+    ts(None, T.B32[:], T.iM[:, 0:8], cG, -1.0 / SG, EQ, MUL, ["iM", "cfa"], ["B32"], 8)
+    mat("WAe", "iM", cWa, -16.0, [kWa], 0, 144)
+    mat("WBc", "iM", cWb, cWc, [kWb, kWc], 0, 192)
+    mat("WBy", "iU", cWb, 1.0, [kWb], 96, 192)
+    mat("E64", "iU", c63, 1.0, ["cfb"])
+    mat("t6", "iU", c64, c78, [k64, k78])
+    scaled("bf0", "bk0", cw, [kw])
+    scaled("bf1", "bk1", cw, [kw])
+    act(None, T.t7[:], T.iX[:], AF.Identity, ["iX", ks, kt], ["t7"], 128, bias=ct, scale=cs)
+    tok[0], grp[0] = 0, "ka"
+    ts(None, T.sP[:], T.spi[:], -1024.0, None, ADD, None, ["spi"], ["sP"], TK * 64)
+    grp[0] = "kb"
+    tt(None, T.KA[:], T.t7[:], T.G8[:], MUL, ["t7", "G8"], ["KA"], 128, 2)
+    grp[0] = "kc"
+    scaled("Jh", "BM", 1.0 / 256)
+    scaled("Lsn", "t5", 128.0)
+    scaled("Ls32", "t5", -128.0)
+    grp[0] = "kd"
+    ca, ka = col(cU, 33.0, -33.0, ["cfb"])
+    c1u, k1u = col(cU, -1.0, 1.0, ["cfb"])
+    scaled("MZ", "I1", ca, [ka])
+    scaled("MU", "E64", ca, [ka], 0, 64)
+    scaled("MU", "E64", c1u, [k1u], 64, 128)
+    grp[0] = "ke"
+    for i in range(8 if opt["gfull"] else 4):
+        grp[0] = "ke" if i < 4 else "kj"
+        act(None, T.TH[:, 128 * i:128 * i + 128], T.G8[:], AF.Identity, ["G8", "cj"], [("TH", i)], 128, scale=T.cj[:, i:i + 1])
+    THK = [("TH", i) for i in range(8 if opt["gfull"] else 4)]
+    grp[0] = "kf"
+    ca, ka = col(cU, 1.0, 0.5, ["cfb"])
+    c16, k16 = col(c1u, -16.0, 0.0, [k1u])
+    cLo, kLo = col(cxx, -16.0, 352.0, [kxx])
+    cHi, kHi = col(cxx, -16.0, 512.0, [kxx])
+    cSq, kSq = col(cAb, 1.0, ca, [kAb, ka])
+    grp[0] = "kg"
+    summed("Sh", ["t6", "E64"])
     for i in range(8):
-        ts(None, T.KB[:, 128 * i:128 * i + 128], T.KA[:], T.cj[:, i:i + 1], None, MUL, None, ["KA", "cj"], [("KB", i)], 128, 0.5)
+        grp[0] = "kh" if i < 4 else "ki"
+        act(None, T.KB[:, 128 * i:128 * i + 128], T.KA[:], AF.Identity, ["KA", "cj"], [("KB", i)], 128, scale=T.cj[:, i:i + 1])
     KBK = [("KB", i) for i in range(8)]
-    ca, ka = vcol(cX, 1.0, cX, ADD, MUL, ["cfa"])
-    cSe, kSe = col(ca, -256.0, 0.0, [ka])
-    scaled("bk0", "bw0", 1.0 / W)
-    scaled("bk1", "bw1", 1.0 / W)
-    mat("WAe", "iM", cWa, 16.0, [kWa], n=144)
+    tok[0] = -1
 
     send("sn", [(1, [T.nl[:, 0:64]], T.nin[:, 0:64], 0, [("nin", 0)])], [("nl", 0, 0), ("nl", 0, 1), "pool"], 16e3)
 
@@ -270,8 +302,7 @@ def build(g, core, T, topo, rank, opt=OPT):
     rot = [0, 1, 2]
 
     def pq_(b, slot, k, a, e):
-        o = 2 * slot * R + (a // 2) * R + 512 * k + 256 * (a % 2)
-        return b[:, o:o + 256 * (e - a)]
+        return b[:, 2 * slot + a // 2, k, 256 * (a % 2):256 * (a % 2 + e - a)]
 
     def h_step(t):
         off = (TK - 1 - t) % NR
@@ -281,22 +312,21 @@ def build(g, core, T, topo, rank, opt=OPT):
             lst, o, key = T.nin, (t + 1) * 64, lambda h: ("nin", t + 1)
         else:
             lst, o, key = T.hl, (off - 2) * 64, lambda h: ("hl", off)
-        for u in range(4):
-            vi, h = T.Vt[:, :].indirect(lst[:, o + 16 * u:o + 16 * u + 16]), u // 2
+        for (u, b) in opt["vg"] if t < TK - 1 else QUARTERS:
+            vi, h = T.Vt[:, :].indirect(lst[:, o + 16 * u:o + 16 * b]), u // 2
             if t == 0:
-                act("Vg%d" % u, qs_(T.hA, u), vi, AF.Tanh, ["Vt", key(h)], [("hA", u)], 256, "ga")
+                act("Vg%d" % u, T.hA[:, 256 * u:256 * b], vi, AF.Tanh, ["Vt", key(h)], [("hA", x) for x in range(u, b)], 256 * (b - u), "ga")
             elif t < TK - 1:
-                copy("Vg%d" % u, qs_(T.Vg, u), vi, ["Vt", key(h)], [("Vg", u)], 256, "ga")
+                act("Vg%d" % u, T.Vg[:, 256 * u:256 * b], vi, AF.Copy, ["Vt", key(h)], [("Vg", x) for x in range(u, b)], 256 * (b - u), "ga")
             else:
                 tt("hv%d" % u, qs_(T.hs, u), vi, qs_(T.hA, u), ADD, ["Vt", key(h), ("hA", u)], [("hs", u)], 256, "ga")
                 act("ht%d" % u, qs_(T.hs, u), qs_(T.hs, u), AF.Tanh, [("hs", u)], [("hs", u)], 256)
-                if u % 2:
-                    dma("Y", hs_(T.yh, h), hs_(T.hs, h), [("hs", u - 1), ("hs", u)], [("yh", h)], 256e3)
+                dma("Y", qs_(T.yh, u), qs_(T.hs, u), [("hs", u)], [("yh", u)], 128e3)
         if 0 < t < TK - 1:
             hk = [("hA", u) for u in range(4)]
             dma("G", T.hA[:], T.Vg[:], hk + [("Vg", u) for u in range(4)], hk, 1000e3, accum=True, name="ha")
-            for h in range(2):
-                act("th%d" % h, hs_(T.hA, h), hs_(T.hA, h), AF.Tanh, hk[2 * h:2 * h + 2], hk[2 * h:2 * h + 2], 512)
+            for (a, b) in opt["th"]:
+                act("th%d" % (a // 2) + "x" * (t == TK - 2), T.hA[:, 256 * a:256 * b], T.hA[:, 256 * a:256 * b], AF.Tanh, hk[a:b], hk[a:b], 256 * (b - a))
 
     for t in range(TK):
         tok[0] = t
@@ -306,13 +336,14 @@ def build(g, core, T, topo, rank, opt=OPT):
         bk = lambda k, h: ("b", 3 * h + rot[k])
         sm = lambda h, a, n: T.ps[:, 512 * (6 + h) + a:512 * (6 + h) + a + n]
         sk = lambda h, a: ("b", 6 + h, a)
-        ud = lambda k, h: T.uu[0:8, (2 * t + k) * R + 512 * h:(2 * t + k) * R + 512 * h + 512]
-        ua = lambda k, h, n: T.uu[32:32 + n, (3 * t + k) * R + 512 * h:(3 * t + k) * R + 512 * h + 512]
+        ud = lambda k, h: hs_(T.uu[0:8, :], h, (2 * t + k) * R)
+        ua = lambda k, h: hs_(T.uu[0:8, :], h, UA + (3 * t + k) * R)
         QK = lambda h: [("q", par, 2 * h), ("q", par, 2 * h + 1)]
-        DK = lambda h: [("d", par, 2 * h), ("d", par, 2 * h + 1)]
+        PK = lambda h: [("p", par, 2 * h), ("p", par, 2 * h + 1)]
         lh = lambda b, h: b[:, oc + 32 * h:oc + 32 * h + 32]
         fh = lambda b, h: b[:, 2 * oc + 64 * h:2 * oc + 64 * h + 64]
         c64 = lambda b, h: b[:, 64 * h:64 * h + 64]
+        dm = lambda nm: "Dm2" if nm in on_v else "Dm"
 
         def fold(wide, src, out, first):
             return [(out, wide[:, 56 - 8 * i:184 - 8 * i], src[:, i:512:8], first and i == 0, i == 7, 64) for i in range(8)]
@@ -320,8 +351,8 @@ def build(g, core, T, topo, rank, opt=OPT):
         def listed(wide, src, out, n):
             return [(out, wide[:, 15 - j:143 - j], src[:, j:n:16], False, j == 15, 64) for j in range(16)]
 
-        def unfold(w, src, out, first, last):
-            return [(out, T[w + str(b)][:], src[:, b:64:2], first and b == 0, last and b == 1, 64) for b in range(2)]
+        def unfold(w, src, out, first, last, n=64):
+            return [(out, T[w + str(b)][:], src[:, b:n:2], first and b == 0, last and b == 1, 64) for b in range(2)]
 
         def offsets(pn, vn, items, rd, dst, h):
             mm(pn, [(sm(h, 0, 32), T.I16[:], lh(T.sP, h), True, False, 64)] + items, ["I16", "sP"] + rd, [sk(h, 0)])
@@ -329,130 +360,164 @@ def build(g, core, T, topo, rank, opt=OPT):
 
         for h in range(2):
             mm("a%d" % h, [(bank(0, h), T.SA[0:8, :], ud(0, h), True, False, 512)], ["SA"] + UK, [bk(0, h)])
-            mm("c%d" % h, [(bank(1, h), T.SC[32:40, :], ua(0, h, 8), True, True, 512)], ["SC"] + UK, [bk(1, h)])
-        for u in range(4):
-            lst = T.nl[:, oc + 16 * u:oc + 16 * u + 16]
-            copy("q%d" % u, pq_(T.pq, par, 1, u, u + 1), Qr.indirect(lst), ["Q", ("nl", t, u // 2)], [("q", par, u)], 256, "ga")
-            copy("p%d" % u, pq_(T.pq, par, 0, u, u + 1), T.Pt[:, :].indirect(lst), ["P", ("nl", t, u // 2)], [("d", par, u)], 256, "ga")
+            mm("c%d" % h, [(bank(1, h), T.SA[0:8, :], ua(0, h), True, True, 512)], ["SA"] + UK, [bk(1, h)])
+        src, key, unit = (T.Q0[:, :], "Q0", SG) if t == 0 else (Qr, "Q", 1.0)
+        for (a, b) in opt["q"]:
+            copy("q%d" % a, pq_(T.pq, par, 1, a, b), src.indirect(T.nl[:, oc + 16 * a:oc + 16 * b]), [key, ("nl", t, a // 2)],
+                 [("q", par, u) for u in range(a, b)], 256 * (b - a), "ga", -unit)
+        for (a, b) in opt["p"]:
+            copy("p%d" % a, pq_(T.pq, par, 0, a, b), T.Pt[:, :].indirect(T.nl[:, oc + 16 * a:oc + 16 * b]), ["P", ("nl", t, a // 2)],
+                 [("p", par, u) for u in range(a, b)], 256 * (b - a), "ga", SG)
+        for (a, b) in opt["p32"]:
+            if t < TK - 1 or any("x1%d" % x not in on_v and x < b and a < y for x, y in opt["x1"]):
+                copy("P%d" % a, T.po[:, o2 + 256 * a:o2 + 256 * b], T.Pt[:, :].indirect(T.nl[:, oc + 16 * a:oc + 16 * b]), ["P", ("nl", t, a // 2)],
+                     [("P", par, u) for u in range(a, b)], 256 * (b - a), "ga", SG)
+        if t == 0:
+            for u in range(4):
+                copy("Qc%d" % u, T.Qw[:, 640 * u:640 * u + 640], T.Q0[:, 640 * u:640 * u + 640], ["Q0"], [("Qc", u)], 640, 1.0, SG)
         for h in range(2):
-            q, d = pq_(T.pq, par, 1, 2 * h, 2 * h + 2), pq_(T.pq, par, 0, 2 * h, 2 * h + 2)
-            send("sr%d" % h, [(1, [T.pq[:, (2 * par + h) * R:(2 * par + h + 1) * R]], T.pin[:, (2 * t + h) * R:(2 * t + h + 1) * R], 0, [("p", t, h)])],
-                 QK(h) + DK(h), 256e3)
-            mm("L%d" % h, [(bank(0, h), T.Lc[:], q, False, True, 512)], ["Lc"] + QK(h), [bk(0, h)])
-            act("m%d" % h, hs_(T.m1, h), bank(0, h), AF.Sign, [], [bk(0, h), ("m1", h)], 512, bias=-0.5)
+            q, p = pq_(T.pq, par, 1, 2 * h, 2 * h + 2), pq_(T.pq, par, 0, 2 * h, 2 * h + 2)
+            sd = (1, [p, q], pq_(T.pin, t, 1, 2 * h, 2 * h + 2), 1, [("d", t, h)])
+            sp = lambda h: (1, [pq_(T.pq, par, 0, 2 * h, 2 * h + 2)], pq_(T.pin, t, 0, 2 * h, 2 * h + 2), 0, [("pi", t, h)])
+            if opt["p32"]:
+                send("sr%d" % h, [sd], QK(h) + PK(h), 200e3)
+                if h and t < TK - 1:
+                    send("sp", [(1, [T.po[:, o2:o2 + R]], T.pw[:, t * R:t * R + R], 0, [("pw", t)])], [("P", par, u) for u in range(4)], 520e3)
+            elif t == TK - 1 or opt["split"]:
+                send("sr%d" % h, [sd], QK(h) + PK(h), 200e3)
+                if h and t < TK - 1:
+                    send("sp", [sp(0), sp(1)], PK(0) + PK(1), 256e3)
+            else:
+                send("sr%d" % h, [sd, sp(h)], QK(h) + PK(h), 400e3)
+            mm("L%d" % h, [(bank(0, h), T.Ln[:], q, False, True, 512)], ["Ln"] + QK(h), [bk(0, h)])
+            sign("m%d" % h, hs_(T.m1, h), bank(0, h), 0.5, [], [bk(0, h), ("m1", h)], 512, True)
             tt("pr%d" % h, hs_(T.pr, h), bank(1, h), q, MUL, QK(h), [bk(1, h), ("pr", h)], 512)
-            mm("e%d" % h, [(bank(2, h), T.I128[:], d, True, False, 512)], ["I128"] + DK(h), [bk(2, h)])
-            mm("D%d" % h, [(bank(2, h), T.Dm[:], hs_(T.m1, h), False, True, 512)], ["Dm", ("m1", h)], [bk(2, h)])
+            mm("e%d" % h, [(bank(2, h), T.I128[:], p, True, False, 512)], ["I128"] + PK(h), [bk(2, h)])
+            mm("D%d" % h, [(bank(2, h), T[dm("m%d" % h)][:], hs_(T.m1, h), False, True, 512)], [dm("m%d" % h), ("m1", h)], [bk(2, h)])
             tt("cm%d" % h, hs_(T.cm, h), bank(2, h), hs_(T.pr, h), OP.is_gt, [("pr", h)], [bk(2, h), ("cm", h)], 512)
             if h in opt["direct"]:
                 offsets("uo%d" % h, "o1%d" % h, listed(T.WAz, hs_(T.cm, h), sm(h, 0, 32), 512), ["WAz", ("cm", h)], "of1", h)
-            mm("fz%d" % h, fold(T.WBy, hs_(T.cm, h), sm(h, 32, 64), True), ["WBy", ("cm", h)], [sk(h, 32)])
+            mm("fz%d" % h, fold(T.WBy, hs_(T.cm, h), sm(h, 32, 64), True), ["WBy", "WByb", ("cm", h)], [sk(h, 32)])
             copy("Z%d" % h, fh(T.Z1, h), sm(h, 32, 64), [], [sk(h, 32), ("Z1", t, h)], 64)
             if h not in opt["direct"]:
-                offsets("uo%d" % h, "o1%d" % h, unfold("bw", fh(T.Z1, h), sm(h, 0, 32), False, True), ["bw0", "bw1", ("Z1", t, h)], "of1", h)
+                offsets("uo%d" % h, "o1%d" % h, unfold("bf", fh(T.Z1, h), sm(h, 0, 32), False, True), ["bf0", "bf1", ("Z1", t, h)], "of1", h)
         send("sz", [(1, [T.Z1[:, 2 * oc:2 * oc + 128]], T.Zin[:, 2 * oc:2 * oc + 128], 0, [("Zin", t)])], [("Z1", t, 0), ("Z1", t, 1)], 32e3)
         su, DW = newsem("d"), [("dW", par, x) for x in range(16)]
         for x in range(16):
-            dma("Y", T.dW[x:128:16, o2:o2 + R], T.ua[:, (3 * t + 1) * R:(3 * t + 2) * R], ["E"], [DW[x]], 100e3, su)
+            dma("Y", T.dW[x:128:16, o2:o2 + R], T.ua[:, (3 * t + 1) * R:(3 * t + 2) * R], ["P"], [DW[x]], 20e3, su)
         if t == 0:
+            dma("Y", T.Et[:], T.nx[:], QK(1) + PK(1), ["E"], 660e3)
             su = newsem("d")
-            dma("Y", T.uu[0:8, 2 * R:2 * TK * R], T.ud[:, 2 * R:], [("p", 0, 1)], ["ura"], 200e3, su)
-            dma("Y", T.uu[32:40, 3 * R:], T.ua[:, 3 * R:], [("p", 0, 1)], ["urb"], 400e3, su)
+            dma("Y", T.uu[0:8, 2 * R:UA], T.ud[:, 2 * R:], [("d", 0, 1)], ["ura"], 200e3, su)
+            dma("Y", T.uu[0:8, UA + 3 * R:], T.ua[:, 3 * R:], [("d", 0, 1)], ["urb"], 400e3, su)
             dma("G", T.Vt[:], T.vf[:], [("Zin", 0)], ["Vt"], 700e3, name="lv")
-        mm("eT", [(sm(0, 128 + 8 * j, 8), ua(2, j // 4, 8)[:, 128 * (j % 4):128 * (j % 4) + 128], T.I1[32:40, 32:40], j == 0, j == 7, 64)
-                  for j in range(8)], ["I1"] + UK, [sk(0, 128)])
-        copy("eC", T.eT[:], sm(0, 128, 64), [], [sk(0, 128), "eT"], 64)
+        mm("eT", [(sm(0, 448 + 8 * j, 8), ua(2, j // 4)[:, 128 * (j % 4):128 * (j % 4) + 128], T.I1[0:8, 0:8], j == 0, j == 7, 64)
+                  for j in range(8)], ["I1"] + UK, [sk(0, 448)])
+        copy("eC", T.eT[:], sm(0, 448, 64), [], [sk(0, 448), "eT"], 64)
         for (a, b) in opt["x1"]:
-            cp("x1%d" % a, Qx.indirect(T.of1[:, 16 * a:16 * b]), pq_(T.pq, par, 0, a, b),
-               [k for u in range(a, b) for k in (("of1", u // 2), ("d", par, u))], ["Q"], 256 * (b - a), "sc")
-        for u in range(4):
-            copy("Eg%d" % u, qs_(T.Eg, u), T.Et[:, :].indirect(T.nin[:, oc + 16 * u:oc + 16 * u + 16]), ["E", ("nin", t)], [("Eg", u)], 256, "ga")
-        for h in range(2):
-            r = hs_(T.rr, h)
-            mm("b%d" % h, [(bank(0, h), T.SA[0:8, :], ud(1, h), True, False, 512)], ["SA"] + UK, [bk(0, h)])
-            mm("U%d" % h, [(bank(1, h), T.I1[:], pq_(T.pin, t, 0, 2 * h, 2 * h + 2), True, False, 512),
-                           (bank(1, h), T.In1[:], pq_(T.pin, t, 1, 2 * h, 2 * h + 2), False, True, 512)], ["I1", "In1", ("p", t, h)], [bk(1, h)])
-            act("r%d" % h, r, bank(1, h), AF.Relu, [], [bk(1, h), ("r", h)], 512)
-            mm("J%d" % h, [(bank(1, h), T.Jh[:], r, True, True, 512)], ["Jh", ("r", h)], [bk(1, h)])
-            mm("R%d" % h, [(bank(2, h), T.I128[:], r, True, False, 512)], ["I128", ("r", h)], [bk(2, h)])
-        for u in range(4):
-            copy("g%d" % u, qs_(T.q2, u), Qr.indirect(T.nin[:, oc + 16 * u:oc + 16 * u + 16]), ["Q", ("nin", t)], [("q2", u)], 256, "ga")
-        for h in range(2):
-            r, q2, K2 = hs_(T.rr, h), hs_(T.q2, h), [("q2", 2 * h), ("q2", 2 * h + 1)]
-            mn = hs_(T.mn, h)
-            mm("M%d" % h, [(bank(0, h), T.Lc[:], q2, False, True, 512)], ["Lc"] + K2, [bk(0, h)])
-            act("n%d" % h, hs_(T.m2, h), bank(0, h), AF.Sign, [], [bk(0, h), ("m2", h)], 512, bias=-0.5)
-            tt("y%d" % h, bank(1, h), bank(1, h), q2, MUL, K2, [bk(1, h)], 512)
-            tt("mn%d" % h, mn, bank(1, h), r, OP.min, [("r", h), bk(1, h)], [("mn", h)], 512)
-            tt("pq%d" % h, hs_(T.pr, h), bank(1, h), hs_(T.dW, h, o2), MUL, DW + [bk(1, h)], [("pr", h)], 512)
-            mm("E%d" % h, [(bank(2, h), T.Dm[:], hs_(T.m2, h), False, True, 512)], ["Dm", ("m2", h)], [bk(2, h)])
-            tt("cn%d" % h, hs_(T.cn, h), bank(2, h), hs_(T.pr, h), OP.is_gt, [("pr", h)], [bk(2, h), ("cn", h)], 512)
-            mm("fy%d" % h, [(sm(h, 256, 64), T.MV[:], fh(T.Zin, h), True, False, 64)] + fold(T.WBy, hs_(T.cn, h), sm(h, 256, 64), False),
-               ["MV0", "MV1", ("Zin", t), "WBy", ("cn", h)], [sk(h, 256)])
-            act("u%d" % h, c64(T.u2, h), sm(h, 256, 64), AF.Relu, [], [sk(h, 256), ("u2", h)], 64)
-            if t < TK - 1:
-                offsets("up%d" % h, "o2%d" % h, unfold("bw", c64(T.u2, h), sm(h, 0, 32), False, True), ["bw0", "bw1", ("u2", h)], "of2", h)
-            tot = sm(h, 96, 32)
-            mm("fw%d" % h, [(tot[:, 8 * j:8 * j + 8], r[:, 128 * j:128 * j + 128], T.B8[:], j == 0, False, 64) for j in range(4)]
-               + [(tot[:, 8 * j:8 * j + 8], mn[:, 128 * j:128 * j + 128], T.B32[:], False, j == 3, 256) for j in range(4)],
-               ["B8", "B32", ("r", h), ("mn", h)], [sk(h, 96)])
-            mm("N%d" % h, [(bank(0, h), T.Lsn[:], r, True, False, 512)], ["Lsn", ("r", h)], [bk(0, h)])
-            for u in range(2):
-                mm("C%d" % (2 * h + u), [(bank(0, h)[:, 256 * u:256 * u + 256], T.Ls32[:], qs_(T.mn, 2 * h + u), False, False, 1024)],
-                   ["Ls32", ("mn", h)], [bk(0, h)])
-            e, hi, lo = T.eT[:, 32 * h:32 * h + 32], T.HL[:, 128 * h:128 * h + 32], T.HL[:, 128 * h + 64:128 * h + 96]
-            tr = sm(h, 128, 128)
-            if opt["lo"] == "V":
-                tt("gA%d" % h, hi, tot, e, MUL, ["eT"], [sk(h, 96), ("HL", h)], 32)
-                tt("gB%d" % h, tot, tot, e, MUL, ["eT"], [sk(h, 96)], 32)
-                tt("gC%d" % h, lo, tot, hi, SUB, [("HL", h), sk(h, 96)], [sk(h, 96), ("HL", h)], 32)
-                mm("tr%d" % h, [(tr, T.HL[:, 128 * h:128 * h + 128], T.I16[:], True, True, 128)], ["I16", ("HL", h)], [sk(h, 128)])
+            if "x1%d" % a in on_v:
+                cp("x1%d" % a, Qx.indirect(T.of1[:, 16 * a:16 * b]), pq_(T.pq, par, 0, a, b),
+                   [("of1", a // 2)] + [("p", par, u) for u in range(a, b)] + [("Qc", u) for u in range(4)], ["Q"], 256 * (b - a), "sc")
             else:
-                gg, o = T.gg[:, 96 * h + 64:96 * h + 96], 128 * h + 64
-                tt("gB%d" % h, gg, tot, e, MUL, ["eT"], [sk(h, 96), ("gg", h)], 32)
-                if opt["lo"] == "S":
-                    copy("gA%d" % h, lo, gg, [("gg", h)], [("HL", h)], 32)
-                else:
-                    tt("gA%d" % h, lo, tot, e, MUL, ["eT"], [sk(h, 96), ("HL", h)], 32)
-                mm("tr%d" % h, [(tr[0:96, :], T.gg[:, 96 * h:96 * h + 96], T.I32[:], True, False, 512),
-                                (tr[0:96, :], T.HL[:, o:o + 96], T.I16[:], False, False, 128),
-                                (tr[0:96, :], T.HL[:, o - 64:o + 32], T.In16[:], False, True, 128)],
-                   ["I16", "In16", "I32", ("HL", h), ("gg", h)], [sk(h, 128)])
-            hf = T.HF[:, 128 * h:128 * h + 128]
-            tr, hf = (tr, hf) if opt["lo"] == "V" else (tr[0:96, :], hf[0:96, :])
+                fn = lambda o=Qx.indirect(T.of1[:, 16 * a:16 * b]), x=T.po[:, o2 + 256 * a:o2 + 256 * b]: S.activation(o, x, AF.Tanh)
+                add("x1%d" % a, "S", fn, [("of1", a // 2)] + [("P", par, u) for u in range(a, b)] + [("Qc", u) for u in range(4)], ["Q"], ("sc", 256 * (b - a)))
+        if t < TK - 1 and not opt["p32"]:
+            if opt["split"]:
+                dma("G", T.p32[:], T.pin[:, 2 * t:2 * t + 2, 0, :], [("pi", t, 0), ("pi", t, 1)], [("p32", 0), ("p32", 1)], 600e3, name="pc")
+            else:
+                for h in range(2):
+                    if any("x2%d" % a not in on_v and a // 2 == h for a, b in opt["x2"]):
+                        dma("G", hs_(T.p32, h), T.pin[:, 2 * t + h, 0, :], [("pi", t, h)], [("p32", h)], 300e3, name="pc%d" % h)
+        for (a, b) in opt["eg"]:
+            copy("Eg%d" % a, T.Eg[:, 256 * a:256 * b], T.Et[:, :].indirect(T.nin[:, oc + 16 * a:oc + 16 * b]), ["E", ("nin", t)],
+                 [("Eg", u) for u in range(a, b)], 256 * (b - a), "ga")
+        dd = lambda h: pq_(T.pin, t, 1, 2 * h, 2 * h + 2)
+        for h in range(2):
+            mm("b%d" % h, [(bank(0, h), T.SA[0:8, :], ud(1, h), True, False, 512)], ["SA"] + UK, [bk(0, h)])
+            relu("r%d" % h, hs_(T.rr, h), dd(h), [("d", t, h)], [("r", h)], 512, f=0.5)
+            mm("J%d" % h, [(bank(1, h), T.Jh[:], hs_(T.rr, h), True, True, 512)], ["Jh", ("r", h)], [bk(1, h)])
+            mm("N%d" % h, [(bank(2, h), T.Lsn[:], dd(h), True, False, 512)], ["Lsn", ("d", t, h)], [bk(2, h)])
+        for (a, b) in opt["g"]:
+            copy("g%d" % a, T.q2[:, 256 * a:256 * b], Qr.indirect(T.nin[:, oc + 16 * a:oc + 16 * b]), ["Q", ("nin", t)],
+                 [("q2", u) for u in range(a, b)], 256 * (b - a), "ga", -1.0)
+        for h in range(2):
+            q2, K2, mn = hs_(T.q2, h), [("q2", 2 * h), ("q2", 2 * h + 1)], hs_(T.mn, h)
+            mm("M%d" % h, [(bank(0, h), T.Ln[:], q2, False, True, 512)], ["Ln"] + K2, [bk(0, h)])
+            sign("n%d" % h, hs_(T.m2, h), bank(0, h), 0.5, [], [bk(0, h), ("m2", h)], 512, True)
+            tt("y%d" % h, bank(1, h), bank(1, h), q2, MUL, K2, [bk(1, h)], 512)
+            tt("mn%d" % h, mn, bank(1, h), dd(h), MIN, [("d", t, h), bk(1, h)], [("mn", h)], 512)
+            tt("pq%d" % h, hs_(T.pr, h), bank(1, h), hs_(T.dW, h, o2), MUL, DW + [bk(1, h)], [("pr", h)], 512)
+            mm("R%d" % h, [(bank(0, h), T.I128[:], dd(h), True, False, 512)], ["I128", ("d", t, h)], [bk(0, h)])
+            mm("E%d" % h, [(bank(0, h), T[dm("n%d" % h)][:], hs_(T.m2, h), False, True, 512)], [dm("n%d" % h), ("m2", h)], [bk(0, h)])
+            tt("cn%d" % h, hs_(T.cn, h), bank(0, h), hs_(T.pr, h), OP.is_gt, [("pr", h)], [bk(0, h), ("cn", h)], 512)
+            mm("fy%d" % h, [(sm(h, 256, 64), T.MZ[:], fh(T.Zin, h), True, False, 64)] + fold(T.WBy, hs_(T.cn, h), sm(h, 256, 64), False),
+               ["MZ", ("Zin", t), "WBy", "WByb", ("cn", h)], [sk(h, 256)])
+            relu("u%d" % h, c64(T.u2, h), sm(h, 256, 64), [], [sk(h, 256), ("u2", h)], 64)
+            if t < TK - 1:
+                offsets("up%d" % h, "o2%d" % h, unfold("bf", fh(T.Zin, h), sm(h, 0, 32), False, False) + unfold("bf", c64(T.u2, h), sm(h, 0, 32), False, True),
+                        ["bf0", "bf1", ("u2", h), ("Zin", t)], "of2", h)
+            tot, tk_ = (sm(0, 96 + 32 * h, 32), sk(0, 96 + 32 * h)) if opt["gfull"] else (sm(h, 96, 32), sk(h, 96))
+            mm("fw%d" % h, [(tot[:, 8 * j:8 * j + 8], mn[:, 128 * j:128 * j + 128], T.B32[:], j == 0, j == 3, 256) for j in range(4)],
+               ["B32", ("mn", h)], [tk_])
+            for u in range(2):
+                mm("C%d" % (2 * h + u), [(bank(2, h)[:, 256 * u:256 * u + 256], T.Ls32[:], qs_(T.mn, 2 * h + u), False, False, 1024)],
+                   ["Ls32", ("mn", h)], [bk(2, h)])
+            if opt["gfull"]:
+                if h == 0:
+                    continue
+                tot, tk_, hi, lo = sm(0, 96, 64), [sk(0, 96), sk(0, 128)], T.HL[:, 0:64], T.HL[:, 64:128]
+                tt("gA1", hi, tot, T.eT[:], MUL, ["eT"], tk_ + ["HL"], 64)
+                tt("gB1", tot, tot, T.eT[:], MUL, ["eT"], tk_, 64)
+                tt("gC1", lo, tot, hi, SUB, ["HL"] + tk_, tk_ + ["HL"], 64)
+                mm("tr1", [(sm(1, 128, 128), T.HL[:, 0:128], T.I16[:], True, True, 128)], ["I16", "HL"], [sk(1, 128)])
+                copy("hF1", T.HF[:, 0:128], sm(1, 128, 128), [], [sk(1, 128), "HF"], 128)
+                for x in range(2):
+                    mm("Th%d" % x, [(bank(2, x)[:, 128 * j:128 * j + 128], T.TH[:, 512 * x + 128 * j:512 * x + 128 * j + 128], T.HF[:, 0:128], False, j == 3, 128)
+                                    for j in range(4)], THK + ["HF"], [bk(2, x)])
+                    sign("ct%d" % x, hs_(T.cnt, x), bank(2, x), -1.0 / 512, [], [bk(2, x), ("cnt", x)], 512)
+                continue
+            e, hi, lo = T.eT[:, 32 * h:32 * h + 32], T.HL[:, 128 * h:128 * h + 32], T.HL[:, 128 * h + 64:128 * h + 96]
+            tr, hf = sm(h, 128, 128), T.HF[:, 128 * h:128 * h + 128]
+            tt("gA%d" % h, hi, tot, e, MUL, ["eT"], [sk(h, 96), ("HL", h)], 32)
+            tt("gB%d" % h, tot, tot, e, MUL, ["eT"], [sk(h, 96)], 32)
+            tt("gC%d" % h, lo, tot, hi, SUB, [("HL", h), sk(h, 96)], [sk(h, 96), ("HL", h)], 32)
+            mm("tr%d" % h, [(tr, T.HL[:, 128 * h:128 * h + 128], T.I16[:], True, True, 128)], ["I16", ("HL", h)], [sk(h, 128)])
             copy("hF%d" % h, hf, tr, [], [sk(h, 128), ("HF", h)], 128)
-            mm("Th%d" % h, [(bank(0, h)[:, 128 * j:128 * j + 128], T.TH[0:hf.shape[0], 128 * j:128 * j + 128], hf, False, j == 3, 128) for j in range(4)],
-               THK + [("HF", h)], [bk(0, h)])
-            act("ct%d" % h, hs_(T.cnt, h), bank(0, h), AF.Sign, [], [bk(0, h), ("cnt", h)], 512, bias=1.0 / 512)
+            mm("Th%d" % h, [(bank(2, h)[:, 128 * j:128 * j + 128], T.TH[:, 128 * j:128 * j + 128], hf, False, j == 3, 128) for j in range(4)],
+               THK + [("HF", h)], [bk(2, h)])
+            sign("ct%d" % h, hs_(T.cnt, h), bank(2, h), -1.0 / 512, [], [bk(2, h), ("cnt", h)], 512)
         if t < TK - 1:
             for (a, b) in opt["x2"]:
-                cp("x2%d" % a, Qx.indirect(T.of2[:, 16 * a:16 * b]), pq_(T.pin, t, 0, a, b),
-                   [k for u in range(a, b) for k in (("of2", u // 2), ("p", t, u // 2))], ["Q"], 256 * (b - a), "sc")
+                if opt["p32"]:
+                    o, x = Qx.indirect(T.of2[:, 16 * a:16 * b]), T.pw[:, t * R + 256 * a:t * R + 256 * b]
+                    fn = (lambda o=o, x=x: V.tensor_copy(o, x)) if "x2%d" % a in on_v else (lambda o=o, x=x: S.activation(o, x, AF.Tanh))
+                    add("x2%d" % a, "V" if "x2%d" % a in on_v else "S", fn, [("of2", a // 2), ("pw", t)], ["Q"], ("sc", 256 * (b - a)))
+                elif "x2%d" % a in on_v:
+                    cp("x2%d" % a, Qx.indirect(T.of2[:, 16 * a:16 * b]), pq_(T.pin, t, 0, a, b), [("of2", a // 2), ("pi", t, a // 2)], ["Q"], 256 * (b - a), "sc")
+                else:
+                    fn = lambda o=Qx.indirect(T.of2[:, 16 * a:16 * b]), x=T.p32[:, 256 * a:256 * b]: S.activation(o, x, AF.Tanh)
+                    add("x2%d" % a, "S", fn, [("of2", a // 2), ("p32", a // 2)], ["Q"], ("sc", 256 * (b - a)))
         for h in range(2):
             ub = c64(T.ub, h)
             mm("I%d" % h, [(bank(1, h), T.I1[:], hs_(T.Eg, h), True, False, 512)], ["I1", ("Eg", 2 * h), ("Eg", 2 * h + 1)], [bk(1, h)])
-            mm("fc%d" % h, [(sm(h, 320, 64), T.MV[:], c64(T.u2, h), True, False, 64)] + fold(T.WBc, hs_(T.cnt, h), sm(h, 320, 64), False),
-               ["WBc", "MV0", "MV1", ("cnt", h), ("u2", h)], [sk(h, 320)])
-            act("ub%d" % h, ub, sm(h, 320, 64), AF.Relu, [], [sk(h, 320), ("ub", h)], 64)
+            mm("fc%d" % h, [(sm(h, 320, 64), T.MU[:], fh(T.Zin, h), True, False, 64), (sm(h, 320, 64), T.MU[:], c64(T.u2, h), False, False, 64)]
+               + fold(T.WBc, hs_(T.cnt, h), sm(h, 320, 64), False), ["WBc", "MU", "MUb", ("Zin", t), ("cnt", h), ("u2", h)], [sk(h, 320)])
+            off16 = last("ct%d" % h) in on_v
+            relu("ub%d" % h, ub, sm(h, 320, 64), [k16] if off16 else [], [sk(h, 320), ("ub", h)], 64, c16 if off16 else 0.0)
             mm("s%d" % h, [(sm(h, 384, 64), T.Sh[:], ub, True, True, 64)], ["Sh", ("ub", h)], [sk(h, 384)])
-            act("tb%d" % h, c64(T.tb, h), sm(h, 384, 64), AF.Sign, [], [sk(h, 384), ("tb", h)], 64, bias=-17.5)
-            mm("k%d" % h, [(sm(h, 448, 64), T.Sh[:], ub, True, False, 64), (sm(h, 448, 64), T.In8[:], c64(T.tb, h), False, True, 64)],
-               ["Sh", "In8", ("ub", h), ("tb", h)], [sk(h, 448)])
-            act("kk%d" % h, c64(T.kk, h), sm(h, 448, 64), AF.Square, [kSq], [sk(h, 448), ("kk", h)], 64, bias=cSq)
+            act("kk%d" % h, c64(T.kk, h), sm(h, 384, 64), AF.Square, [kSq], [sk(h, 384), ("kk", h)], 64, bias=cSq)
+            act("ab%d" % h, c64(T.ab, h), sm(h, 384, 64), AF.Abs, [kAb], [sk(h, 384), ("ab", h)], 64, bias=cAb)
             mm("K%d" % h, [(bank(1, h)[:, i:512:8], T.KB[:, 128 * i:128 * i + 128], c64(T.kk, h), False, i == 7, 64) for i in range(8)],
                KBK + [("kk", h)], [bk(1, h)])
-            act("se%d" % h, hs_(T.sel, h), bank(1, h), AF.Relu, [kSe], [bk(1, h), ("sel", h)], 512, bias=cSe)
-            if not opt["full"]:
-                nx_ = sm(h, 0, 32)
-                mm("v%d" % h, unfold("bk", ub, nx_, True, False), ["bk0", "bk1", ("ub", h), ("kk", h)], [sk(h, 0)], 1)
-                mm("W%d" % h, listed(T.WAe, hs_(T.sel, h), nx_, 512), ["WAe", ("sel", h)], [sk(h, 0)], -1)
-                ts("nn%d" % h, T.nl[:, oc + 64 + 32 * h:oc + 96 + 32 * h], nx_, -1.0, None, ADD, None, [], [sk(h, 0), ("nl", t + 1, h)], 32)
-        if opt["full"]:
-            nx_ = sm(0, 256, 64)
-            mm("v1", [(nx_, T["bk%d" % b][:], T.ub[:, b:128:2], b == 0, False, 64) for b in range(2)],
-               ["bk0", "bk1", ("ub", 0), ("ub", 1), ("kk", 0)], [sk(0, 256)], 1)
-            mm("W1", listed(T.WAe, T.sel, nx_, R), ["WAe", ("sel", 0), ("sel", 1)], [sk(0, 256)], -1)
-            ts("nn1", T.nl[:, oc + 64:oc + 128], nx_, -1.0, None, ADD, None, [], [sk(0, 256), ("nl", t + 1, 0), ("nl", t + 1, 1)], 64)
+            ts("se%d" % h, hs_(T.sel, h), bank(1, h), cLo, cHi, MAX, MIN, [kLo, kHi], [bk(1, h), ("sel", h)], 512)
+        for hh in ([(0, 1)] if opt["full"] else [(0,), (1,)]):
+            h, n = hh[-1], 32 * len(hh)
+            nx_, key = (sm(0, 256, n), sk(0, 256)) if n == 64 else (sm(h, 0, n), sk(h, 0))
+            a = 64 * hh[0]
+            mm("v%d" % h, unfold("bk", T.ub[:, a:a + 2 * n], nx_, True, False, 2 * n) + unfold("bf", T.ab[:, a:a + 2 * n], nx_, False, False, 2 * n),
+               ["bk0", "bk1", "bf0", "bf1"] + [(k, x) for k in ("ub", "ab") for x in hh], [key], 1)
+            mm("W%d" % h, listed(T.WAe, T.sel[:, 8 * a:8 * a + 16 * n], nx_, 16 * n), ["WAe"] + [("sel", x) for x in hh], [key], -1)
+            ts("nn%d" % h, T.nl[:, oc + 64 + a // 2:oc + 64 + a // 2 + n], nx_, -1.0, -170753.0, MUL, ADD, [], [key] + [("nl", t + 1, x) for x in hh], n)
         if t < TK - 1:
             nn = T.nl[:, oc + 64:oc + 128]
             it = [(1, [nn], T.nin[:, oc + 64:oc + 128], 0, [("nin", t + 1)])]
@@ -460,11 +525,13 @@ def build(g, core, T, topo, rank, opt=OPT):
             if off > 1:
                 it.append((off, [nn], T.hl[:, (off - 2) * 64:(off - 2) * 64 + 64], 0, [("hl", off)]))
             send("sn", it, [("nl", t + 1, 0), ("nl", t + 1, 1)], 16e3)
-        else:
-            cp("nf", T.nF[:], T.nl[:, 64:], [("nl", k + 1, h) for k in range(TK) for h in range(2)], ["nF"], TK * 64)
-            dma("Y", T.yn[:], T.nF[:], ["nF"], ["yn"], 200e3)
+        if t == TK - 2:
+            cp("nF", T.nF[:, 0:oc + 64], T.nl[:, 64:oc + 128], [("nl", k + 1, h) for k in range(t + 1) for h in range(2)], ["nFa"], oc + 64)
         h_step(t)
-        rot = [rot[2], rot[0], rot[1]]
+        if t == TK - 1:
+            cp("hvn", T.nF[:, oc:], T.nl[:, oc + 64:], [("nl", t + 1, 0), ("nl", t + 1, 1)], ["nFb"], 64)
+            dma("S", T.yn[:], T.nF[:], ["nFa", "nFb"], ["yn"], 200e3, name="hty")
+        rot = [rot[0], rot[2], rot[1]]
     return ops
 
 
@@ -487,20 +554,16 @@ def times(o, c):
 
 def order(ops, lists=ORDER, c=COST):
     n = len(ops)
-    named, queue, fill = {}, {e: [] for e in "VSPGY"}, {e: [] for e in "VSPGY"}
+    named, queue = {}, {e: [] for e in "VSPGY"}
     for i, o in enumerate(ops):
         if o["name"] == "ld" or o["eng"] == "Y":
             queue[o["eng"]].append(i)
         elif o["name"]:
-            named[(o["name"], o["tok"])] = i
-        elif o["eng"]:
-            fill[o["eng"]].append(i)
+            named.setdefault((o["name"], o["tok"]), []).append(i)
     for t in range(-1, TK + 1):
         for e, names in lists.items():
             for w in names.split():
-                k = (w.rstrip("+-"), t + (w[-1] == "+") - (w[-1] == "-"))
-                if k in named and ops[named[k]]["eng"] == e:
-                    queue[e].append(named.pop(k))
+                queue[e] += named.pop((w.rstrip("+-"), t + (w[-1] == "+") - (w[-1] == "-")), [])
     assert not named, named
     deps = [dict(o["deps"]) for o in ops]
     succ = [[] for _ in ops]
@@ -541,21 +604,14 @@ def order(ops, lists=ORDER, c=COST):
         best = None
         for e in queue:
             a = can(queue[e][head[e]]) if head[e] < len(queue[e]) else None
-            pick = (a, queue[e][head[e]]) if a is not None else None
-            for i in fill[e]:
-                b = can(i)
-                if b is not None and (a is None or b + tm[i][0] <= a + 0.05) and (pick is None or b < pick[0] - 0.05):
-                    pick = (b, i)
-            if pick and (best is None or pick < best):
-                best = pick
-        assert best, "the queues wait for one another"
+            if a is not None and (best is None or (a, queue[e][head[e]]) < best):
+                best = (a, queue[e][head[e]])
+        assert best, [(ops[q[head[e]]]["name"], ops[q[head[e]]]["tok"], [ops[j]["name"] for j in deps[q[head[e]]] if not end[j]])
+                      for e, q in queue.items() if head[e] < len(q)]
         st, i = best
         o = ops[i]
         e = o["eng"]
-        if i in fill[e]:
-            fill[e].remove(i)
-        else:
-            head[e] += 1
+        head[e] += 1
         if o["bank"]:
             b = o["bank"][0]
             if b in user:

from concourse.bass import DstId, RemoteDMATransfer
from concourse.mybir import AluOpType as OP, ActivationFunctionType as AF

W, R, TK, NR = 2560, 1024, 6, 4
SG = 2.0 ** -12
H = 65536.0
BF, F32, F16, I32, U16 = "bfloat16", "float32", "float16", "int32", "uint16"

SCRATCH = {
    "Qw": ("sbuf", [128, 3 * W], F32), "uu": ("sbuf", [128, 5 * TK * R], BF),
    "pq": ("sbuf", [128, 4, 2, 512], BF), "pin": ("sbuf", [128, 2 * TK, 2, 512], BF), "dW": ("sbuf", [128, 2 * R], BF),
    "n0i": ("sbuf", [128, 64], I32), "spi": ("sbuf", [128, TK * 64], I32), "sP": ("sbuf", [128, TK * 64], F16),
    "nl": ("sbuf", [128, (TK + 1) * 64], U16), "nin": ("sbuf", [128, TK * 64], U16), "hl": ("sbuf", [128, 128], U16),
    "of1": ("sbuf", [128, 64], U16), "of2": ("sbuf", [128, 64], U16), "nF": ("sbuf", [128, TK * 64], F32),
    "Z1": ("sbuf", [128, TK * 128], BF), "Zin": ("sbuf", [128, TK * 128], BF), "eT": ("sbuf", [128, 64], BF),
    "HL": ("sbuf", [128, 256], F16), "HF": ("sbuf", [128, 256], F16), "I16": ("sbuf", [128, 128], F16),
    "TH": ("sbuf", [128, R], F16), "sel": ("sbuf", [128, R], F16), "WAe": ("sbuf", [128, 144], F16),
    "ci": ("sbuf", [128, 8], I32), "cf": ("sbuf", [128, 32], F32), "cj": ("sbuf", [128, 8], F32),
    "Ls32": ("sbuf", [128, 128], F32), "B32": ("sbuf", [128, 8], F32),
    "p32": ("sbuf", [128, R], F32),
    "ps": ("psum", [128, 4096], F32),
}
for _n in ("Q0", "Pt", "Et", "Vt"):
    SCRATCH[_n] = ("sbuf", [128, W], BF)
for _n in ("q2", "rr", "m1", "m2", "cm", "cn", "cnt", "Eg", "Vg", "KB"):
    SCRATCH[_n] = ("sbuf", [128, R], BF)
for _n in ("pr", "mn", "hA", "hs"):
    SCRATCH[_n] = ("sbuf", [128, R], F32)
for _n in ("BM", "Ln", "Dm", "Dm2", "t1", "t2", "t3", "t4", "t5", "t6", "t7", "I128", "Lsn", "I1", "MU", "MZ", "Jh", "E64", "bf0", "bf1",
           "Sh", "bk0", "bk1", "SA", "iG", "iD", "iX", "G8", "KA", "u2", "ub", "ab", "kk"):
    SCRATCH[_n] = ("sbuf", [128, 128], BF)
for _n in ("WAz", "WBc", "WBy", "iM", "iU"):
    SCRATCH[_n] = ("sbuf", [128, 192], BF)

SEMAPHORES = (["eV", "eS", "eP", "eG"] + ["d%d" % i for i in range(36)] + ["l%d" % i for i in range(36)]
              + ["a%d" % i for i in range(58)])

ORDER = {'V': 'hv0- hv1- hv2- hv3- hvn- q2 pr0 pr1 cm0 cm1 o10 x10 o11 x12 nF- g0 g2 y0 mn0 pq0 cn0 y1 mn1 o20 gA0 gB0 pq1 gC0 gA1 gB1 gC1 cn1 ct0 u1 ct1 o21 x22 se0 se1 nn0 p1+ nn1 q1+ q3+', 'S': 'ht0- ht1- ht2- ht3- m1 Qc3 Qc2 Qc0 Vg0- Vg2- Vg3- Vg1- eC Z1 Eg2 r0 r1 Z0 Eg1 Eg0 g1 g3 n0 n1 Eg3 th1- u0 th0- x20 hF0 hF1 x21 ub0 kk0 ub1 ab0 kk1 ab1 x23 p0+ q0+ p2+ Qc1+ p3+ m0+', 'P': 'L0 c1 L1 e0 D0 e1 D1 uo0 b0 fz1 uo1 N0 fz0 J0 b1 J1 N1 M0 M1 R0 E0 fw0 R1 C0 fy0 E1 up0 C1 fw1 C2 tr0 C3 tr1 Th0 fy1 Th1 fc0 up1 I0 s0 fc1 K0 s1 I1 K1 v0 W0 v1 W1 c0+ a1+ eT+ a0+', 'G': 'lv- sn- sr0 sp sr1 ha- sz pc'}
ORDER = {'V': 'x12 g0 hvn- g2 y0 mn0 pq0 cn0 hv2- y1 mn1 Qc0+ gA0 gB0 o20 gC0 pq1 gA1 hF0 gB1 gC1 cn1 ct0 u1 ub0 o21 x22 se0 se1 nn0 hv0 hv3- p0+ q1+ nn1 q2+ q3+ pr0+ kaV+ pr1+ cm0+ kbV+ nF cm1+ o10+ x10+ hv1 o11+', 'S': 'r0 kfS Vg3- Eg0 Qc3+ kiS r1 hty- g1 g3 kcS+ ht1- n0 ht2- Qc1+ n1 eC keS Eg3 u0 kgS khS x20 hF1 x21 ct1 kk0 ab0 ub1 kk1 ab1 x23 q0+ p1+ ht3- p2+ m0+ p3+ m1+ Qc2+ th0- th1- kdS+ Vg0 Eg1+ Z1+ Vg2 Eg2+ Z0+ ht0 Vg1', 'P': 'a1 c1 L0 e0 L1 D0 e1 D1 uo0 fz1 uo1 fz0 b1 b0 N1 J0 kgP+ J1 M0 eT N0 M1 R0 E0 C0 fw0 fy0 C1 up0 R1 E1 fw1 tr0 C2 Th0 tr1 C3 fy1 Th1 fc0 up1 c0+ I0 s0 fc1 K0 s1 v0 I1 K1 W0 v1 a0+ W1', 'G': 'sr0 sp sr1 sz pc ha- lv sn'}
ORDER = {'V': 'g0 g2 y0 pq0 mn0 cn0 y1 mn1 gA0 gB0 o20 gC0 pq1 gA1 hF0 gB1 Qc0+ gC1 cn1 ct0 u1 ub0 kbV+ o21 x22 se0 se1 nn0 p0+ hv0 nn1 q1+ q2+ hvn hv1 pr0+ hv3- p2+ pr1+ cm0+ kaV+ nF hv2 cm1+ o10+ x10+ o11+ x12+', 'S': 'g3 n0 Qc1+ n1 kfS Qc2+ Eg0 u0 Eg2 x20 hF1 x21 ct1 kk0 ub1 ab0 kk1 ab1 x23 q0+ p1+ q3+ p3+ m0+ m1+ keS+ hty- Qc3+ ht1- th0- khS+ ht2- Vg2 Z0+ Z1+ kcS+ th1- kdS+ eC+ r0+ ht3- ht0 kiS+ kgS+ Vg0 r1+ g1+', 'P': 'uo0 fz1 fz0 uo1 eT b1 J0 b0 N1 M0 N0 M1 J1 R0 E0 R1 E1 fw0 kgP+ fy0 C0 up0 C1 fw1 tr0 C2 Th0 tr1 C3 Th1 fy1 fc0 up1 a1+ I0 s0 fc1 K0 s1 I1 K1 v0 W0 v1 W1 a0+ c0+ L0+ c1+ L1+ e0+ D0+ e1+ D1+', 'G': 'sn- sr0 sr1 sz pc0 pc1 ha- lv'}
ORDER = {'V': 'P2 Z1 hv2- P3 nF- kbV+ o11 Qc1+ x12 x13 g1 r1 y0 mn0 y1 pq0 Qc0+ hv3- gA0 cn0 mn1 gB0 u0 gC0 pq1 o20 gA1 gB1 gC1 hF0 cn1 hF1 ct0 u1 ct1 o21 x22 se0 se1 nn0 hv0 q1+ p1+ hv1 nn1 q2+ kaV+ pr0+ hvn cm0+ p2+ o10+ pr1+ P1+ cm1+', 'S': 'n1 Eg2 Eg0 kfS x20 x21 ub0 Qc2+ ht1- kk0 ab0 ub1 kk1 ab1 x23 th0- kcS+ Qc3+ ht2- q0+ khS+ p0+ m0+ q3+ p3+ P0+ m1+ x10+ x11+ th1- Z0+ keS+ r0+ Vg2 kiS+ Vg0 kdS+ ht0 ht3- g0+ g2+ g3+ eC+ hty kgS+ n0+', 'P': 'c1 e0 D0 a1 L1 uo0 e1 fz0 D1 eT fz1 kgP+ b0 uo1 J0 b1 N1 N0 M0 J1 M1 fw0 R0 E0 C0 R1 fy0 E1 fw1 up0 C1 tr0 C2 tr1 Th0 C3 fy1 Th1 fc0 up1 I0 s0 fc1 K0 s1 v0 I1 K1 W0 v1 a0+ W1 L0+ c0+', 'G': 'sz sp lv ha- sr0+ sn sr1+'}
ORDER = {'V': 'u0 pq1 gA1 gB1 gC1 o20 cn1 ct0 u1 ct1 kbV+ nF- o21 x22 se0 se1 nn0 hv0 q1+ nn1 Qc0+ hvn pr0+ m0+ hv1 kaV+ p2+ pr1+ cm0+ hv2 cm1+ o10+ x10+ o11+ x12+ g0+ hv3 y0+ r1+ mn0+ pq0+ y1+ cn0+ mn1+', 'S': 'kjS+ r0 g1 g2 n0 kdS+ n1 kiS kfS kgS+ Eg2 Eg0 hF1 x20 ub0 kk0 ub1 ab0 kk1 ab1 x23 hty- ht1- q0+ p0+ q2+ Qc2+ m1+ th0- Vg0 Qc1+ Qc3+ keS+ kcS+ ht2- Z1+ ht0 Vg2 Z0+ ht3- khS+ eC+', 'P': 'a1 c1 L1 D0 e1 D1 uo0 fz1 b0 fz0 uo1 eT J0 M0 N0 b1 N1 M1 J1 R0 fw0 E0 R1 C0 fy0 C1 fw1 up0 C2 E1 tr1 C3 Th0 fy1 Th1 I0 fc0 up1 I1 s0 fc1 K0 kgP+ s1 c0+ v0 K1 v1 W0 W1 a0+ L0+ e0+', 'G': 'sr1 sz pc0 pc1 lv ha- sn sr0+'}
ORDER = {'V': 'cn0 y1 mn1 pq1 Qc0+ gA1 gB1 gC1 o20 hF1 cn1 nF- ct0 u1 ct1 o21 x22 se0 se1 nn0 hv0 q0+ kbV+ hv1 nn1 q1+ p2+ hvn pr0+ kaV+ pr1+ cm0+ cm1+ o10+ hv2 x10+ o11+ x12+ eC+ g0+ y0+ r1+ hv3 mn0+ pq0+', 'S': 'Qc3+ Qc1+ g1 g2 n0 n1 Eg2 kfS u0x u0 Eg0 hF1x kcS+ khS x20 ct0x ct1x ub0 u1x kk0 ab0 ub1 kk1 th0x- ab1 ht0 x23 p0+ q2+ ht1 m0+ kgS+ hty ht3- m1+ Qc2+ kiS+ kdS+ ht2 th0- Z0+ Z1+ kjS+ Vg2 Vg0 r0+ keS+', 'P': 'D1 uo0 b0 fz0 fz1 uo1 eT N0 J0 b1 M0 N1 M1 J1 R0 E0 C0 fw0 fy0 C1 R1 up0 fw1 E1 C2 tr1 C3 Th0 Th1 kgP+ fy1 I0 fc0 up1 s0 fc1 K0 s1 I1 v0 K1 W0 v1 W1 c0+ a0+ L0+ c1+ a1+ L1+ e0+ D0+ e1+', 'G': 'pc1 ha- lv sn sr0+ sr1+ sz+ pc0+'}
HALVES, QUARTERS = ((0, 2), (2, 4)), ((0, 1), (1, 2), (2, 3), (3, 4))
OPT = dict(direct=(0,), full=False, split=False, p32=(), x1=HALVES, q=((0, 1), (1, 2), (2, 4)), p=HALVES, g=((0, 1), (1, 2), (2, 4)), th=((0, 4),), gfull=True, last=("ct0", "ct1", "hF1", "u0", "u1"), x2=((0, 2), (2, 3), (3, 4)), eg=HALVES, vg=HALVES)
COST = dict(cy=0.0009, pcy=0.00045, ga=1.56, sc=3.8, fix=0.06, lat=0.10, same=0.06, rlat=2.0, riss=0.5, giss=1.0, dlat=1.6, bw=400e3)


def build(g, core, T, topo, rank, opt=OPT):
    ops = []
    lastw, readers = {}, {}
    nsem = {"d": 0, "l": 0, "a": 0}
    tok, grp = [0], ["ld"]
    on_v = opt.get("on_v") or [w.rstrip("+-") for w in ORDER["V"].split()]

    def newsem(k):
        nsem[k] += 1
        return "%s%d" % (k, nsem[k] - 1)

    def add(name, eng, fn, rd, wr, cost, kind="c", sem=None, inc=0, after=(), hold=0, start=False):
        i = len(ops)
        if name is None and eng and eng != "Y":
            name = grp[0] + (eng if grp[0] != "ld" else "")
        deps = {}
        psum = lambda k: k[0] == "b" and k != str(k)
        for k in rd:
            if k in lastw:
                deps[lastw[k]] = True
        for k in wr:
            for j in readers.get(k, []) + ([lastw[k]] if k in lastw else []):
                deps[j] = deps.get(j, False) or not psum(k)
        for j in after:
            deps.setdefault(j, False)
        for k in rd:
            readers.setdefault(k, []).append(i)
        for k in wr:
            lastw[k] = i
            readers[k] = []
        ops.append(dict(name=name, tok=tok[0], eng=eng, fn=fn, deps=deps, cost=cost, kind=kind, sem=sem, inc=inc, hold=hold,
                        start=start, bank=[k[1] for k in wr if psum(k) and len(k) == 3]))
        return i

    V, S, P = g.vector, g.scalar, g.tensor
    EQ, MUL, ADD, SUB, MAX, MIN = OP.is_equal, OP.mult, OP.add, OP.subtract, OP.max, OP.min
    vc = lambda n, f: (f, n) if f == str(f) else ("cy", max(64, n * f))

    def ts(name, out, in0, s1, s2, o0, o1, rd, wr, n, f=1.0):
        if o1 is None:
            return add(name, "V", lambda: V.tensor_scalar(out, in0, s1, None, o0), rd, wr, vc(n, f))
        return add(name, "V", lambda: V.tensor_scalar(out, in0, s1, s2, o0, o1), rd, wr, vc(n, f))

    def tt(name, out, a, b, o, rd, wr, n, f=1.0):
        return add(name, "V", lambda: V.tensor_tensor(out, a, b, o), rd, wr, vc(n, f))

    def cp(name, out, a, rd, wr, n, f=1.0):
        return add(name, "V", lambda: V.tensor_copy(out, a), rd, wr, vc(n, f))

    def act(name, out, a, fn, rd, wr, n, f=1.0, bias=0.0, scale=1.0):
        return add(name, "S", lambda: S.activation(out, a, fn, bias=bias, scale=scale), rd, wr, vc(n, f))

    def copy(name, out, a, rd, wr, n, f=1.0, scale=1.0):
        name = last(name)
        if name not in on_v:
            return act(name, out, a, AF.Copy, rd, wr, n, f, scale=scale)
        return cp(name, out, a, rd, wr, n, f) if scale == 1.0 else ts(name, out, a, scale, None, MUL, None, rd, wr, n, f)

    def last(name):
        return name + "x" if tok[0] == TK - 1 and name in opt["last"] else name

    def relu(name, out, a, rd, wr, n, bias=0.0, f=1.0):
        name = last(name)
        if name in on_v:
            return ts(name, out, a, bias, 0.0, ADD, MAX, rd, wr, n, f)
        return act(name, out, a, AF.Relu, rd, wr, n, bias=bias)

    def sign(name, out, a, over, rd, wr, n, half=False):
        name = last(name)
        if name in on_v:
            return ts(name, out, a, over, 0.5 if half else 2.0, OP.is_gt, SUB if half else MUL, rd, wr, n)
        return act(name, out, a, AF.Sign, rd, wr, n, bias=-over)

    def mm(name, items, rd, wr, hold=0):
        def run():
            r = None
            for (o, l, x, st, sp, c) in items:
                r = P.matmul(o, l, x, st, sp)
            return r
        i = add(name, "P", run, rd, wr, ("pcy", sum(it[5] for it in items)), hold=hold, start=items[0][3])
        ops[i]["nmm"] = len(items)

    def dma(q, out, a, rd, wr, nbytes, sem=None, accum=False, name=None):
        e = {"Y": g.sync, "S": g.scalar, "G": g}[q]
        if accum:
            fn = lambda: e.dma_start(out, a, accum_op=OP.add)
        else:
            fn = lambda: e.dma_start(out, a)
        return add(name, q, fn, rd, wr, ("dma", nbytes), "dma", sem or newsem("d"), 16)

    def send(name, items, rd, nbytes):
        trs, arr, tot = [], [], 0
        for k, (off, srcs, dst, alu, wr) in enumerate(items):
            to = T.cores[(rank + off) % NR]
            en = topo.engines(core, to)
            m = len(en) // len(items)
            mask = sum(1 << e for e in en[k * m:(k + 1) * m])
            rid, pid = topo.addr(to)[:2]
            sem = newsem("a")
            trs.append(RemoteDMATransfer(dst_ids=[DstId(rid=rid, pnc=pid)], dma_engine_mask=mask, remote_sem=T.sem[sem],
                                         srcs=srcs, dsts=[dst], alu_op=alu))
            frm = T.cores[(rank - off) % NR]
            arr.append((sem, len(topo.engines(frm, core)) // len(items), wr))
            tot += m
        ls = newsem("l")
        i = add(name, "G", lambda: g.remote_dma_fused(trs, local_sem=T.sem[ls]), rd, [], ("send", nbytes), "send", ls, tot)
        for (sem, m, wr) in arr:
            add(None, None, None, [], wr, ("arr", 0), "arr", sem, m, after=[i])

    def gp(fn, rd, wr, n):
        return add(None, "G", fn, rd + ["pool"], wr + ["pool"], ("gp", n))

    tok[0] = -1
    UA = 2 * TK * R
    dma("Y", T.n0i[:], T.n0[:], [], ["n0i"], 32e3)
    dma("S", T.Q0[:], T.qd[:], [], ["Q0"], 660e3, name="ld")
    dma("Y", T.Pt[:], T.pt[:], [], ["P"], 660e3)
    su = newsem("d")
    dma("S", T.uu[0:8, 0:2 * R], T.ud[:, 0:2 * R], [], ["u0a"], 40e3, su, name="ld")
    dma("S", T.uu[0:8, UA:UA + 3 * R], T.ua[:, 0:3 * R], [], ["u0b"], 60e3, su, name="ld")
    dma("Y", T.spi[:], T.spot[:], [], ["spi"], 200e3)

    gp(lambda: g.iota(T.ci[:, 0:1], [[0, 1]], 0, 1), [], ["ci0"], 1)
    io = lambda out, pat, base, cm: (lambda: g.iota(out, pat, base, cm, allow_small_or_imprecise_dtypes=True))
    gp(io(T.iG[:], [[1, 8], [0, 16]], 0, 0), [], ["iG"], 128)
    gp(io(T.iD[:], [[1, 128]], 0, -1), [], ["iD"], 128)
    gp(io(T.iM[:], [[1, 192]], 0, 0), [], ["iM"], 192)
    p0 = T.ci[:, 0:1]
    AND, SHR = OP.bitwise_and, OP.logical_shift_right
    ts(None, T.ci[:, 1:2], p0, 15, None, AND, None, ["ci0"], ["ci1"], 1)
    ts(None, T.ci[:, 2:3], p0, 4, None, SHR, None, ["ci0"], ["ci2"], 1)
    cp(None, T.cf[:, 0:3], T.ci[:, 0:3], ["ci0", "ci1", "ci2"], ["cfa"], 3)
    C = lambda k: T.cf[:, k:k + 1]
    cP, cX, cG, cG8, cJ, cU, c63 = [C(k) for k in range(7)]
    ncol = [7]

    def col(a, scale, bias, rd):
        k = ncol[0]
        ncol[0] += 1
        act(None, C(k), a, AF.Identity, rd, [("c", k)], 1, bias=bias, scale=scale)
        return C(k), ("c", k)

    def vcol(a, s1, s2, o0, o1, rd):
        k = ncol[0]
        ncol[0] += 1
        ts(None, C(k), a, s1, s2, o0, o1, rd, [("c", k)], 1)
        return C(k), ("c", k)

    def mat(name, idx, c, w, rd, a=0, b=128):
        ts(None, T[name][:, a:b], T[idx][:, a:b], c, w, EQ, MUL, [idx] + rd, [name if a == 0 else name + "b"], b - a, 0.5)

    def scaled(name, src, w, rd=(), a=0, b=128):
        act(None, T[name][:, a:b], T[src][:, a:b], AF.Identity, [src] + list(rd), [name if a == 0 else name + "b"], b - a, scale=w)

    def summed(name, parts, also=()):
        out, key = T.ps[:, 3712:3840], ("b", 7, 128)
        mm(None, [(out, T.I1[:], T[a][:], a == parts[0], a == parts[-1], 128) for a in parts], ["I1"] + parts, [key])
        for nm, w in ((name, 1.0),) + also:
            act(None, T[nm][:], out, AF.Copy, [], [key, nm], 128, scale=w)

    if not opt["gfull"]:
        add(None, "V", lambda: V.memset(T.HL[:], 0.0), [], [("HL", 0), ("HL", 1)], vc(256, 0.5))
    ts(None, T.ci[:, 3:4], p0, 7, None, AND, None, ["ci0"], ["ci3"], 1)
    ts(None, T.ci[:, 4:5], p0, 3, 7, SHR, AND, ["ci0"], ["ci4"], 1)
    ts(None, T.ci[:, 5:6], p0, 6, None, SHR, None, ["ci0"], ["ci5"], 1)
    ts(None, T.ci[:, 6:7], p0, 63, None, AND, None, ["ci0"], ["ci6"], 1)
    mat("BM", "iG", cG, -1.0 / SG, ["cfa"])
    cp(None, T.cf[:, 3:7], T.ci[:, 3:7], ["ci3", "ci4", "ci5", "ci6"], ["cfb"], 4)
    gp(lambda: g.affine_select(T.Ln[:], T.BM[:], [[1, 128]], OP.is_ge, 0.0, 0, -1), ["BM"], ["Ln"], 128)
    gp(io(T.iU[:], [[0, 3], [1, 64]], 0, 0), [], ["iU"], 192)
    gp(io(T.iX[:], [[0, 8], [256, 16]], 0, 0), [], ["iX"], 128)
    gp(lambda: g.affine_select(T.t5[:], T.BM[:], [[1, 128]], OP.is_gt, 0.0, 0, -1), ["BM"], ["t5"], 128)
    cWa, kWa = col(cG, 16.0, 15.0, ["cfa"])
    cWb, kWb = col(cG, 1.0, 56.0, ["cfa"])
    cWy, kWy = col(cX, 1.0, 1.0, ["cfa"])
    cA, kA = vcol(cX, 15.0, -H, OP.not_equal, MUL, ["cfa"])
    cB, kB = vcol(cX, 15.0, 2 * H * SG, EQ, MUL, ["cfa"])
    cC, kC = vcol(cX, 15.0, H, EQ, MUL, ["cfa"])
    cWc, kWc = vcol(cX, 0.0, 0.0625, EQ, ADD, ["cfa"])
    mat("I128", "iD", 0.0, 128.0, [])
    mat("SA", "iG", cP, -1.0, ["cfa"])
    cb, kb = col(cG8, 16.0, cJ, ["cfb"])
    c64, k64 = col(c63, 1.0, 1.0, ["cfb"])
    cc, kc = col(cb, 1.0, 8.0, [kb])
    scaled("t3", "BM", cB, [kB])
    scaled("I1", "I128", 1.0 / 128)
    scaled("t1", "I128", H / 128)
    mat("t2", "iD", 1.0, cA, [kA])
    mat("t4", "iD", -15.0, cC, [kC])
    mat("I16", "iD", 0.0, 1.0, [])
    mat("G8", "iG", cG8, 1.0, ["cfb"])
    c78, k78 = vcol(cG8, 7.0, None, OP.not_equal, None, ["cfb"])
    cAb, kAb = vcol(cG8, 0.0, -17.5, EQ, ADD, ["cfb"])
    cxx, kxx = vcol(cX, -13.0, cX, ADD, MUL, ["cfa"])
    cp(None, T.nl[:, 0:64], T.n0i[:], ["n0i"], [("nl", 0, 0), ("nl", 0, 1)], 64)
    cs, ks = col(cU, -0.125, 0.0625, ["cfb"])
    ct, kt = col(cU, 208.0, -96.0, ["cfb"])
    cw, kw = col(cU, -float(W), 0.0, ["cfb"])
    cWc, kWc = col(cWc, 8.0, 0.0, [kWc])
    halves = any(w in on_v for w in ("m0", "m1", "n0", "n1"))
    summed("Dm", ["t1", "t2", "t3", "t4"], (("Dm2", 2.0),) * halves)
    mat("WAz", "iM", cWa, float(W), [kWa], 0, 144)
    mat("WBy", "iM", cWb, cWy, [kWb, kWy], 0, 96)
    mat("bk0", "iM", cb, -1.0, [kb])
    mat("bk1", "iM", cc, -1.0, [kc])
    ts(None, T.cj[:], T.iM[:, 0:8], cJ, None, EQ, None, ["iM", "cfb"], ["cj"], 8)
    ts(None, T.B32[:], T.iM[:, 0:8], cG, -1.0 / SG, EQ, MUL, ["iM", "cfa"], ["B32"], 8)
    mat("WAe", "iM", cWa, -16.0, [kWa], 0, 144)
    mat("WBc", "iM", cWb, cWc, [kWb, kWc], 0, 192)
    mat("WBy", "iU", cWb, 1.0, [kWb], 96, 192)
    mat("E64", "iU", c63, 1.0, ["cfb"])
    mat("t6", "iU", c64, c78, [k64, k78])
    scaled("bf0", "bk0", cw, [kw])
    scaled("bf1", "bk1", cw, [kw])
    act(None, T.t7[:], T.iX[:], AF.Identity, ["iX", ks, kt], ["t7"], 128, bias=ct, scale=cs)
    tok[0], grp[0] = 0, "ka"
    ts(None, T.sP[:], T.spi[:], -1024.0, None, ADD, None, ["spi"], ["sP"], TK * 64)
    grp[0] = "kb"
    tt(None, T.KA[:], T.t7[:], T.G8[:], MUL, ["t7", "G8"], ["KA"], 128, 2)
    grp[0] = "kc"
    scaled("Jh", "BM", 1.0 / 256)
    scaled("Lsn", "t5", 128.0)
    scaled("Ls32", "t5", -128.0)
    grp[0] = "kd"
    ca, ka = col(cU, 33.0, -33.0, ["cfb"])
    c1u, k1u = col(cU, -1.0, 1.0, ["cfb"])
    scaled("MZ", "I1", ca, [ka])
    scaled("MU", "E64", ca, [ka], 0, 64)
    scaled("MU", "E64", c1u, [k1u], 64, 128)
    grp[0] = "ke"
    for i in range(8 if opt["gfull"] else 4):
        grp[0] = "ke" if i < 4 else "kj"
        act(None, T.TH[:, 128 * i:128 * i + 128], T.G8[:], AF.Identity, ["G8", "cj"], [("TH", i)], 128, scale=T.cj[:, i:i + 1])
    THK = [("TH", i) for i in range(8 if opt["gfull"] else 4)]
    grp[0] = "kf"
    ca, ka = col(cU, 1.0, 0.5, ["cfb"])
    c16, k16 = col(c1u, -16.0, 0.0, [k1u])
    cLo, kLo = col(cxx, -16.0, 352.0, [kxx])
    cHi, kHi = col(cxx, -16.0, 512.0, [kxx])
    cSq, kSq = col(cAb, 1.0, ca, [kAb, ka])
    grp[0] = "kg"
    summed("Sh", ["t6", "E64"])
    for i in range(8):
        grp[0] = "kh" if i < 4 else "ki"
        act(None, T.KB[:, 128 * i:128 * i + 128], T.KA[:], AF.Identity, ["KA", "cj"], [("KB", i)], 128, scale=T.cj[:, i:i + 1])
    KBK = [("KB", i) for i in range(8)]
    tok[0] = -1

    send("sn", [(1, [T.nl[:, 0:64]], T.nin[:, 0:64], 0, [("nin", 0)])], [("nl", 0, 0), ("nl", 0, 1), "pool"], 16e3)

    Qr, Qx = T.Qw[:, 0:W], T.Qw[:, :]
    hs_ = lambda b, h, o=0: b[:, o + 512 * h:o + 512 * h + 512]
    qs_ = lambda b, u, o=0: b[:, o + 256 * u:o + 256 * u + 256]
    rot = [0, 1, 2]

    def pq_(b, slot, k, a, e):
        return b[:, 2 * slot + a // 2, k, 256 * (a % 2):256 * (a % 2 + e - a)]

    def h_step(t):
        off = (TK - 1 - t) % NR
        if off == 0:
            lst, o, key = T.nl, (t + 1) * 64, lambda h: ("nl", t + 1, h)
        elif off == 1:
            lst, o, key = T.nin, (t + 1) * 64, lambda h: ("nin", t + 1)
        else:
            lst, o, key = T.hl, (off - 2) * 64, lambda h: ("hl", off)
        for (u, b) in opt["vg"] if t < TK - 1 else QUARTERS:
            vi, h = T.Vt[:, :].indirect(lst[:, o + 16 * u:o + 16 * b]), u // 2
            if t == 0:
                act("Vg%d" % u, T.hA[:, 256 * u:256 * b], vi, AF.Tanh, ["Vt", key(h)], [("hA", x) for x in range(u, b)], 256 * (b - u), "ga")
            elif t < TK - 1:
                act("Vg%d" % u, T.Vg[:, 256 * u:256 * b], vi, AF.Copy, ["Vt", key(h)], [("Vg", x) for x in range(u, b)], 256 * (b - u), "ga")
            else:
                tt("hv%d" % u, qs_(T.hs, u), vi, qs_(T.hA, u), ADD, ["Vt", key(h), ("hA", u)], [("hs", u)], 256, "ga")
                act("ht%d" % u, qs_(T.hs, u), qs_(T.hs, u), AF.Tanh, [("hs", u)], [("hs", u)], 256)
                dma("Y", qs_(T.yh, u), qs_(T.hs, u), [("hs", u)], [("yh", u)], 128e3)
        if 0 < t < TK - 1:
            hk = [("hA", u) for u in range(4)]
            dma("G", T.hA[:], T.Vg[:], hk + [("Vg", u) for u in range(4)], hk, 1000e3, accum=True, name="ha")
            for (a, b) in opt["th"]:
                act("th%d" % (a // 2) + "x" * (t == TK - 2), T.hA[:, 256 * a:256 * b], T.hA[:, 256 * a:256 * b], AF.Tanh, hk[a:b], hk[a:b], 256 * (b - a))

    for t in range(TK):
        tok[0] = t
        par, o2, oc = t % 2, (t % 2) * R, t * 64
        UK = ["u0a", "u0b"] if t == 0 else ["ura", "urb"]
        bank = lambda k, h: T.ps[:, 512 * (3 * h + rot[k]):512 * (3 * h + rot[k]) + 512]
        bk = lambda k, h: ("b", 3 * h + rot[k])
        sm = lambda h, a, n: T.ps[:, 512 * (6 + h) + a:512 * (6 + h) + a + n]
        sk = lambda h, a: ("b", 6 + h, a)
        ud = lambda k, h: hs_(T.uu[0:8, :], h, (2 * t + k) * R)
        ua = lambda k, h: hs_(T.uu[0:8, :], h, UA + (3 * t + k) * R)
        QK = lambda h: [("q", par, 2 * h), ("q", par, 2 * h + 1)]
        PK = lambda h: [("p", par, 2 * h), ("p", par, 2 * h + 1)]
        lh = lambda b, h: b[:, oc + 32 * h:oc + 32 * h + 32]
        fh = lambda b, h: b[:, 2 * oc + 64 * h:2 * oc + 64 * h + 64]
        c64 = lambda b, h: b[:, 64 * h:64 * h + 64]
        dm = lambda nm: "Dm2" if nm in on_v else "Dm"

        def fold(wide, src, out, first):
            return [(out, wide[:, 56 - 8 * i:184 - 8 * i], src[:, i:512:8], first and i == 0, i == 7, 64) for i in range(8)]

        def listed(wide, src, out, n):
            return [(out, wide[:, 15 - j:143 - j], src[:, j:n:16], False, j == 15, 64) for j in range(16)]

        def unfold(w, src, out, first, last, n=64):
            return [(out, T[w + str(b)][:], src[:, b:n:2], first and b == 0, last and b == 1, 64) for b in range(2)]

        def offsets(pn, vn, items, rd, dst, h):
            mm(pn, [(sm(h, 0, 32), T.I16[:], lh(T.sP, h), True, False, 64)] + items, ["I16", "sP"] + rd, [sk(h, 0)])
            ts(vn, T[dst][:, 32 * h:32 * h + 32], sm(h, 0, 32), 1024.0, None, ADD, None, [], [sk(h, 0), (dst, h)], 32)

        for h in range(2):
            mm("a%d" % h, [(bank(0, h), T.SA[0:8, :], ud(0, h), True, False, 512)], ["SA"] + UK, [bk(0, h)])
            mm("c%d" % h, [(bank(1, h), T.SA[0:8, :], ua(0, h), True, True, 512)], ["SA"] + UK, [bk(1, h)])
        src, key, unit = (T.Q0[:, :], "Q0", SG) if t == 0 else (Qr, "Q", 1.0)
        for (a, b) in opt["q"]:
            copy("q%d" % a, pq_(T.pq, par, 1, a, b), src.indirect(T.nl[:, oc + 16 * a:oc + 16 * b]), [key, ("nl", t, a // 2)],
                 [("q", par, u) for u in range(a, b)], 256 * (b - a), "ga", -unit)
        for (a, b) in opt["p"]:
            copy("p%d" % a, pq_(T.pq, par, 0, a, b), T.Pt[:, :].indirect(T.nl[:, oc + 16 * a:oc + 16 * b]), ["P", ("nl", t, a // 2)],
                 [("p", par, u) for u in range(a, b)], 256 * (b - a), "ga", SG)
        for (a, b) in opt["p32"]:
            if t < TK - 1 or any("x1%d" % x not in on_v and x < b and a < y for x, y in opt["x1"]):
                copy("P%d" % a, T.po[:, o2 + 256 * a:o2 + 256 * b], T.Pt[:, :].indirect(T.nl[:, oc + 16 * a:oc + 16 * b]), ["P", ("nl", t, a // 2)],
                     [("P", par, u) for u in range(a, b)], 256 * (b - a), "ga", SG)
        if t == 0:
            for u in range(4):
                copy("Qc%d" % u, T.Qw[:, 640 * u:640 * u + 640], T.Q0[:, 640 * u:640 * u + 640], ["Q0"], [("Qc", u)], 640, 1.0, SG)
        for h in range(2):
            q, p = pq_(T.pq, par, 1, 2 * h, 2 * h + 2), pq_(T.pq, par, 0, 2 * h, 2 * h + 2)
            sd = (1, [p, q], pq_(T.pin, t, 1, 2 * h, 2 * h + 2), 1, [("d", t, h)])
            sp = lambda h: (1, [pq_(T.pq, par, 0, 2 * h, 2 * h + 2)], pq_(T.pin, t, 0, 2 * h, 2 * h + 2), 0, [("pi", t, h)])
            if opt["p32"]:
                send("sr%d" % h, [sd], QK(h) + PK(h), 200e3)
                if h and t < TK - 1:
                    send("sp", [(1, [T.po[:, o2:o2 + R]], T.pw[:, t * R:t * R + R], 0, [("pw", t)])], [("P", par, u) for u in range(4)], 520e3)
            elif t == TK - 1 or opt["split"]:
                send("sr%d" % h, [sd], QK(h) + PK(h), 200e3)
                if h and t < TK - 1:
                    send("sp", [sp(0), sp(1)], PK(0) + PK(1), 256e3)
            else:
                send("sr%d" % h, [sd, sp(h)], QK(h) + PK(h), 400e3)
            mm("L%d" % h, [(bank(0, h), T.Ln[:], q, False, True, 512)], ["Ln"] + QK(h), [bk(0, h)])
            sign("m%d" % h, hs_(T.m1, h), bank(0, h), 0.5, [], [bk(0, h), ("m1", h)], 512, True)
            tt("pr%d" % h, hs_(T.pr, h), bank(1, h), q, MUL, QK(h), [bk(1, h), ("pr", h)], 512)
            mm("e%d" % h, [(bank(2, h), T.I128[:], p, True, False, 512)], ["I128"] + PK(h), [bk(2, h)])
            mm("D%d" % h, [(bank(2, h), T[dm("m%d" % h)][:], hs_(T.m1, h), False, True, 512)], [dm("m%d" % h), ("m1", h)], [bk(2, h)])
            tt("cm%d" % h, hs_(T.cm, h), bank(2, h), hs_(T.pr, h), OP.is_gt, [("pr", h)], [bk(2, h), ("cm", h)], 512)
            if h in opt["direct"]:
                offsets("uo%d" % h, "o1%d" % h, listed(T.WAz, hs_(T.cm, h), sm(h, 0, 32), 512), ["WAz", ("cm", h)], "of1", h)
            mm("fz%d" % h, fold(T.WBy, hs_(T.cm, h), sm(h, 32, 64), True), ["WBy", "WByb", ("cm", h)], [sk(h, 32)])
            copy("Z%d" % h, fh(T.Z1, h), sm(h, 32, 64), [], [sk(h, 32), ("Z1", t, h)], 64)
            if h not in opt["direct"]:
                offsets("uo%d" % h, "o1%d" % h, unfold("bf", fh(T.Z1, h), sm(h, 0, 32), False, True), ["bf0", "bf1", ("Z1", t, h)], "of1", h)
        send("sz", [(1, [T.Z1[:, 2 * oc:2 * oc + 128]], T.Zin[:, 2 * oc:2 * oc + 128], 0, [("Zin", t)])], [("Z1", t, 0), ("Z1", t, 1)], 32e3)
        su, DW = newsem("d"), [("dW", par, x) for x in range(16)]
        for x in range(16):
            dma("Y", T.dW[x:128:16, o2:o2 + R], T.ua[:, (3 * t + 1) * R:(3 * t + 2) * R], ["P"], [DW[x]], 20e3, su)
        if t == 0:
            dma("Y", T.Et[:], T.nx[:], QK(1) + PK(1), ["E"], 660e3)
            su = newsem("d")
            dma("Y", T.uu[0:8, 2 * R:UA], T.ud[:, 2 * R:], [("d", 0, 1)], ["ura"], 200e3, su)
            dma("Y", T.uu[0:8, UA + 3 * R:], T.ua[:, 3 * R:], [("d", 0, 1)], ["urb"], 400e3, su)
            dma("G", T.Vt[:], T.vf[:], [("Zin", 0)], ["Vt"], 700e3, name="lv")
        mm("eT", [(sm(0, 448 + 8 * j, 8), ua(2, j // 4)[:, 128 * (j % 4):128 * (j % 4) + 128], T.I1[0:8, 0:8], j == 0, j == 7, 64)
                  for j in range(8)], ["I1"] + UK, [sk(0, 448)])
        copy("eC", T.eT[:], sm(0, 448, 64), [], [sk(0, 448), "eT"], 64)
        for (a, b) in opt["x1"]:
            if "x1%d" % a in on_v:
                cp("x1%d" % a, Qx.indirect(T.of1[:, 16 * a:16 * b]), pq_(T.pq, par, 0, a, b),
                   [("of1", a // 2)] + [("p", par, u) for u in range(a, b)] + [("Qc", u) for u in range(4)], ["Q"], 256 * (b - a), "sc")
            else:
                fn = lambda o=Qx.indirect(T.of1[:, 16 * a:16 * b]), x=T.po[:, o2 + 256 * a:o2 + 256 * b]: S.activation(o, x, AF.Tanh)
                add("x1%d" % a, "S", fn, [("of1", a // 2)] + [("P", par, u) for u in range(a, b)] + [("Qc", u) for u in range(4)], ["Q"], ("sc", 256 * (b - a)))
        if t < TK - 1 and not opt["p32"]:
            if opt["split"]:
                dma("G", T.p32[:], T.pin[:, 2 * t:2 * t + 2, 0, :], [("pi", t, 0), ("pi", t, 1)], [("p32", 0), ("p32", 1)], 600e3, name="pc")
            else:
                for h in range(2):
                    if any("x2%d" % a not in on_v and a // 2 == h for a, b in opt["x2"]):
                        dma("G", hs_(T.p32, h), T.pin[:, 2 * t + h, 0, :], [("pi", t, h)], [("p32", h)], 300e3, name="pc%d" % h)
        for (a, b) in opt["eg"]:
            copy("Eg%d" % a, T.Eg[:, 256 * a:256 * b], T.Et[:, :].indirect(T.nin[:, oc + 16 * a:oc + 16 * b]), ["E", ("nin", t)],
                 [("Eg", u) for u in range(a, b)], 256 * (b - a), "ga")
        dd = lambda h: pq_(T.pin, t, 1, 2 * h, 2 * h + 2)
        for h in range(2):
            mm("b%d" % h, [(bank(0, h), T.SA[0:8, :], ud(1, h), True, False, 512)], ["SA"] + UK, [bk(0, h)])
            relu("r%d" % h, hs_(T.rr, h), dd(h), [("d", t, h)], [("r", h)], 512, f=0.5)
            mm("J%d" % h, [(bank(1, h), T.Jh[:], hs_(T.rr, h), True, True, 512)], ["Jh", ("r", h)], [bk(1, h)])
            mm("N%d" % h, [(bank(2, h), T.Lsn[:], dd(h), True, False, 512)], ["Lsn", ("d", t, h)], [bk(2, h)])
        for (a, b) in opt["g"]:
            copy("g%d" % a, T.q2[:, 256 * a:256 * b], Qr.indirect(T.nin[:, oc + 16 * a:oc + 16 * b]), ["Q", ("nin", t)],
                 [("q2", u) for u in range(a, b)], 256 * (b - a), "ga", -1.0)
        for h in range(2):
            q2, K2, mn = hs_(T.q2, h), [("q2", 2 * h), ("q2", 2 * h + 1)], hs_(T.mn, h)
            mm("M%d" % h, [(bank(0, h), T.Ln[:], q2, False, True, 512)], ["Ln"] + K2, [bk(0, h)])
            sign("n%d" % h, hs_(T.m2, h), bank(0, h), 0.5, [], [bk(0, h), ("m2", h)], 512, True)
            tt("y%d" % h, bank(1, h), bank(1, h), q2, MUL, K2, [bk(1, h)], 512)
            tt("mn%d" % h, mn, bank(1, h), dd(h), MIN, [("d", t, h), bk(1, h)], [("mn", h)], 512)
            tt("pq%d" % h, hs_(T.pr, h), bank(1, h), hs_(T.dW, h, o2), MUL, DW + [bk(1, h)], [("pr", h)], 512)
            mm("R%d" % h, [(bank(0, h), T.I128[:], dd(h), True, False, 512)], ["I128", ("d", t, h)], [bk(0, h)])
            mm("E%d" % h, [(bank(0, h), T[dm("n%d" % h)][:], hs_(T.m2, h), False, True, 512)], [dm("n%d" % h), ("m2", h)], [bk(0, h)])
            tt("cn%d" % h, hs_(T.cn, h), bank(0, h), hs_(T.pr, h), OP.is_gt, [("pr", h)], [bk(0, h), ("cn", h)], 512)
            mm("fy%d" % h, [(sm(h, 256, 64), T.MZ[:], fh(T.Zin, h), True, False, 64)] + fold(T.WBy, hs_(T.cn, h), sm(h, 256, 64), False),
               ["MZ", ("Zin", t), "WBy", "WByb", ("cn", h)], [sk(h, 256)])
            relu("u%d" % h, c64(T.u2, h), sm(h, 256, 64), [], [sk(h, 256), ("u2", h)], 64)
            if t < TK - 1:
                offsets("up%d" % h, "o2%d" % h, unfold("bf", fh(T.Zin, h), sm(h, 0, 32), False, False) + unfold("bf", c64(T.u2, h), sm(h, 0, 32), False, True),
                        ["bf0", "bf1", ("u2", h), ("Zin", t)], "of2", h)
            tot, tk_ = (sm(0, 96 + 32 * h, 32), sk(0, 96 + 32 * h)) if opt["gfull"] else (sm(h, 96, 32), sk(h, 96))
            mm("fw%d" % h, [(tot[:, 8 * j:8 * j + 8], mn[:, 128 * j:128 * j + 128], T.B32[:], j == 0, j == 3, 256) for j in range(4)],
               ["B32", ("mn", h)], [tk_])
            for u in range(2):
                mm("C%d" % (2 * h + u), [(bank(2, h)[:, 256 * u:256 * u + 256], T.Ls32[:], qs_(T.mn, 2 * h + u), False, False, 1024)],
                   ["Ls32", ("mn", h)], [bk(2, h)])
            if opt["gfull"]:
                if h == 0:
                    continue
                tot, tk_, hi, lo = sm(0, 96, 64), [sk(0, 96), sk(0, 128)], T.HL[:, 0:64], T.HL[:, 64:128]
                tt("gA1", hi, tot, T.eT[:], MUL, ["eT"], tk_ + ["HL"], 64)
                tt("gB1", tot, tot, T.eT[:], MUL, ["eT"], tk_, 64)
                tt("gC1", lo, tot, hi, SUB, ["HL"] + tk_, tk_ + ["HL"], 64)
                mm("tr1", [(sm(1, 128, 128), T.HL[:, 0:128], T.I16[:], True, True, 128)], ["I16", "HL"], [sk(1, 128)])
                copy("hF1", T.HF[:, 0:128], sm(1, 128, 128), [], [sk(1, 128), "HF"], 128)
                for x in range(2):
                    mm("Th%d" % x, [(bank(2, x)[:, 128 * j:128 * j + 128], T.TH[:, 512 * x + 128 * j:512 * x + 128 * j + 128], T.HF[:, 0:128], False, j == 3, 128)
                                    for j in range(4)], THK + ["HF"], [bk(2, x)])
                    sign("ct%d" % x, hs_(T.cnt, x), bank(2, x), -1.0 / 512, [], [bk(2, x), ("cnt", x)], 512)
                continue
            e, hi, lo = T.eT[:, 32 * h:32 * h + 32], T.HL[:, 128 * h:128 * h + 32], T.HL[:, 128 * h + 64:128 * h + 96]
            tr, hf = sm(h, 128, 128), T.HF[:, 128 * h:128 * h + 128]
            tt("gA%d" % h, hi, tot, e, MUL, ["eT"], [sk(h, 96), ("HL", h)], 32)
            tt("gB%d" % h, tot, tot, e, MUL, ["eT"], [sk(h, 96)], 32)
            tt("gC%d" % h, lo, tot, hi, SUB, [("HL", h), sk(h, 96)], [sk(h, 96), ("HL", h)], 32)
            mm("tr%d" % h, [(tr, T.HL[:, 128 * h:128 * h + 128], T.I16[:], True, True, 128)], ["I16", ("HL", h)], [sk(h, 128)])
            copy("hF%d" % h, hf, tr, [], [sk(h, 128), ("HF", h)], 128)
            mm("Th%d" % h, [(bank(2, h)[:, 128 * j:128 * j + 128], T.TH[:, 128 * j:128 * j + 128], hf, False, j == 3, 128) for j in range(4)],
               THK + [("HF", h)], [bk(2, h)])
            sign("ct%d" % h, hs_(T.cnt, h), bank(2, h), -1.0 / 512, [], [bk(2, h), ("cnt", h)], 512)
        if t < TK - 1:
            for (a, b) in opt["x2"]:
                if opt["p32"]:
                    o, x = Qx.indirect(T.of2[:, 16 * a:16 * b]), T.pw[:, t * R + 256 * a:t * R + 256 * b]
                    fn = (lambda o=o, x=x: V.tensor_copy(o, x)) if "x2%d" % a in on_v else (lambda o=o, x=x: S.activation(o, x, AF.Tanh))
                    add("x2%d" % a, "V" if "x2%d" % a in on_v else "S", fn, [("of2", a // 2), ("pw", t)], ["Q"], ("sc", 256 * (b - a)))
                elif "x2%d" % a in on_v:
                    cp("x2%d" % a, Qx.indirect(T.of2[:, 16 * a:16 * b]), pq_(T.pin, t, 0, a, b), [("of2", a // 2), ("pi", t, a // 2)], ["Q"], 256 * (b - a), "sc")
                else:
                    fn = lambda o=Qx.indirect(T.of2[:, 16 * a:16 * b]), x=T.p32[:, 256 * a:256 * b]: S.activation(o, x, AF.Tanh)
                    add("x2%d" % a, "S", fn, [("of2", a // 2), ("p32", a // 2)], ["Q"], ("sc", 256 * (b - a)))
        for h in range(2):
            ub = c64(T.ub, h)
            mm("I%d" % h, [(bank(1, h), T.I1[:], hs_(T.Eg, h), True, False, 512)], ["I1", ("Eg", 2 * h), ("Eg", 2 * h + 1)], [bk(1, h)])
            mm("fc%d" % h, [(sm(h, 320, 64), T.MU[:], fh(T.Zin, h), True, False, 64), (sm(h, 320, 64), T.MU[:], c64(T.u2, h), False, False, 64)]
               + fold(T.WBc, hs_(T.cnt, h), sm(h, 320, 64), False), ["WBc", "MU", "MUb", ("Zin", t), ("cnt", h), ("u2", h)], [sk(h, 320)])
            off16 = last("ct%d" % h) in on_v
            relu("ub%d" % h, ub, sm(h, 320, 64), [k16] if off16 else [], [sk(h, 320), ("ub", h)], 64, c16 if off16 else 0.0)
            mm("s%d" % h, [(sm(h, 384, 64), T.Sh[:], ub, True, True, 64)], ["Sh", ("ub", h)], [sk(h, 384)])
            act("kk%d" % h, c64(T.kk, h), sm(h, 384, 64), AF.Square, [kSq], [sk(h, 384), ("kk", h)], 64, bias=cSq)
            act("ab%d" % h, c64(T.ab, h), sm(h, 384, 64), AF.Abs, [kAb], [sk(h, 384), ("ab", h)], 64, bias=cAb)
            mm("K%d" % h, [(bank(1, h)[:, i:512:8], T.KB[:, 128 * i:128 * i + 128], c64(T.kk, h), False, i == 7, 64) for i in range(8)],
               KBK + [("kk", h)], [bk(1, h)])
            ts("se%d" % h, hs_(T.sel, h), bank(1, h), cLo, cHi, MAX, MIN, [kLo, kHi], [bk(1, h), ("sel", h)], 512)
        for hh in ([(0, 1)] if opt["full"] else [(0,), (1,)]):
            h, n = hh[-1], 32 * len(hh)
            nx_, key = (sm(0, 256, n), sk(0, 256)) if n == 64 else (sm(h, 0, n), sk(h, 0))
            a = 64 * hh[0]
            mm("v%d" % h, unfold("bk", T.ub[:, a:a + 2 * n], nx_, True, False, 2 * n) + unfold("bf", T.ab[:, a:a + 2 * n], nx_, False, False, 2 * n),
               ["bk0", "bk1", "bf0", "bf1"] + [(k, x) for k in ("ub", "ab") for x in hh], [key], 1)
            mm("W%d" % h, listed(T.WAe, T.sel[:, 8 * a:8 * a + 16 * n], nx_, 16 * n), ["WAe"] + [("sel", x) for x in hh], [key], -1)
            ts("nn%d" % h, T.nl[:, oc + 64 + a // 2:oc + 64 + a // 2 + n], nx_, -1.0, -170753.0, MUL, ADD, [], [key] + [("nl", t + 1, x) for x in hh], n)
        if t < TK - 1:
            nn = T.nl[:, oc + 64:oc + 128]
            it = [(1, [nn], T.nin[:, oc + 64:oc + 128], 0, [("nin", t + 1)])]
            off = (TK - 1 - t) % NR
            if off > 1:
                it.append((off, [nn], T.hl[:, (off - 2) * 64:(off - 2) * 64 + 64], 0, [("hl", off)]))
            send("sn", it, [("nl", t + 1, 0), ("nl", t + 1, 1)], 16e3)
        if t == TK - 2:
            cp("nF", T.nF[:, 0:oc + 64], T.nl[:, 64:oc + 128], [("nl", k + 1, h) for k in range(t + 1) for h in range(2)], ["nFa"], oc + 64)
        h_step(t)
        if t == TK - 1:
            cp("hvn", T.nF[:, oc:], T.nl[:, oc + 64:], [("nl", t + 1, 0), ("nl", t + 1, 1)], ["nFb"], 64)
            dma("S", T.yn[:], T.nF[:], ["nFa", "nFb"], ["yn"], 200e3, name="hty")
        rot = [rot[0], rot[2], rot[1]]
    return ops


def times(o, c):
    k, n = o["cost"]
    if k == "cy":
        return c["fix"] + n * c["cy"], 0.0
    if k in ("ga", "sc"):
        return c["fix"] + n * c[k] * c["cy"], 0.0
    if k == "pcy":
        return n * c["pcy"], 0.0
    if k == "gp":
        return 0.15 + 2 * n * c["cy"], 0.0
    if k == "dma":
        return (c["giss"] if o["eng"] == "G" else 0.08), c["dlat"] + n / c["bw"]
    if k == "send":
        return c["riss"], c["rlat"] + n / c["bw"]
    return 0.0, 0.0


def order(ops, lists=ORDER, c=COST):
    n = len(ops)
    named, queue = {}, {e: [] for e in "VSPGY"}
    for i, o in enumerate(ops):
        if o["name"] == "ld" or o["eng"] == "Y":
            queue[o["eng"]].append(i)
        elif o["name"]:
            named.setdefault((o["name"], o["tok"]), []).append(i)
    for t in range(-1, TK + 1):
        for e, names in lists.items():
            for w in names.split():
                queue[e] += named.pop((w.rstrip("+-"), t + (w[-1] == "+") - (w[-1] == "-")), [])
    assert not named, named
    deps = [dict(o["deps"]) for o in ops]
    succ = [[] for _ in ops]
    for i in range(n):
        for j in deps[i]:
            succ[j].append(i)
    left = [len(d) for d in deps]
    tm = [times(o, c) for o in ops]
    ready = {i: 0.0 for i in range(n) if left[i] == 0}
    free, end, seq, user, held = {e: 0.0 for e in queue}, [0.0] * n, [], {}, {}
    head = {e: 0 for e in queue}

    def can(i):
        if i not in ready:
            return None
        o, r = ops[i], ready[i]
        if o["bank"]:
            b = o["bank"][0]
            if o["start"] and held.get(b):
                return None
            if b in user and ops[user[b]]["eng"] != o["eng"]:
                r = max(r, end[user[b]] + c["lat"])
        return max(r, free[o["eng"]])

    def done(i, at):
        end[i] = at
        seq.append(i)
        del ready[i]
        for j in succ[i]:
            left[j] -= 1
            if left[j] == 0:
                ready[j] = max(end[k] + ((c["same"] if raw else 0.0) if ops[k]["eng"] == ops[j]["eng"] and ops[k]["kind"] == "c" else c["lat"])
                               for k, raw in deps[j].items())
                if ops[j]["kind"] == "arr":
                    done(j, ready[j] - c["lat"])

    while len(seq) < n:
        best = None
        for e in queue:
            a = can(queue[e][head[e]]) if head[e] < len(queue[e]) else None
            if a is not None and (best is None or (a, queue[e][head[e]]) < best):
                best = (a, queue[e][head[e]])
        assert best, [(ops[q[head[e]]]["name"], ops[q[head[e]]]["tok"], [ops[j]["name"] for j in deps[q[head[e]]] if not end[j]])
                      for e, q in queue.items() if head[e] < len(q)]
        st, i = best
        o = ops[i]
        e = o["eng"]
        head[e] += 1
        if o["bank"]:
            b = o["bank"][0]
            if b in user:
                deps[i].setdefault(user[b], False)
            user[b] = i
            if o["hold"]:
                held[b] = o["hold"] > 0
        free[e] = st + tm[i][0]
        done(i, free[e] + tm[i][1])
    return seq, end, [dict(o, deps=d) for o, d in zip(ops, deps)]


def emit(g, T, ops, seq):
    queue = {"V": g.vector, "S": g.scalar, "P": g.tensor, "G": g, "Y": g.sync}

    def must(j, o, raw):
        if o["kind"] == "arr":
            return False
        return ops[j]["kind"] != "c" or o["kind"] != "c" or ops[j]["eng"] != o["eng"] or raw

    need = set(j for o in ops for j, raw in o["deps"].items() if must(j, o, raw))
    total, event = {}, {}
    for i in seq:
        o = ops[i]
        if o["kind"] == "c":
            if i in need:
                s = "e" + o["eng"]
                total[s] = total.get(s, 0) + 1
                event[i] = (s, total[s])
        else:
            total[o["sem"]] = total.get(o["sem"], 0) + o["inc"]
    for i in seq:
        if ops[i]["kind"] != "c":
            event[i] = (ops[i]["sem"], total[ops[i]["sem"]])
    seen = {e: {} for e in queue}
    for i in seq:
        o = ops[i]
        if o["kind"] == "arr":
            continue
        want = {}
        for j, raw in o["deps"].items():
            if must(j, o, raw):
                s, v = event[j]
                want[s] = max(want.get(s, 0), v)
        for s, v in want.items():
            if seen[o["eng"]].get(s, 0) < v:
                queue[o["eng"]].wait_ge(T.sem[s], v)
                seen[o["eng"]][s] = v
        r = o["fn"]()
        if o["kind"] == "dma":
            r.then_inc(T.sem[o["sem"]], 16)
        elif o["kind"] == "c" and i in event:
            r.then_inc(T.sem[event[i][0]], 1)
    for s, v in total.items():
        if max(seen[e].get(s, 0) for e in seen) < v:
            g.wait_ge(T.sem[s], v)


def rank_program(g, core, T, topo):
    rank = T.rank_of(core)
    if rank is None:
        return
    seq, _t, ops = order(build(g, core, T, topo, rank))
    emit(g, T, ops, seq)
